import numpy as np, ml_dtypes
CORES = [24,25,26,27,28,29,30,31]
N = 8
BF = ml_dtypes.bfloat16
def gentries(a):
    return np.ascontiguousarray(a.reshape(8, 16, -1).transpose(0, 2, 1)).reshape(8, -1)
def gtable(e):
    e = np.asarray(e); return np.ascontiguousarray(e.reshape(8, -1, 16).transpose(0, 2, 1)).reshape(128, -1).astype(np.int32)
L, M, B, P = 4, 512, 32, 3
H, F, E, G, LN = (N - 1) * B, (L - 1) * M, L * M, (L - 1) * (N - 1) * B, M // 2
NONE = E + G
LEV = np.concatenate([np.arange(E) // M, np.arange(G) // H, np.array([-1])])
DL = np.broadcast_to((np.arange(F) // M + 1)[:, None], (N, 8, F, 16)); SL = np.broadcast_to(np.concatenate([np.arange(F) // M, np.arange(G) // H]), (N, 8, F + G))
GM = [np.arange(8), 7 - np.arange(8), (8 - np.arange(8)) % 8]
def names(rng, lv, low):
    x = np.where(rng.random(lv.shape) < low, 0, (rng.random(lv.shape) * lv).astype(np.int64))
    y = rng.integers(0, M + H, lv.shape)
    return np.where(y < M, x * M + y, E + x * H + y - M)
def parts(rng):
    A = np.minimum((256 * rng.random((N, 8, E, 16)) ** 0.1666).astype(np.int64), 255); c = np.arange(E)[:, None]
    tight = rng.random((N, 8, E, 1)) < np.where(c < M, 0.0, np.where(c < F, 0.12, 0.3))
    A = np.where(tight, (A * (0.3 + 0.5 * rng.random((N, 8, E, 1)))).astype(np.int64), A)
    dp = names(rng, DL, 0.6); dp = np.where(rng.random(dp.shape) < rng.choice(np.array([0.0, 0.25, 0.5]), (N, 8, 1, 1)), NONE, dp)
    sb = names(rng, SL + 1, 0.3); sb = np.where(rng.random(sb.shape) < 0.0625, NONE, sb)
    return A, dp, sb, rng.integers(0, M, (N, 8, L - 1, N - 1, B)), rng.integers(40, 161, (N, 8, M))
def pack(A, dp, sb, bd, th):
    return {"av": np.ascontiguousarray(A.transpose(0, 1, 3, 2)).reshape(N, 128, E).astype(np.float32).astype(BF),
            "dp": np.ascontiguousarray(dp.transpose(0, 1, 3, 2)).reshape(N, 128, F).astype(np.int32), "sb": np.ascontiguousarray(sb).astype(np.int32),
            "bd": np.stack([gtable(a.reshape(8, -1)) for a in bd]), "th": np.ascontiguousarray(th).astype(np.int32)}
def setup_inputs(rng):
    A, dp, sb, bd, th = parts(rng)
    return pack(A, dp, sb, bd, th)
def setup_inputs_spread(rng):
    A, dp, sb, bd, th = parts(rng)
    A = np.where(rng.random((N, 8, E, 1)) < 0.1, np.exp2(8 * rng.random(A.shape)).astype(np.int64) - 1, 256 - np.exp2(7 * rng.random(A.shape)).astype(np.int64))
    dp = np.where(rng.random(dp.shape) < rng.choice(np.array([0.3, 0.6, 0.9]), (N, 8, F, 1)), NONE, dp)
    bd = np.where(rng.random(bd.shape) < 0.5, (M * rng.random(bd.shape) ** 4).astype(np.int64), bd)
    th = np.where(rng.random(th.shape) < 0.5, np.exp2(8 * rng.random(th.shape)).astype(np.int64) - 1, rng.integers(0, 256, th.shape))
    return pack(A, dp, sb, bd, th)
def setup_inputs_ends(rng):
    A, dp, sb, bd, th = parts(rng)
    A = np.where(rng.random((N, 8, E, 1)) < 0.1, rng.integers(16, 255, A.shape), np.where(rng.random(A.shape) < rng.choice(np.array([0.02, 0.06, 0.15]), (N, 8, 1, 1)), 0, 255))
    A[:, :, 0] = np.where(rng.random((N, 8, 16)) < 0.5, 0, 255)
    c = rng.random((N, 8, F, 1)); x = names(rng, DL, 0.6)
    z = np.where((c > 0.4) & (c < 0.6) & (rng.random(x.shape) < 0.5), 0, NONE)
    dp = np.where(rng.random(x.shape) < np.where(c < 0.6, 0.125, 0.5), x, z)
    sb = np.where(rng.random(sb.shape) < 0.7, np.where(rng.random(sb.shape) < 0.5, 0, NONE), sb)
    bd = np.where(rng.random(bd.shape) < 0.75, np.where(rng.random(bd.shape) < 0.5, 0, M - 1), bd)
    e = np.where(rng.random(th.shape) < 0.5, 0, 255); th = np.where(rng.random(th.shape) < 0.8, e, rng.integers(1, 255, th.shape))
    for j in (F, F + 1, E - 2, E - 1):
        A[:, :, j] = 255; dp[:, :, j - M] = NONE; th[:, :, j - F] = e[:, :, j - F]
    for j in (F, E - 2): dp[:, :, j - M, 15] = NONE - 1
    for j in (F + 1, E - 1): dp[:, :, j - M, 14:] = F - 1
    A[:, :, F - 1] = 0; A[:, :, F - 1, 15] = 254; dp[:, :, F - 1 - M] = NONE
    for j in (F + 2, E - 3): A[:, :, j] = 0; th[:, :, j - F] = e[:, :, j - F]
    for j in (F + 4, E - 5): A[:, :, j] = 255; dp[:, :, j - M] = NONE; th[:, :, j - F] = e[:, :, j - F]
    return pack(A, dp, sb, bd, th)
def couples(rng):
    o = np.concatenate([np.array([0, LN - 1, LN - 3, LN - 2]), 1 + rng.permutation(LN - 4)]).reshape(-1, 2)
    return np.min(o, axis=1), np.max(o, axis=1)
def setup_inputs_crowd(rng):
    A, dp, sb, bd, th = parts(rng); i = np.arange(M)
    for r in range(N):
        for g in range(8):
            kind = (r + g) % 7; z = rng.permutation(M)[:17]; A[r, g, F:] = 10; A[r, g, F + i, rng.integers(0, 16, M)] = 255
            if kind < 2:
                hub = int(z[16]); A[r, g, hub] = rng.integers(70, 121, 16); th[r, g] = rng.integers(0, 21, M)
            elif kind < 4:
                hub = F - M + int(rng.integers(0, M)); dp[r, g, hub - M] = z[:16]; A[r, g, hub] = 255
                A[r, g, z[:16]] = 255; A[r, g, z[:16], rng.permutation(16)] = rng.integers(60, 121, 16); th[r, g] = rng.integers(200, 256, M)
            elif kind == 4:
                hub = F - M + int(rng.integers(0, M)); dp[r, g, hub - M] = z[:16]; dates = rng.permutation(16)
                A[r, g, hub] = 255; A[r, g, hub, dates[:8]] = rng.integers(60, 121, 8)
                A[r, g, z[:16]] = 255; A[r, g, z[:16], np.concatenate([dates[8:], dates[8:]])] = rng.integers(60, 121, 16)
                th[r, g] = np.where(rng.random(M) < 0.5, rng.integers(0, 21, M), rng.integers(200, 256, M))
            else:
                a, b = couples(rng); n = len(a); u = 1 + rng.permutation(M - 1); u[2] = 0
                za, zb = u[:n], u[n:2 * n]; y = rng.random(n) < 0.25; da, db = 2 * rng.integers(0, 8, n), 2 * rng.integers(0, 8, n) + 1
                if kind == 5:
                    y[:2] = False; y[2] = True; da[y] = 0
                w = np.zeros(LN, np.int64); w[a] = np.arange(n); w[b] = np.arange(n)
                dt = np.zeros(LN, np.int64); dt[a] = da; dt[b] = db
                A[r, g, F:] = 10; A[r, g, F + i, dt[i >> 1]] = 255
                if kind == 5:
                    hub = za; A[r, g, hub] = rng.integers(70, 121, (n, 16)); th[r, g] = rng.integers(0, 21, M); A[r, g, za[y], 0] = 0
                    for h in (0, 1):
                        j = 2 * a[y] + h; A[r, g, F + j] = 0; A[r, g, F + j, 0] = 255; th[r, g, j] = 0
                else:
                    y[0] = True; y[1] = False; hub = F - M + 1 + rng.permutation(M - 1)[:n]; hub[1] = M
                    A[r, g, hub] = 255; A[r, g, za] = 255; A[r, g, zb] = 255
                    A[r, g, za, da] = rng.integers(60, 121, n); A[r, g, zb, db] = rng.integers(60, 121, n)
                    s = np.argsort(rng.random((n, 16)), axis=1); dp[r, g, hub - M] = NONE
                    dp[r, g, hub - M, s[:, 0]] = za; dp[r, g, hub - M, s[:, 1]] = zb
                    sb[r, g, za[y]] = za[y]; sb[r, g, zb[0]] = NONE; sb[r, g, za[1]] = NONE
                    bk = rng.random(n) < 0.25; bk[:2] = False; bk[2] = True
                    th[r, g] = np.where(bk[w[i >> 1]], rng.integers(0, 13, M), rng.integers(200, 256, M))
                hub = hub[w[i >> 1]][:, None]
            m = rng.random((M, 16)) < 0.2; m[i, rng.integers(0, 16, M)] = True
            dp[r, g, F - M:] = np.where(m, hub, NONE)
            if kind in (1, 3):
                j = 2 * int(rng.choice(np.array([0, LN - 1, rng.integers(0, LN)]))); dp[r, g, F - M + j:F - M + j + 2] = NONE
    return pack(A, dp, sb, bd, th)
def setup_inputs_chains(rng):
    A, dp, sb, bd, th = parts(rng)
    A[:, :, M:] = rng.integers(254, 256, (N, 8, F, 16)); A[:, :, :M] = rng.choice(np.array([0, 15, 16, 50, 51, 100, 101] + [253] * 20), (N, 8, M, 16))
    odd = ((np.arange(N)[:, None] + np.arange(8)) % 2 == 1)[:, :, None, None]
    x = np.where(odd & (rng.random(DL.shape) < 0.25), E + (DL - 1) * H + rng.integers(0, H, DL.shape), (DL - 1) * M + rng.integers(0, M, DL.shape))
    x = np.where(rng.random((N, 8, F, 1)) < 0.25, x[..., :1], x); k = np.arange(16)
    m = (k == rng.integers(0, 16, (N, 8, F, 1))) | (k == rng.choice(np.array([0, 7, 15]), (N, 8, F, 1)))
    dp = np.where(m, x, NONE); u = rng.integers(0, 4, SL.shape)
    own = np.concatenate([np.arange(F), E + np.arange(G)])
    sb = np.where(u == 0, NONE, np.where(u == 1, own, np.where(u == 2, E + (SL + 1) * H - 1, sb)))
    th = rng.choice(np.array([0, 16, 50, 51, 52, 100, 101, 102, 253, 254, 255]), (N, 8, M))
    return pack(A, dp, sb, bd, th)
def setup_inputs_calm(rng):
    A, dp, sb, bd, th = parts(rng); base = np.array([16, 17, 18, 19, 33, 35, 254, 255]); i = np.arange(LN)
    for r in range(N):
        for g in range(8):
            a = np.where(rng.random(LN) < 0.7, base[(r + g) % 8], rng.choice(base, LN)); z = rng.permutation(M)[:LN]
            A[r, g, z] = np.maximum(a - 64, 0)[:, None]; A[r, g, z, rng.integers(0, 16, LN)] = a
            A[r, g, F:] = 255; A[r, g, F - M + i] = 255
            dp[r, g, F - 2 * M + i] = NONE; dp[r, g, F - 2 * M + i, rng.integers(0, 16, LN)] = z
            hub = np.where(i % 2 == 1, F - M + i, z)
            for h in (0, 1):
                dp[r, g, F - M + 2 * i + h] = NONE; dp[r, g, F - M + 2 * i + h, rng.integers(0, 16, LN)] = hub
            w = i[rng.random(LN) < 0.125]; dp[r, g, F - M + 2 * w + 1, rng.integers(0, 16, len(w))] = E + rng.integers(0, H, len(w))
            th[r, g, 2 * i] = np.maximum(a - rng.choice(np.array([15, 16, 31, 32]), LN), 0); th[r, g, 2 * i + 1] = np.maximum(a - rng.choice(np.array([15, 16, 17]), LN), 0)
    return pack(A, dp, sb, bd, th)
def check_inputs(d):
    bad = []
    for k, lo, hi in (("av", 0, 255), ("dp", 0, NONE), ("sb", 0, NONE), ("bd", 0, M - 1), ("th", 0, 255)):
        x = np.asarray(d[k]).astype(np.float64)
        if not np.all((x >= lo) & (x <= hi)): bad.append("range of " + k)
        elif not np.all(x == np.floor(x)): bad.append("whole numbers in " + k)
    if np.any(LEV[np.clip(np.asarray(d["dp"]).astype(np.int64), 0, NONE)] > np.arange(F) // M): bad.append("levels of dp")
    if np.any(LEV[np.clip(np.asarray(d["sb"]).astype(np.int64), 0, NONE)] > SL): bad.append("levels of sb")
    return bad
def first(want, at):
    lo = np.full((N, 8, E), LN); n, g, i = np.nonzero(want); np.minimum.at(lo, (n, g, at[want]), i)
    return want & (np.take_along_axis(lo, np.where(want, at, 0), 2) == np.arange(LN))
def reference(av, dp, sb, bd, th):
    A = np.ascontiguousarray(av.astype(np.int32).reshape(N, 8, 16, E).transpose(0, 1, 3, 2))
    D = np.ascontiguousarray(dp.astype(np.int64).reshape(N, 8, 16, F).transpose(0, 1, 3, 2))
    S = sb.astype(np.int64); t0 = th.astype(np.int64)
    bl = np.stack([gentries(a) for a in bd]).astype(np.int64).reshape(N, 8, L - 1, N - 1, B)
    ni = np.arange(N)[:, None, None]; gi = np.arange(8)[None, :, None]
    for t in range(P):
        R = np.full((N, 8, NONE + 1, 16), 255, np.int32)
        for l in range(L):
            a = A[:, :, l * M:(l + 1) * M]
            if l > 0:
                ix = D[:, :, (l - 1) * M:l * M].reshape(N, 8, M * 16)
                a = np.minimum(a, np.min(R[ni, gi, ix].reshape(N, 8, M, 16, 16), axis=3))
            R[:, :, l * M:(l + 1) * M] = a
            if l < L - 1:
                for r in range(N):
                    for d in range(1, N):
                        q = r ^ d; h = GM[d % 3]; s = E + l * H + (d - 1) * B
                        R[r, :, s:s + B] = R[q, h[:, None], l * M + bl[q, h, l, d - 1]]
        e = np.broadcast_to(F + 2 * np.arange(LN) + (t & 1), (N, 8, LN))
        re = R[ni, gi, e]; p = np.argmax(re, axis=3); v = np.max(re, axis=3)
        f = e; q = np.full((N, 8, LN), -1); k = np.zeros((N, 8, LN), np.int64)
        for step in range(L - 1):
            go = (f < E) & (A[ni, gi, np.where(f < E, f, 0), p] != v)
            c = D[ni, gi, np.where(go, f - M, 0)]
            k1 = np.argmax(R[ni[..., None], gi[..., None], c, p[..., None]] == v[..., None], axis=3)
            to = np.take_along_axis(c, k1[..., None], 3)[..., 0]
            q = np.where(go, f, q); k = np.where(go, k1, k); f = np.where(go, to, f)
        b = np.take_along_axis(t0, e - F, 2); ok = v >= b
        wa = first((ok & (f < E)) | (~ok & (f == e)), f); wd = first(~ok & (f != e), q)
        na = np.where(ok, np.maximum(v - 16, 0), b); nd = S[ni, gi, np.where(f != e, np.where(f < E, f, f - M), 0)]
        n, g, i = np.nonzero(wa); A[n, g, f[wa], p[wa]] = na[wa]
        n, g, i = np.nonzero(wd); D[n, g, q[wd] - M, k[wd]] = nd[wd]
    return {"ya": np.ascontiguousarray(A.transpose(0, 1, 3, 2)).reshape(N, 128, E).astype(np.float32).astype(BF),
            "yd": np.ascontiguousarray(D.transpose(0, 1, 3, 2)).reshape(N, 128, F).astype(np.float32),
            "yr": np.ascontiguousarray(R[:, :, F:E].transpose(0, 1, 3, 2)).reshape(N, 128, M).astype(np.float32).astype(BF)}

@@ -1,0 +1,478 @@
+from concourse.bass import DstId, RemoteDMATransfer, IndirectOffsetOnAxis
+from concourse.mybir import AluOpType as Op, ActivationFunctionType as Fn
+
+F32, BF, I32, U16, F16 = "float32", "bfloat16", "int32", "uint16", "float16"
+NP = 304
+NPT = 144
+PC = {NP: (16, 32, 32, 36, 36), NPT: (16, 24, 32)}
+NC = {512 - NP: (64, 64, 48, 16, 16), 256 - NPT: (48, 32, 16, 16)}
+A0, DB, WN = 8, 2080, 3616
+DCOL = {1: DB + 1024, 2: DB + 512, 3: DB}
+KCOL = {1: 768, 2: 256}
+M16, M12, M0 = 1.5 * 2 ** 39, 1.5 * 2 ** 35, 1.5 * 2 ** 23
+SB = {
+    "avs": (2048, BF), "dps": (1536, I32), "bds": (42, I32), "bdo": (42, U16), "sbs": (2208, I32), "ths": (512, I32),
+    "W": (WN, F32), "TT": (2728, F32), "KC": (1280, F32), "SD": (2736, I32),
+    "gs": (8 * NP, F32), "gp": (8 * NP, F32), "sp": (8 * NP, F32), "gn": (16 * (512 - NP), F32), "sn": (16 * (512 - NP), F32),
+    "go": (4096, BF), "so": (4096, BF), "hi": (512, F32), "hb": (512, BF), "abd": (448, BF), "tmp": (1536, F32),
+    "on1": (512 - NP, U16), "on2": (512 - NP, U16), "on3": (256 - NPT, U16), "ono": (256, U16),
+    "op1": (NP, U16), "op2": (NP, U16), "op3": (NPT, U16),
+    "dN": (1024, BF), "dP": (1024, BF), "dO": (1024, BF), "dX": (256, BF), "dC": (256, BF), "dD": (256, BF), "c30": (512, BF),
+    "ramp": (512, F32), "gc0": (672, F32), "one": (128, F32), "oneb": (128, BF), "ident": (128, BF), "pm1": (128, BF), "pm2": (128, BF),
+    "bo": (128, F32), "bob": (128, BF), "pp": (512, F32), "sh": (1920, BF), "slt": (2048, BF), "colr": (256, F32), "dg": (256, F32), "ng": (256, BF),
+    "tri": (256, BF), "cp": (256, F32), "pi": (4, I32), "gi": (4, I32), "pf": (8, F32), "lc": (160, F32), "oc": (16, U16),
+    "rt": (256, BF), "rtt": (256, BF), "ax": (256, F32), "mt": (256, BF), "mp": (256, BF), "mm": (256, F32), "ll": (256, F32),
+    "li": (128, I32), "sm": (512, F32), "oh": (16, U16), "os": (16, U16), "ot": (16, U16), "ow": (32, U16), "t16": (16, F16),
+    "xd": (32, BF), "mk": (256, BF), "t2": (256, F32), "t3": (256, F32), "nw": (256, F32), "yro": (512, BF),
+}
+for _i in range(9):
+    SB["snd%d" % _i] = (224, BF)
+    SB["lnd%d" % _i] = (224, BF)
+SCRATCH = {k: ("sbuf", [128, v[0]], v[1]) for k, v in SB.items()}
+for _i in range(8):
+    SCRATCH["ps%d" % _i] = ("psum", [128, 512], F32)
+SEMAPHORES = ["cv", "cs", "ct", "cg", "loc"] + ["arr%d" % i for i in range(9)] + ["dm%d" % i for i in range(16)]
+
+
+def chunks(sizes):
+    out, a = [], 0
+    for n in sizes:
+        out.append((a, a + n)); a += n
+    return out
+
+
+def rank_program(g, core, T, topo):
+    rank = T.rank_of(core)
+    if rank is None:
+        return
+    Q = {"v": g.vector, "s": g.scalar, "t": g.tensor, "g": g, "y": g.sync}
+    cnt = {"v": 0, "s": 0, "t": 0, "g": 0}
+    seen = {e: {} for e in Q}
+    hist = {}
+    ends = {}
+    ndma = [0]
+
+    def A(name, lo=0, hi=None, st=1):
+        if hi is None:
+            hi = SCRATCH[name][1][1]
+        ap = T[name][:, lo:hi] if st == 1 else T[name][:, lo:hi:st]
+        return (ap, [(name, lo, hi)])
+
+    def X(win, off):
+        return (win[0].indirect(off[0]), win[1] + off[1])
+
+    def order(e, w, r):
+        need = {}
+        for regs, isw in ((r, False), (w, True)):
+            for name, lo, hi in regs:
+                ps = name[:2] == "ps"
+                for (a, b, sem, n, who, ww) in hist.get(name, ()):
+                    if who == e:
+                        hit = (ww or isw) and e != "t" and a < hi and lo < b
+                    else:
+                        hit = ps or ((ww or isw) and a < hi and lo < b)
+                    if hit and need.get(sem, 0) < n:
+                        need[sem] = n
+        for sem, n in need.items():
+            if seen[e].get(sem, 0) < n:
+                Q[e].wait_ge(T.sem[sem], n); seen[e][sem] = n
+
+    def note(w, r, sem, n, who):
+        for regs, isw in ((r, False), (w, True)):
+            for name, lo, hi in regs:
+                h = hist.setdefault(name, [])
+                if isw:
+                    h[:] = [x for x in h if not (lo <= x[0] and x[1] <= hi and (x[4] == who or name[:2] != "ps"))]
+                else:
+                    h[:] = [x for x in h if not (x[4] == who and not x[5] and lo <= x[0] and x[1] <= hi)]
+                h.append((lo, hi, sem, n, who, isw))
+        ends[sem] = n
+
+    def do(e, f, w, r, inc=True, scat=False):
+        wr = list(w[1]); rr = [x for o in r for x in o[1]]
+        if scat:
+            rr += wr[1:]; wr = wr[:1]
+        order(e, wr, rr)
+        ins = f()
+        if inc:
+            cnt[e] += 1; ins.then_inc(T.sem["c" + e], 1)
+        note(wr, rr, "c" + e, cnt[e] + (0 if inc else 1), e)
+
+    def dma(e, f, w, r):
+        wr = [x for o in w for x in o[1]]; rr = [x for o in r for x in o[1]]
+        order(e, wr, rr)
+        sem = "dm%d" % ndma[0]; ndma[0] += 1
+        f().then_inc(T.sem[sem], 16)
+        note(wr, rr, sem, 16, sem)
+
+    def cp(o, i, scat=False): do("v", lambda: g.vector.tensor_copy(o[0], i[0]), o, [i], scat=scat)
+    def tt(o, a, b, op): do("v", lambda: g.vector.tensor_tensor(o[0], a[0], b[0], op), o, [a, b])
+    def ms(o, c): do("v", lambda: g.vector.memset(o[0], c), o, [])
+    def tr(o, i): do("v", lambda: g.vector.transpose(o[0], i[0]), o, [i])
+    def sc(o, a, b, o0, o1): do("v", lambda: g.vector.tensor_tensor_scan(o[0], a[0], b[0], 0.0, o0, o1), o, [a, b])
+
+    def ts(o, a, s1, o0, s2=None, o1=None):
+        r = [a] + [s for s in (s1, s2) if isinstance(s, tuple)]
+        v1 = s1[0] if isinstance(s1, tuple) else s1
+        v2 = s2[0] if isinstance(s2, tuple) else s2
+        if o1 is None:
+            do("v", lambda: g.vector.tensor_scalar(o[0], a[0], v1, None, o0), o, r)
+        else:
+            do("v", lambda: g.vector.tensor_scalar(o[0], a[0], v1, v2, o0, o1), o, r)
+
+    def act(o, i, scale=1.0, bias=0.0):
+        do("s", lambda: g.scalar.activation(o[0], i[0], Fn.Copy, bias=bias, scale=scale), o, [i])
+
+    def mm(o, l, r, st, sp, inc=None):
+        do("t", lambda: g.tensor.matmul(o[0], l[0], r[0], st, sp), o, [l, r], inc=sp if inc is None else inc)
+
+    def iota(o, pat, base, cm, fl=True):
+        if fl:
+            do("g", lambda: g.iota(o[0], pat, base, cm, allow_small_or_imprecise_dtypes=True), o, [])
+        else:
+            do("g", lambda: g.iota(o[0], pat, base, cm), o, [])
+
+    def sel(o, i, pat, op, fill, base, cm):
+        do("g", lambda: g.affine_select(o[0], i[0], pat, op, fill, base, cm), o, [i])
+
+    def strip(o, i): ts(o, i, M16, Op.add, M16, Op.subtract)
+    def S(j): return A("sm", 16 * j, 16 * j + 16)
+    def LI(j): return A("li", 16 * j, 16 * j + 16)
+    def LC(j): return A("lc", 16 * j, 16 * j + 16)
+    def PF(j): return A("pf", j, j + 1)
+    def BD(l): return A("bdo", 14 * l, 14 * l + 14)
+    def AT(l): return A("W", A0 + 512 * l, A0 + 512 * l + 512)
+    TW = A("TT")
+
+    def send(x):
+        order("g", [], A("snd%d" % x)[1])
+        trs = []
+        used = [0, 0]
+        for d in range(1, 8):
+            dst = T.cores[rank ^ d]
+            rid, pid, _ = topo.addr(dst)
+            en = topo.engines(core, dst)
+            k = len(en) // 8
+            same = int(topo.die(dst) == topo.die(core))
+            mine = en[same::2][used[same]:used[same] + k]
+            used[same] += k
+            trs.append(RemoteDMATransfer(dst_ids=[DstId(rid=rid, pnc=pid)], dma_engine_mask=sum(1 << e for e in mine),
+                                         remote_sem=T.sem["arr%d" % x], src=A("snd%d" % x, 32 * d - 32, 32 * d)[0], dst=A("lnd%d" % x, 32 * d - 32, 32 * d)[0]))
+        g.remote_dma_fused(trs, local_sem=T.sem.loc)
+        ends["loc"] = ends.get("loc", 0) + 7 * k
+        note(A("lnd%d" % x)[1], [], "arr%d" % x, 7 * k, "arr")
+
+    def ghosts_pe(x):
+        for d in range(1, 8):
+            mm(A("ps3", 32 * d - 32, 32 * d), A(("ident", "pm1", "pm2")[d % 3]), A("lnd%d" % x, 32 * d - 32, 32 * d), True, True, inc=d == 7)
+
+    def ghosts_v(x):
+        l = x % 3
+        tt(A("TT", 2048 + 224 * l, 2272 + 224 * l), A("ps3", 0, 224), A("gc0", 224 * l, 224 * l + 224), Op.add)
+
+    def pair_ps(l):
+        return ("ps4", 0) if l == 1 else (("ps5", 0) if l == 2 else ("ps7", 0))
+
+    def pairs_pe(l, par):
+        n = NP if l < 3 else NPT
+        b, c0 = pair_ps(l)
+        for h in (0, 1):
+            for a in (0, 1):
+                r = A("W", DCOL[l] + a, DCOL[l] + n, 2) if l < 3 else A("W", DB + par + 2 * a, DB + 2 * n, 4)
+                mm(A(b, c0 + h * n // 2, c0 + (h + 1) * n // 2), A("pp", 256 * h + 128 * a, 256 * h + 128 * a + 128), r, a == 0, a == 1, inc=h + a == 2)
+
+    def pairs_v(l):
+        n = NP if l < 3 else NPT
+        b, c0 = pair_ps(l)
+        cp(A("op%d" % l), A(b, c0, c0 + n))
+
+    def plain_v(l, par):
+        if l < 3:
+            cp(A("on%d" % l), A("W", DCOL[l] + NP, DCOL[l] + 512))
+        else:
+            cp(A("on3"), A("W", DB + 2 * NPT + par, DB + 512, 2))
+
+    def released(l): strip(A("abd", 224 * l - 224, 224 * l), X(AT(l), BD(l)))
+
+    def level(l, x):
+        n, m = (NP, 512 - NP) if l < 3 else (NPT, 256 - NPT)
+        o, on = "op%d" % l, "on%d" % l
+        pc, nc = chunks(PC[n]), chunks(NC[m])
+        for j, (a, b) in enumerate(pc):
+            if j == 0:
+                ts(A("gs", 16 * a, 16 * b), X(TW, A(o, n // 2 + a, n // 2 + b)), -4096.0, Op.add)
+            else:
+                act(A("gs", 16 * a, 16 * b), X(TW, A(o, n // 2 + a, n // 2 + b)), bias=-4096.0)
+        for a, b in nc[:2]:
+            act(A("gn", 16 * a, 16 * b), X(TW, A(on, a, b)))
+        for a, b in pc:
+            tt(A("gp", 16 * a, 16 * b), X(TW, A(o, a, b)), A("gs", 16 * a, 16 * b), Op.min)
+        for a in range(0, 8 * n, 1024):
+            b = min(a + 1024, 8 * n)
+            sc(A("sp", a, b), A("dP", 0, b - a), A("gp", a, b), Op.add, Op.min)
+        for a, b in nc[2:]:
+            act(A("gn", 16 * a, 16 * b), X(TW, A(on, a, b)))
+        if l < 3:
+            act(A("hi", 0, n), A("sp", 7, 8 * n, 8), 1.0, M16)
+            act(A("hb", 0, n), A("hi", 0, n), 1.0, -M16)
+        for a, b in nc:
+            sc(A("sn", 16 * a, 16 * b), A("dN", 0, 16 * (b - a)), A("gn", 16 * a, 16 * b), Op.add, Op.min)
+        if l < 3:
+            strip(A("hb", n, 512), A("sn", 15, 16 * m, 16))
+            tt(A("snd%d" % x), X(A("hb"), BD(l)), A("abd", 224 * l - 224, 224 * l), Op.min)
+            send(x)
+            tt(A("ps2"), A("ps%d" % (l - 1)), A("hb"), Op.add)
+            tt(A("TT", 512 * l, 512 * l + 512), A("ps2"), AT(l), Op.min)
+            act(A("KC", KCOL[l], KCOL[l] + n), A("sp", 7, 8 * n, 8))
+            act(A("KC", KCOL[l] + n, KCOL[l] + 512), A("sn", 15, 16 * m, 16))
+
+    def to_list(j):
+        for h, b in zip((0, 128), HB[j]):
+            sc(A("ll", h, h + 128), A("dC", 0, 128), A(b, 0, 128), Op.add, Op.max)
+        cp(LI(j), A("ll", 15, 256, 16))
+        ts(LI(j + 3), LI(j), 4095, Op.bitwise_and)
+
+    HB = (("ps4", "ps7"), ("ps6", "ps2"), ("ps4", "ps7"))
+
+    def pre(j):
+        for b in HB[j]:
+            mm(A(b, 0, 128), A("ident"), A("ng", 0, 128), True, False)
+
+    def pick(j, src):
+        for h, b in zip((0, 128), HB[j]):
+            tt(A("mm", h, h + 128), src(h), A("mp", h, h + 128), Op.mult)
+            mm(A(b, 0, 128), A("bo"), A("mm", h, h + 128), False, True)
+
+    def hop(h): return X(A("KC"), A("oh", h // 16, h // 16 + 8))
+
+    def plain_a(lo, hi):
+        act(A("W", lo, hi), A("W", lo, hi), 2.0 ** -16, M0)
+        act(A("W", lo, hi), A("W", lo, hi), 1.0, -M0)
+
+    def odd_scan(j): sc(A("so", 1024 * j, 1024 * j + 1024), A("dO"), A("go", 1024 * j, 1024 * j + 1024), Op.add, Op.min)
+    def odd_get(j): act(A("go", 1024 * j, 1024 * j + 1024), X(TW, A("ono", 64 * j, 64 * j + 64)), 2.0 ** -16, -0.4375)
+
+    def walk(t):
+        par, last = t & 1, t == 2
+        K0 = A("ps2", 0, 256)
+        pre(0)
+        mm(A("ps5"), A("ident"), A("c30"), True, False)
+        mm(A("ps3", 0, 256), A("ident"), A("tri"), True, False)
+        if last:
+            odd_get(0)
+        tt(A("ps2", 0, NPT), A("sp", 7, 8 * NPT, 8), A("ps6", 0, NPT), Op.min)
+        tt(A("ps2", NPT, 256), A("sn", 15, 16 * (256 - NPT), 16), A("ps6", NPT, 256), Op.min)
+        strip(A("rt"), K0)
+        act(A("KC", 0, 256), K0)
+        if last:
+            odd_get(1)
+            plain_a(A0 + 1536, A0 + 2048)
+            act(A("yro", 0, 512, 2), A("rt"), 2.0 ** -16)
+            odd_get(2); odd_get(3)
+        tr(A("rtt"), A("rt"))
+        sc(A("ax"), A("dX"), A("rtt"), Op.add, Op.max)
+        strip(S(0), A("ax", 15, 256, 16))
+        tt(S(1), A("ax", 15, 256, 16), S(0), Op.subtract)
+        tt(A("mt"), X(S(1), A("oc")), A("cp"), Op.is_equal)
+        tr(A("mp"), A("mt"))
+        pick(0, lambda h: A("ps2", h, h + 128))
+        pre(1)
+        if last:
+            odd_scan(0)
+        to_list(0)
+        pre(2)
+        tt(S(2), LI(3), LC(1), Op.max)
+        ts(A("oh"), S(2), -2816.0, Op.add)
+        pick(1, hop)
+        v, bv, ok, nm, s, al, base = LI(6), S(3), S(4), S(5), S(6), S(7), S(10)
+        u = 2.0 ** -16 if last else 1.0
+        ts(v, LI(0), 0xFF0000, Op.bitwise_and)
+        ts(nm, LI(3), 1.0, Op.is_equal)
+        tt(bv, LC(6 + par), v, Op.subtract)
+        ts(S(11), v, 2.0 ** 20, Op.min, -u, Op.mult)
+        ts(ok, bv, 0.0, Op.is_le)
+        ts(S(12), bv, 0.0, Op.max, u, Op.mult)
+        tt(s, ok, nm, Op.max)
+        tt(S(11), S(11), ok, Op.mult)
+        tt(S(12), S(12), nm, Op.mult)
+        ts(S(8), s, 2.0 ** 20, Op.mult)
+        tt(A("xd", 16, 32), S(11), S(12), Op.add)
+        tt(A("xd", 0, 16), S(8), v, Op.subtract)
+        for r in range(16):
+            mm(A("ps5", r, 512, 16), A("slt", 128 * r, 128 * r + 128), A("xd"), False, False)
+        to_list(1)
+        tt(S(14), LI(4), S(2), Op.max)
+        ts(A("oh"), S(14), -2816.0, Op.add)
+        pick(2, hop)
+        mm(A("ps5", 0, 256), A("bo"), A("mm"), False, True)
+        ts(S(15), S(14), 3072.0, Op.is_lt)
+        tt(S(13), nm, LC(2 + par), Op.mult)
+        ts(S(16), s, -1.0, Op.mult, 1.0, Op.add)
+        tt(S(15), S(15), LC(4 + par), Op.mult)
+        ts(S(9), S(14), float(DB - 2560), Op.add)
+        tt(al, ok, nm, Op.is_gt)
+        ts(S(13), S(13), -1808.0, Op.add)
+        tt(S(15), S(15), S(9), Op.add)
+        ts(al, al, 2056.0, Op.mult)
+        tt(S(15), S(15), S(16), Op.mult)
+        tt(base, S(15), S(13), Op.add)
+        to_list(2)
+        tt(S(17), LI(5), al, Op.min)
+        tt(A("t16"), S(17), base, Op.add)
+        for k in range(1, 16):
+            mm(A("ps3", k, 256, 16), A("sh", 128 * k - 128, 128 * k), A("t16"), False, k == 15)
+        ts(A("os"), LI(5), 0.0, Op.add)
+        ts(A("ot"), A("t16"), 1808.0, Op.add)
+        ts(S(18), A("t16"), PF(4), Op.subtract)
+        ts(A("mk"), A("ps5", 0, 256), M12, Op.add, PF(2), Op.is_equal)
+        tt(A("ps2", 0, 256), A("ps5", 256, 512), A("mp"), Op.mult)
+        tt(A("t2"), X(A("SD"), A("os")), A("mk"), Op.mult)
+        sc(A("ax"), A("ps3", 0, 256), A("dD"), Op.mult, Op.add)
+        tt(A("t3"), A("ps2", 0, 256), A("t2"), Op.add)
+        ts(S(19), A("ax", 15, 256, 16), 0.0, Op.not_equal)
+        tt(A("nw"), X(A("W"), A("ot")), A("t3"), Op.add)
+        tt(S(19), S(19), S(18), Op.mult)
+        ts(A("ow", 0, 32, 2), S(19), PF(3), Op.add)
+        for c in range(15, -1, -1):
+            cp(X(A("W"), A("ow", 2 * c, 2 * c + 1)), A("nw", 16 * c, 16 * c + 16), scat=True)
+
+    dma("y", lambda: g.sync.dma_start(T.bds[:], T.bd[:]), [A("bds")], [])
+    dma("s", lambda: g.scalar.dma_start(T.avs[:, 0:512], T.av[:, 0:512]), [A("avs", 0, 512)], [])
+    dma("y", lambda: g.sync.dma_start(T.dps[:, 0:512], T.dp[:, 0:512]), [A("dps", 0, 512)], [])
+    dma("s", lambda: g.scalar.dma_start(T.avs[:, 512:2048], T.av[:, 512:2048]), [A("avs", 512, 2048)], [])
+    dma("y", lambda: g.sync.dma_start(T.dps[:, 512:1536], T.dp[:, 512:1536]), [A("dps", 512, 1536)], [])
+    ms(A("one"), 1.0); ms(A("oneb"), 1.0)
+    iota(A("ramp"), [[1, 512]], 28680, 0)
+    for h in (0, 1):
+        for a in (0, 1):
+            sel(A("pp", 256 * h + 128 * a, 256 * h + 128 * a + 128), A("one"), [[-16, 8], [200, 2], [-2, 8]], Op.is_equal, 0.0, -200 * a - (1 - h), 1)
+    iota(A("pi", 0, 1), [[0, 1]], 0, 1, False)
+    ms(A("dP"), -8192.0); ms(A("dN"), -4096.0)
+    ms(A("dP", 0, 1024, 8), 2.0 ** 25); ms(A("dN", 0, 1024, 16), 2.0 ** 25)
+    ms(A("TT", 2272, 2728), 255.0 * 65536 + 28680 + 2720)
+    act(A("ps0"), A("ramp"), 1.0, 3064.0 + 512)
+    for a in (512, 1024, 1536):
+        act(A("TT", a, a + 512), A("ramp"))
+    cp(A("bdo"), A("bds"))
+    ts(A("snd0"), X(A("avs", 0, 512), BD(0)), 65536.0, Op.mult)
+    send(0)
+    sel(A("pm1"), A("oneb"), [[16, 8], [-1, 16]], Op.is_equal, 0.0, -112, 1)
+    sel(A("pm2", 16, 128), A("oneb", 16, 128), [[16, 7], [-1, 16]], Op.is_equal, 0.0, -112, 1)
+    sel(A("pm2", 0, 16), A("oneb", 0, 16), [[-1, 16]], Op.is_equal, 0.0, 0, 1)
+    sel(A("ident"), A("oneb"), [[-1, 128]], Op.is_equal, 0.0, 0, 1)
+    iota(A("gc0"), [[1, 672]], 28680 + 2048, 0)
+    act(A("tmp", 0, 512), A("avs", 0, 512), 65536.0, -3576.0)
+    cp(A("W", DCOL[1], DCOL[1] + 512), A("dps", 0, 512))
+    pairs_pe(1, 0)
+    tt(A("TT", 0, 512), A("ps0"), A("tmp", 0, 512), Op.add)
+    plain_v(1, 0)
+    act(A("tmp", 512, 1024), A("avs", 512, 1024), 65536.0, -3064.0)
+    act(A("ps1"), A("ramp"), 1.0, 2040.0 + 1024)
+    tt(AT(1), A("ps0"), A("tmp", 512, 1024), Op.add)
+    released(1)
+    ts(A("gi", 0, 1), A("pi", 0, 1), 4, Op.arith_shift_right)
+    cp(A("W", DCOL[2], DCOL[2] + 512), A("dps", 512, 1024))
+    pairs_v(1)
+    iota(A("colr"), [[0, 16], [1, 16]], 0, 0)
+    iota(LC(0), [[16, 16]], 0, 1)
+    iota(LC(9), [[1, 16]], 0, 0)
+    sel(A("bo"), A("one"), [[-16, 8], [0, 16]], Op.is_ge, 0.0, 0, 1)
+    sel(A("bo"), A("bo"), [[16, 8], [0, 16]], Op.is_ge, 0.0, 15, -1)
+    act(A("sh"), A("avs", 0, 1920), 0.0, 1.0 / 64)
+    dma("g", lambda: g.indirect_dma_start(T.sbs[:], None, T.sb[:], IndirectOffsetOnAxis(ap=T.gi[:, 0:1], axis=0), bounds_check=7), [A("sbs")], [A("gi")])
+    dma("g", lambda: g.indirect_dma_start(T.ths[:], None, T.th[:], IndirectOffsetOnAxis(ap=T.gi[:, 0:1], axis=0), bounds_check=7), [A("ths")], [A("gi")])
+    sel(A("sh"), A("sh"), [[-1, 15], [1, 128]], Op.is_equal, 0.0, -1, -1)
+
+    def setup1():
+        act(A("tmp", 1024, 1536), A("avs", 1024, 1536), 65536.0, -2040.0)
+        act(AT(3), A("avs", 1536, 2048), 65536.0, -32767.0)
+        act(AT(0), A("TT", 0, 512))
+        iota(A("SD"), [[-1, 2736]], 8, 0, False)
+        dma("g", lambda: g.dma_start(T.SD[:, 8:1544], T.sbs[:, 0:1536], accum_op=Op.add), [A("SD", 8, 1544)], [A("sbs"), A("SD", 8, 1544)])
+        dma("g", lambda: g.dma_start(T.SD[:, 2056:2728], T.sbs[:, 1536:2208], accum_op=Op.add), [A("SD", 2056, 2728)], [A("sbs"), A("SD", 2056, 2728)])
+        sel(A("sh"), A("sh"), [[0, 15], [1, 128]], Op.not_equal, -1.0 / 64, 0, -1)
+        tt(AT(2), A("ps1"), A("tmp", 1024, 1536), Op.add)
+        cp(A("W", DB, DB + 512), A("dps", 1024, 1536))
+        released(2)
+        ts(A("pi", 1, 2), A("pi", 0, 1), 15, Op.bitwise_and)
+        ts(PF(1), A("gi", 0, 1), 16.0, Op.mult)
+        cp(PF(0), A("pi", 1, 2))
+        ms(A("W", 0, A0), 0.0); ms(A("W", A0 + 2048, DB), 0.0)
+        ms(A("dX"), 2048.0); ms(A("dC"), 0.0); ms(A("dD"), 0.0); ms(A("c30", 0, 256), 30720.0); ms(A("c30", 256, 512), 0.0)
+
+    def setup2():
+        sel(A("sh"), A("sh"), [[-1, 15], [0, 8], [1, 16]], Op.is_ge, 0.0, -1, 0)
+        ts(LC(0), LC(0), PF(1), Op.subtract)
+        ts(PF(2), PF(0), 4096.0, Op.mult, M12, Op.add)
+        ts(PF(3), PF(0), 2064.0, Op.add)
+        ts(PF(4), PF(0), 256.0, Op.add)
+        ts(A("dg"), A("colr"), PF(0), Op.is_equal)
+        ts(A("tri"), A("colr"), PF(0), Op.is_gt)
+        act(A("ng"), A("dg"), 2.0 ** 25 + 32768, -2.0 ** 25)
+        act(A("cp"), A("colr"), -2048.0, 30720.0)
+        act(A("bob"), A("bo"))
+        for r in range(16):
+            do("s", lambda: g.scalar.activation(T.slt[:, 128 * r:128 * r + 128], T.bob[:], Fn.Copy, scale=T.dg[:, r:r + 1]), A("slt", 128 * r, 128 * r + 128), [A("bob"), A("dg")])
+        cp(A("oc"), LC(9))
+        ms(A("dX", 0, 256, 16), -2.0 ** 25); ms(A("dC", 0, 256, 16), -2.0 ** 26); ms(A("dD", 0, 256, 16), 1.0)
+        ts(LC(1), LC(0), 2816.0, Op.add)
+        for par in (0, 1):
+            ts(LC(2 + par), LC(0), 2.0, Op.mult, 1536.0 + A0 + par, Op.add)
+            ts(LC(4 + par), LC(0), par - 256.0, Op.add)
+
+    def thresholds(par):
+        tt(A("mm"), A("ths", par, 512, 2), A("ng"), Op.add)
+        sc(A("ll"), A("dC"), A("mm"), Op.add, Op.max)
+        ts(LC(6 + par), A("ll", 15, 256, 16), -32768.0, Op.add, 65536.0, Op.mult)
+
+    for t in range(3):
+        par = t & 1
+        if t > 0:
+            strip(A("snd%d" % (3 * t)), X(AT(0), BD(0)))
+            send(3 * t)
+            act(A("TT", 0, 512), AT(0))
+            pairs_pe(1, par)
+            plain_v(1, par); released(1); plain_v(2, par); released(2); plain_v(3, par)
+            if t == 2:
+                cp(A("ono"), A("W", DB + 1, DB + 512, 2))
+                ms(A("dO"), 0.0); ms(A("dO", 0, 1024, 16), 1024.0)
+            else:
+                thresholds(1)
+            pairs_v(1)
+        ghosts_pe(3 * t)
+        pairs_pe(2, par)
+        ghosts_v(3 * t)
+        if t > 0:
+            pairs_pe(3, par)
+        level(1, 3 * t + 1)
+        pairs_v(2)
+        if t == 0:
+            plain_v(2, par)
+            setup1()
+        else:
+            pairs_v(3)
+        ghosts_pe(3 * t + 1)
+        if t == 0:
+            pairs_pe(3, par)
+        ghosts_v(3 * t + 1)
+        level(2, 3 * t + 2)
+        act(A("ps6", 0, 256), A("W", A0 + 1536 + par, A0 + 2048, 2))
+        if t == 0:
+            pairs_v(3); plain_v(3, par)
+            setup2(); thresholds(0)
+        if t == 2:
+            plain_a(A0, A0 + 1536)
+        ghosts_pe(3 * t + 2)
+        ghosts_v(3 * t + 2)
+        level(3, None)
+        walk(t)
+
+    dma("g", lambda: g.dma_start(T.ya[:], T.W[:, A0:A0 + 2048]), [], [A("W")])
+    for l, e in ((1, "y"), (2, "s"), (3, "y")):
+        dma(e, lambda: Q[e].dma_start(T.yd[:, 512 * l - 512:512 * l], T.W[:, DCOL[l]:DCOL[l] + 512]), [], [A("W")])
+    odd_scan(1); odd_scan(2); odd_scan(3)
+    ts(A("mm"), A("so", 15, 4096, 16), M0, Op.add, M0, Op.subtract)
+    tt(A("yro", 1, 512, 2), A("mm"), A("W", A0 + 1537, A0 + 2048, 2), Op.min)
+    dma("s", lambda: g.scalar.dma_start(T.yr[:], T.yro[:]), [], [A("yro")])
+    for sem, n in ends.items():
+        g.sync.wait_ge(T.sem[sem], n)

@@ -4,26 +4,27 @@ from concourse.mybir import AluOpType as Op, ActivationFunctionType as Fn
 F32, BF, I32, U16, F16 = "float32", "bfloat16", "int32", "uint16", "float16"
 NP = 304
 NPT = 144
-PC = {NP: (16, 32, 32, 36, 36), NPT: (16, 24, 32)}
+PC = {NP: (16, 8, 24, 32, 36, 36), NPT: (16, 8, 24, 24)}
 NC = {512 - NP: (64, 64, 48, 16, 16), 256 - NPT: (48, 32, 16, 16)}
-A0, DB, WN = 8, 2080, 3616
+A0, DB, WN = 8, 2128, 3664
 DCOL = {1: DB + 1024, 2: DB + 512, 3: DB}
 KCOL = {1: 768, 2: 256}
 M16, M12, M0 = 1.5 * 2 ** 39, 1.5 * 2 ** 35, 1.5 * 2 ** 23
 SB = {
     "avs": (2048, BF), "dps": (1536, I32), "bds": (42, I32), "bdo": (42, U16), "sbs": (2208, I32), "ths": (512, I32),
-    "W": (WN, F32), "TT": (2728, F32), "KC": (1280, F32), "SD": (2736, I32),
+    "W": (WN, F32), "TT": (2728, F32), "KC": (1280, F32), "KN": (1280, F32), "SD": (2736, I32), "ki": (512, I32), "pc": (512, F32),
     "gs": (8 * NP, F32), "gp": (8 * NP, F32), "sp": (8 * NP, F32), "gn": (16 * (512 - NP), F32), "sn": (16 * (512 - NP), F32),
     "go": (4096, BF), "so": (4096, BF), "hi": (512, F32), "hb": (512, BF), "abd": (448, BF), "tmp": (1536, F32),
     "on1": (512 - NP, U16), "on2": (512 - NP, U16), "on3": (256 - NPT, U16), "ono": (256, U16),
     "op1": (NP, U16), "op2": (NP, U16), "op3": (NPT, U16),
-    "dN": (1024, BF), "dP": (1024, BF), "dO": (1024, BF), "dX": (256, BF), "dC": (256, BF), "dD": (256, BF), "c30": (512, BF),
+    "dN": (1024, BF), "dP": (1024, BF), "dO": (1024, BF), "dX": (256, BF), "dC": (256, BF), "dD": (256, BF), "dE": (768, BF), "c30": (256, BF),
     "ramp": (512, F32), "gc0": (672, F32), "one": (128, F32), "oneb": (128, BF), "ident": (128, BF), "pm1": (128, BF), "pm2": (128, BF),
-    "bo": (128, F32), "bob": (128, BF), "pp": (512, F32), "sh": (1920, BF), "slt": (2048, BF), "colr": (256, F32), "dg": (256, F32), "ng": (256, BF),
-    "tri": (256, BF), "cp": (256, F32), "pi": (4, I32), "gi": (4, I32), "pf": (8, F32), "lc": (160, F32), "oc": (16, U16),
-    "rt": (256, BF), "rtt": (256, BF), "ax": (256, F32), "mt": (256, BF), "mp": (256, BF), "mm": (256, F32), "ll": (256, F32),
-    "li": (128, I32), "sm": (512, F32), "oh": (16, U16), "os": (16, U16), "ot": (16, U16), "ow": (32, U16), "t16": (16, F16),
-    "xd": (32, BF), "mk": (256, BF), "t2": (256, F32), "t3": (256, F32), "nw": (256, F32), "yro": (512, BF),
+    "bo": (128, F32), "bob": (128, BF), "nbo": (128, BF), "pp": (512, F32), "sh": (1920, BF), "slt": (2048, BF), "colr": (256, F32),
+    "dg": (256, F32), "ng": (256, BF), "tri": (256, BF), "pi": (4, I32), "gi": (4, I32), "pf": (8, F32), "lc": (160, F32), "oc": (16, U16),
+    "rt": (256, BF), "rtt": (256, BF), "ax": (256, F32), "mt": (256, BF), "mp": (256, BF), "mm": (256, F32), "ll": (256, F32), "l1": (256, F32),
+    "li": (128, I32), "sm": (512, F32), "oh": (16, U16), "os": (16, U16), "ot": (16, U16), "ow": (16, U16), "t16": (32, F16), "m16": (256, F16),
+    "rm": (256, BF), "mq": (256, BF), "ne": (768, BF), "kp": (768, BF), "mk": (256, BF), "t2": (256, F32), "t3": (256, F32), "nw": (256, F32),
+    "yro": (512, BF),
 }
 for _i in range(9):
     SB["snd%d" % _i] = (224, BF)
@@ -105,8 +106,8 @@ def rank_program(g, core, T, topo):
         f().then_inc(T.sem[sem], 16)
         note(wr, rr, sem, 16, sem)
 
-    def cp(o, i, scat=False): do("v", lambda: g.vector.tensor_copy(o[0], i[0]), o, [i], scat=scat)
-    def tt(o, a, b, op): do("v", lambda: g.vector.tensor_tensor(o[0], a[0], b[0], op), o, [a, b])
+    def cp(o, i): do("v", lambda: g.vector.tensor_copy(o[0], i[0]), o, [i])
+    def tt(o, a, b, op, scat=False): do("v", lambda: g.vector.tensor_tensor(o[0], a[0], b[0], op), o, [a, b], scat=scat)
     def ms(o, c): do("v", lambda: g.vector.memset(o[0], c), o, [])
     def tr(o, i): do("v", lambda: g.vector.transpose(o[0], i[0]), o, [i])
     def sc(o, a, b, o0, o1): do("v", lambda: g.vector.tensor_tensor_scan(o[0], a[0], b[0], 0.0, o0, o1), o, [a, b])
@@ -205,7 +206,7 @@ def rank_program(g, core, T, topo):
                 act(A("gs", 16 * a, 16 * b), X(TW, A(o, n // 2 + a, n // 2 + b)), bias=-4096.0)
         for a, b in nc[:2]:
             act(A("gn", 16 * a, 16 * b), X(TW, A(on, a, b)))
-        for a, b in pc:
+        for a, b in [pc[1], pc[0]] + pc[2:]:
             tt(A("gp", 16 * a, 16 * b), X(TW, A(o, a, b)), A("gs", 16 * a, 16 * b), Op.min)
         for a in range(0, 8 * n, 1024):
             b = min(a + 1024, 8 * n)
@@ -218,7 +219,9 @@ def rank_program(g, core, T, topo):
         for a, b in nc:
             sc(A("sn", 16 * a, 16 * b), A("dN", 0, 16 * (b - a)), A("gn", 16 * a, 16 * b), Op.add, Op.min)
         if l < 3:
-            strip(A("hb", n, 512), A("sn", 15, 16 * m, 16))
+            a = nc[-1][0]
+            strip(A("hb", n, n + a), A("sn", 15, 16 * a, 16))
+            strip(A("hb", n + a, 512), A("sn", 16 * a + 15, 16 * m, 16))
             tt(A("snd%d" % x), X(A("hb"), BD(l)), A("abd", 224 * l - 224, 224 * l), Op.min)
             send(x)
             tt(A("ps2"), A("ps%d" % (l - 1)), A("hb"), Op.add)
@@ -226,24 +229,22 @@ def rank_program(g, core, T, topo):
             act(A("KC", KCOL[l], KCOL[l] + n), A("sp", 7, 8 * n, 8))
             act(A("KC", KCOL[l] + n, KCOL[l] + 512), A("sn", 15, 16 * m, 16))
 
-    def to_list(j):
-        for h, b in zip((0, 128), HB[j]):
-            sc(A("ll", h, h + 128), A("dC", 0, 128), A(b, 0, 128), Op.add, Op.max)
-        cp(LI(j), A("ll", 15, 256, 16))
-        ts(LI(j + 3), LI(j), 4095, Op.bitwise_and)
-
     HB = (("ps4", "ps7"), ("ps6", "ps2"), ("ps4", "ps7"))
+
+    def diag(j, out):
+        for h, b in zip((0, 128), HB[j]):
+            sc(A(out, h, h + 128), A("dC", 0, 128), A(b, 0, 128), Op.add, Op.max)
 
     def pre(j):
         for b in HB[j]:
             mm(A(b, 0, 128), A("ident"), A("ng", 0, 128), True, False)
 
-    def pick(j, src):
+    def pick(j, src, buf="mm", ones="bo"):
         for h, b in zip((0, 128), HB[j]):
-            tt(A("mm", h, h + 128), src(h), A("mp", h, h + 128), Op.mult)
-            mm(A(b, 0, 128), A("bo"), A("mm", h, h + 128), False, True)
+            tt(A(buf, h, h + 128), src(h), A("mp", h, h + 128), Op.mult)
+            mm(A(b, 0, 128), A(ones), A(buf, h, h + 128), False, True)
 
-    def hop(h): return X(A("KC"), A("oh", h // 16, h // 16 + 8))
+    def hop(tab): return lambda h: X(A(tab), A("oh", h // 16, h // 16 + 8))
 
     def plain_a(lo, hi):
         act(A("W", lo, hi), A("W", lo, hi), 2.0 ** -16, M0)
@@ -256,7 +257,7 @@ def rank_program(g, core, T, topo):
         par, last = t & 1, t == 2
         K0 = A("ps2", 0, 256)
         pre(0)
-        mm(A("ps5"), A("ident"), A("c30"), True, False)
+        mm(A("ps5", 0, 256), A("ident"), A("c30"), True, False)
         mm(A("ps3", 0, 256), A("ident"), A("tri"), True, False)
         if last:
             odd_get(0)
@@ -266,75 +267,85 @@ def rank_program(g, core, T, topo):
         act(A("KC", 0, 256), K0)
         if last:
             odd_get(1)
-            plain_a(A0 + 1536, A0 + 2048)
+            plain_a(A0 + 1024, A0 + 2048)
             act(A("yro", 0, 512, 2), A("rt"), 2.0 ** -16)
             odd_get(2); odd_get(3)
         tr(A("rtt"), A("rt"))
         sc(A("ax"), A("dX"), A("rtt"), Op.add, Op.max)
-        strip(S(0), A("ax", 15, 256, 16))
-        tt(S(1), A("ax", 15, 256, 16), S(0), Op.subtract)
-        tt(A("mt"), X(S(1), A("oc")), A("cp"), Op.is_equal)
+        tt(A("t2"), A("ps6", 256, 512), A("rtt"), Op.add)
+        tt(A("mt"), X(A("ax"), A("oc")), A("t2"), Op.is_equal)
         tr(A("mp"), A("mt"))
         pick(0, lambda h: A("ps2", h, h + 128))
         pre(1)
-        if last:
-            odd_scan(0)
-        to_list(0)
+        tt(A("rm"), A("rt"), A("mp"), Op.mult)
+        mm(A("ps5", 0, 256), A("nbo"), A("rm"), False, False)
+        act(A("mq"), A("mp"), 1.0 if last else 65536.0)
+        diag(0, "ll")
+        cp(LI(0), A("ll", 15, 256, 16))
+        ts(LI(3), LI(0), 4095, Op.bitwise_and)
         pre(2)
         tt(S(2), LI(3), LC(1), Op.max)
         ts(A("oh"), S(2), -2816.0, Op.add)
-        pick(1, hop)
-        v, bv, ok, nm, s, al, base = LI(6), S(3), S(4), S(5), S(6), S(7), S(10)
-        u = 2.0 ** -16 if last else 1.0
+        pick(1, hop("KN"), "m16", "bob")
+        v, bv, ok, nm, rp, al, base = LI(6), S(3), S(4), S(5), S(6), S(7), S(10)
+        q2, t16 = A("l1", 15, 256, 16), A("t16", 0, 16)
         ts(v, LI(0), 0xFF0000, Op.bitwise_and)
         ts(nm, LI(3), 1.0, Op.is_equal)
+        sc(A("l1", 0, 128), A("dC", 0, 128), A(HB[1][0], 0, 128), Op.add, Op.max)
         tt(bv, LC(6 + par), v, Op.subtract)
-        ts(S(11), v, 2.0 ** 20, Op.min, -u, Op.mult)
+        sc(A("l1", 128, 256), A("dC", 0, 128), A(HB[1][1], 0, 128), Op.add, Op.max)
+        ts(S(11), v, 2.0 ** 20, Op.min, -2.0 ** -16, Op.mult)
         ts(ok, bv, 0.0, Op.is_le)
-        ts(S(12), bv, 0.0, Op.max, u, Op.mult)
-        tt(s, ok, nm, Op.max)
-        tt(S(11), S(11), ok, Op.mult)
-        tt(S(12), S(12), nm, Op.mult)
-        ts(S(8), s, 2.0 ** 20, Op.mult)
-        tt(A("xd", 16, 32), S(11), S(12), Op.add)
-        tt(A("xd", 0, 16), S(8), v, Op.subtract)
-        for r in range(16):
-            mm(A("ps5", r, 512, 16), A("slt", 128 * r, 128 * r + 128), A("xd"), False, False)
-        to_list(1)
-        tt(S(14), LI(4), S(2), Op.max)
-        ts(A("oh"), S(14), -2816.0, Op.add)
-        pick(2, hop)
+        ts(A("oh"), q2, -32768.0, Op.add)
+        ts(S(12), bv, 0.0, Op.max, 2.0 ** -16, Op.mult)
+        ts(S(15), q2, 32768.0 + 256, Op.is_lt)
+        pick(2, hop("KC"))
         mm(A("ps5", 0, 256), A("bo"), A("mm"), False, True)
-        ts(S(15), S(14), 3072.0, Op.is_lt)
-        tt(S(13), nm, LC(2 + par), Op.mult)
-        ts(S(16), s, -1.0, Op.mult, 1.0, Op.add)
+        tt(S(16), ok, nm, Op.max)
         tt(S(15), S(15), LC(4 + par), Op.mult)
-        ts(S(9), S(14), float(DB - 2560), Op.add)
+        ts(S(9), q2, float(DB - 2560 + 2816 - 32768), Op.add)
+        tt(S(13), nm, LC(2 + par), Op.mult)
+        ts(rp, S(16), -1.0, Op.mult, 1.0, Op.add)
+        tt(S(15), S(15), S(9), Op.add)
         tt(al, ok, nm, Op.is_gt)
         ts(S(13), S(13), -1808.0, Op.add)
-        tt(S(15), S(15), S(9), Op.add)
+        tt(S(15), S(15), rp, Op.mult)
         ts(al, al, 2056.0, Op.mult)
-        tt(S(15), S(15), S(16), Op.mult)
+        tt(S(11), S(11), ok, Op.mult)
         tt(base, S(15), S(13), Op.add)
-        to_list(2)
+        diag(2, "ll")
+        tt(S(12), S(12), nm, Op.mult)
+        cp(LI(2), A("ll", 15, 256, 16))
+        tt(A("t16", 16, 32), S(11), S(12), Op.add)
+        ts(LI(5), LI(2), 4095, Op.bitwise_and)
         tt(S(17), LI(5), al, Op.min)
-        tt(A("t16"), S(17), base, Op.add)
+        tt(S(8), LI(5), rp, Op.mult)
+        tt(t16, S(17), base, Op.add)
+        for r in range(16):
+            mm(A("ps6", r, 512, 16), A("slt", 128 * r, 128 * r + 128), A("t16"), True, True, inc=r == 15)
         for k in range(1, 16):
-            mm(A("ps3", k, 256, 16), A("sh", 128 * k - 128, 128 * k), A("t16"), False, k == 15)
-        ts(A("os"), LI(5), 0.0, Op.add)
-        ts(A("ot"), A("t16"), 1808.0, Op.add)
-        ts(S(18), A("t16"), PF(4), Op.subtract)
+            mm(A("ps3", k, 256, 16), A("sh", 128 * k - 128, 128 * k), t16, False, k == 15)
+        tt(S(14), S(17), base, Op.add)
+        ts(A("os"), S(8), 0.0, Op.add)
+        ts(A("ot"), t16, 1808.0, Op.add)
+        act(A("nw"), X(A("W"), A("ot")))
         ts(A("mk"), A("ps5", 0, 256), M12, Op.add, PF(2), Op.is_equal)
-        tt(A("ps2", 0, 256), A("ps5", 256, 512), A("mp"), Op.mult)
+        tt(S(18), t16, LC(8), Op.subtract)
         tt(A("t2"), X(A("SD"), A("os")), A("mk"), Op.mult)
+        for c in range(16):
+            if c % 4:
+                ts(A("ne", 48 * c, 48 * c + 16 * (c % 4)), A("ps6", 64 * (c // 4), 16 * c), A("sm", 224 + c, 225 + c), Op.not_equal)
+        tt(A("ps2", 0, 256), A("ps6", 256, 512), A("mq"), Op.mult)
+        sc(A("kp"), A("dE"), A("ne"), Op.add, Op.min)
         sc(A("ax"), A("ps3", 0, 256), A("dD"), Op.mult, Op.add)
-        tt(A("t3"), A("ps2", 0, 256), A("t2"), Op.add)
+        tt(S(18), S(18), A("kp", 47, 768, 48), Op.mult)
         ts(S(19), A("ax", 15, 256, 16), 0.0, Op.not_equal)
-        tt(A("nw"), X(A("W"), A("ot")), A("t3"), Op.add)
+        tt(A("t3"), A("ps2", 0, 256), A("t2"), Op.add)
         tt(S(19), S(19), S(18), Op.mult)
-        ts(A("ow", 0, 32, 2), S(19), PF(3), Op.add)
-        for c in range(15, -1, -1):
-            cp(X(A("W"), A("ow", 2 * c, 2 * c + 1)), A("nw", 16 * c, 16 * c + 16), scat=True)
+        for i in range(4):
+            ts((T.ow[:, i:16:4], [("ow", i, i + 1)]), A("sm", 304 + i, 320, 4), PF(3 + i), Op.add)
+        for b in range(3, -1, -1):
+            tt(X(A("W"), (T.ow[:, 4 * b:4 * b + 4], [("ow", 0, 4)])), A("nw", 64 * b, 64 * b + 64), A("t3", 64 * b, 64 * b + 64), Op.add, scat=True)
 
     dma("y", lambda: g.sync.dma_start(T.bds[:], T.bd[:]), [A("bds")], [])
     dma("s", lambda: g.scalar.dma_start(T.avs[:, 0:512], T.av[:, 0:512]), [A("avs", 0, 512)], [])
@@ -350,6 +361,9 @@ def rank_program(g, core, T, topo):
     ms(A("dP"), -8192.0); ms(A("dN"), -4096.0)
     ms(A("dP", 0, 1024, 8), 2.0 ** 25); ms(A("dN", 0, 1024, 16), 2.0 ** 25)
     ms(A("TT", 2272, 2728), 255.0 * 65536 + 28680 + 2720)
+    ms(A("W", 0, A0), 0.0); ms(A("W", A0 + 2048, DB), 0.0)
+    ms(A("dX"), 2048.0); ms(A("dC"), 0.0); ms(A("dD"), 0.0); ms(A("c30"), 30720.0)
+    ms(A("dX", 0, 256, 16), -2.0 ** 25); ms(A("dC", 0, 256, 16), -2.0 ** 26); ms(A("dD", 0, 256, 16), 1.0)
     act(A("ps0"), A("ramp"), 1.0, 3064.0 + 512)
     for a in (512, 1024, 1536):
         act(A("TT", a, a + 512), A("ramp"))
@@ -376,6 +390,7 @@ def rank_program(g, core, T, topo):
     iota(A("colr"), [[0, 16], [1, 16]], 0, 0)
     iota(LC(0), [[16, 16]], 0, 1)
     iota(LC(9), [[1, 16]], 0, 0)
+    iota(LC(8), [[0, 4], [16, 4]], 256, 0)
     sel(A("bo"), A("one"), [[-16, 8], [0, 16]], Op.is_ge, 0.0, 0, 1)
     sel(A("bo"), A("bo"), [[16, 8], [0, 16]], Op.is_ge, 0.0, 15, -1)
     act(A("sh"), A("avs", 0, 1920), 0.0, 1.0 / 64)
@@ -387,6 +402,12 @@ def rank_program(g, core, T, topo):
         act(A("tmp", 1024, 1536), A("avs", 1024, 1536), 65536.0, -2040.0)
         act(AT(3), A("avs", 1536, 2048), 65536.0, -32767.0)
         act(AT(0), A("TT", 0, 512))
+        act(A("KN", 0, 256), A("ramp", 0, 256), 1.0, -28680.0)
+        act(A("pc"), A("ramp"), 1.0, 256 - 28680.0)
+        act(A("KN", 768, 1280), A("ramp"), 1.0, 768 - 28680.0)
+        act(A("ne"), A("avs", 0, 768), 0.0, 1.0)
+        act(A("dE"), A("avs", 0, 768), 0.0, 0.0)
+        act(A("dE", 0, 768, 48), A("avs", 0, 16), 0.0, 2.0)
         iota(A("SD"), [[-1, 2736]], 8, 0, False)
         dma("g", lambda: g.dma_start(T.SD[:, 8:1544], T.sbs[:, 0:1536], accum_op=Op.add), [A("SD", 8, 1544)], [A("sbs"), A("SD", 8, 1544)])
         dma("g", lambda: g.dma_start(T.SD[:, 2056:2728], T.sbs[:, 1536:2208], accum_op=Op.add), [A("SD", 2056, 2728)], [A("sbs"), A("SD", 2056, 2728)])
@@ -397,24 +418,23 @@ def rank_program(g, core, T, topo):
         ts(A("pi", 1, 2), A("pi", 0, 1), 15, Op.bitwise_and)
         ts(PF(1), A("gi", 0, 1), 16.0, Op.mult)
         cp(PF(0), A("pi", 1, 2))
-        ms(A("W", 0, A0), 0.0); ms(A("W", A0 + 2048, DB), 0.0)
-        ms(A("dX"), 2048.0); ms(A("dC"), 0.0); ms(A("dD"), 0.0); ms(A("c30", 0, 256), 30720.0); ms(A("c30", 256, 512), 0.0)
+        ts(LC(0), LC(0), PF(1), Op.subtract)
+        ts(PF(2), PF(0), 4096.0, Op.mult, M12, Op.add)
+        ts(LC(8), LC(8), PF(0), Op.add)
+        for i in range(4):
+            ts(PF(3 + i), PF(0), 2064.0 + 16 * i, Op.add)
+        ts(A("dg"), A("colr"), PF(0), Op.is_equal)
+        ts(A("tri"), A("colr"), PF(0), Op.is_gt)
 
     def setup2():
         sel(A("sh"), A("sh"), [[-1, 15], [0, 8], [1, 16]], Op.is_ge, 0.0, -1, 0)
-        ts(LC(0), LC(0), PF(1), Op.subtract)
-        ts(PF(2), PF(0), 4096.0, Op.mult, M12, Op.add)
-        ts(PF(3), PF(0), 2064.0, Op.add)
-        ts(PF(4), PF(0), 256.0, Op.add)
-        ts(A("dg"), A("colr"), PF(0), Op.is_equal)
-        ts(A("tri"), A("colr"), PF(0), Op.is_gt)
         act(A("ng"), A("dg"), 2.0 ** 25 + 32768, -2.0 ** 25)
-        act(A("cp"), A("colr"), -2048.0, 30720.0)
         act(A("bob"), A("bo"))
+        act(A("nbo"), A("bo"), -1.0)
         for r in range(16):
             do("s", lambda: g.scalar.activation(T.slt[:, 128 * r:128 * r + 128], T.bob[:], Fn.Copy, scale=T.dg[:, r:r + 1]), A("slt", 128 * r, 128 * r + 128), [A("bob"), A("dg")])
-        cp(A("oc"), LC(9))
-        ms(A("dX", 0, 256, 16), -2.0 ** 25); ms(A("dC", 0, 256, 16), -2.0 ** 26); ms(A("dD", 0, 256, 16), 1.0)
+        ts(A("oc"), LC(9), 16.0, Op.mult, 15.0, Op.add)
+        ms(A("SD", 0, 4), 0)
         ts(LC(1), LC(0), 2816.0, Op.add)
         for par in (0, 1):
             ts(LC(2 + par), LC(0), 2.0, Op.mult, 1536.0 + A0 + par, Op.add)
@@ -457,11 +477,16 @@ def rank_program(g, core, T, topo):
         ghosts_v(3 * t + 1)
         level(2, 3 * t + 2)
         act(A("ps6", 0, 256), A("W", A0 + 1536 + par, A0 + 2048, 2))
+        act(A("ps6", 256, 512), A("colr"), -2048.0, 30720.0)
+        ts(A("ki"), A("KC", 256, 768), 32768.0, Op.add)
+        ts(A("ki"), A("ki"), 4095, Op.bitwise_and)
+        ts(A("ps2"), A("ki"), -2816.0, Op.add)
+        tt(A("KN", 256, 768), A("ps2"), A("pc"), Op.max)
         if t == 0:
             pairs_v(3); plain_v(3, par)
             setup2(); thresholds(0)
         if t == 2:
-            plain_a(A0, A0 + 1536)
+            plain_a(A0, A0 + 1024)
         ghosts_pe(3 * t + 2)
         ghosts_v(3 * t + 2)
         level(3, None)
@@ -470,7 +495,7 @@ def rank_program(g, core, T, topo):
     dma("g", lambda: g.dma_start(T.ya[:], T.W[:, A0:A0 + 2048]), [], [A("W")])
     for l, e in ((1, "y"), (2, "s"), (3, "y")):
         dma(e, lambda: Q[e].dma_start(T.yd[:, 512 * l - 512:512 * l], T.W[:, DCOL[l]:DCOL[l] + 512]), [], [A("W")])
-    odd_scan(1); odd_scan(2); odd_scan(3)
+    odd_scan(0); odd_scan(1); odd_scan(2); odd_scan(3)
     ts(A("mm"), A("so", 15, 4096, 16), M0, Op.add, M0, Op.subtract)
     tt(A("yro", 1, 512, 2), A("mm"), A("W", A0 + 1537, A0 + 2048, 2), Op.min)
     dma("s", lambda: g.scalar.dma_start(T.yr[:], T.yro[:]), [], [A("yro")])

@@ -2,33 +2,33 @@ from concourse.bass import DstId, RemoteDMATransfer, IndirectOffsetOnAxis
 from concourse.mybir import AluOpType as Op, ActivationFunctionType as Fn
 
 F32, BF, I32, U16, F16 = "float32", "bfloat16", "int32", "uint16", "float16"
-NP = 304
-NPT = 144
-PC = {NP: (16, 8, 24, 32, 36, 36), NPT: (16, 8, 24, 24)}
-NC = {512 - NP: (64, 64, 48, 16, 16), 256 - NPT: (48, 32, 16, 16)}
-A0, DB, WN = 8, 2128, 3664
-DCOL = {1: DB + 1024, 2: DB + 512, 3: DB}
-KCOL = {1: 768, 2: 256}
-M16, M12, M0 = 1.5 * 2 ** 39, 1.5 * 2 ** 35, 1.5 * 2 ** 23
+NP = 352
+NPT = 176
+PC = {NP: (16, 8, 24, 32, 48, 48), NPT: (16, 8, 24, 40)}
+NC = {512 - NP: (64, 48, 24, 16, 8), 256 - NPT: (40, 24, 8, 8)}
+A0, SP, DE, WN = 2048, 4104, 4224, 5760
+STOP = 127 + 63 / 64
+RND = 1536 + 63 / 128
 SB = {
     "avs": (2048, BF), "dps": (1536, I32), "bds": (42, I32), "bdo": (42, U16), "sbs": (2208, I32), "ths": (512, I32),
-    "W": (WN, F32), "TT": (2728, F32), "KC": (1280, F32), "KN": (1280, F32), "SD": (2736, I32), "ki": (512, I32), "pc": (512, F32),
-    "gs": (8 * NP, F32), "gp": (8 * NP, F32), "sp": (8 * NP, F32), "gn": (16 * (512 - NP), F32), "sn": (16 * (512 - NP), F32),
-    "go": (4096, BF), "so": (4096, BF), "hi": (512, F32), "hb": (512, BF), "abd": (448, BF), "tmp": (1536, F32),
+    "W": (WN, F32), "TT": (2728, BF), "KC": (2728, F32), "SD": (2736, I32), "d16": (NP, F16), "rh": (512, F16),
+    "gs": (8 * NP, F32), "gp": (8 * NP, F16), "sp": (8 * NP, F16), "gn": (16 * (512 - NP), BF), "sn": (16 * (512 - NP), F16),
+    "go": (4096, BF), "so": (4096, BF),
     "on1": (512 - NP, U16), "on2": (512 - NP, U16), "on3": (256 - NPT, U16), "ono": (256, U16),
     "op1": (NP, U16), "op2": (NP, U16), "op3": (NPT, U16),
-    "dN": (1024, BF), "dP": (1024, BF), "dO": (1024, BF), "dX": (256, BF), "dC": (256, BF), "dD": (256, BF), "dE": (768, BF), "c30": (256, BF),
-    "ramp": (512, F32), "gc0": (672, F32), "one": (128, F32), "oneb": (128, BF), "ident": (128, BF), "pm1": (128, BF), "pm2": (128, BF),
-    "bo": (128, F32), "bob": (128, BF), "nbo": (128, BF), "pp": (512, F32), "sh": (1920, BF), "slt": (2048, BF), "colr": (256, F32),
-    "dg": (256, F32), "ng": (256, BF), "tri": (256, BF), "pi": (4, I32), "gi": (4, I32), "pf": (8, F32), "lc": (160, F32), "oc": (16, U16),
-    "rt": (256, BF), "rtt": (256, BF), "ax": (256, F32), "mt": (256, BF), "mp": (256, BF), "mm": (256, F32), "ll": (256, F32), "l1": (256, F32),
-    "li": (128, I32), "sm": (512, F32), "oh": (16, U16), "os": (16, U16), "ot": (16, U16), "ow": (16, U16), "t16": (32, F16), "m16": (256, F16),
-    "rm": (256, BF), "mq": (256, BF), "ne": (768, BF), "kp": (768, BF), "mk": (256, BF), "t2": (256, F32), "t3": (256, F32), "nw": (256, F32),
+    "dN": (1024, BF), "dP": (1024, BF), "dO": (1024, BF), "dX": (256, BF), "dC": (256, BF), "dD": (256, BF), "dE": (784, BF),
+    "one": (128, F32), "oneb": (128, BF), "ident": (128, BF), "pm1": (128, BF), "pm2": (128, BF),
+    "bo": (128, F32), "bob": (128, BF), "nbo": (128, BF), "nb2": (128, BF), "lm": (384, BF), "pp": (512, F32), "ppb": (512, BF),
+    "sh": (1920, BF), "slt": (2048, BF), "colr": (256, F32),
+    "dg": (256, F32), "ng": (256, BF), "ng2": (256, BF), "tri": (256, BF), "pi": (4, I32), "gi": (4, I32), "pf": (8, F32), "lc": (160, F32), "oc": (16, U16),
+    "rt": (256, F16), "rtt": (256, F16), "ax": (256, F32), "mt": (256, BF), "mp": (256, BF), "mm": (256, F32), "ll": (1024, F32),
+    "sm": (640, F32), "oh": (32, U16), "os": (16, U16), "ot": (16, U16), "ow": (16, U16), "t16": (32, F16), "m16": (256, F16), "z16": (256, F16),
+    "rm": (256, F16), "eq": (768, BF), "ne": (784, BF), "kp": (784, BF), "sg": (256, BF), "mk": (256, BF), "t2": (256, F32), "t3": (256, F32), "nw": (256, F32),
     "yro": (512, BF),
 }
 for _i in range(9):
-    SB["snd%d" % _i] = (224, BF)
-    SB["lnd%d" % _i] = (224, BF)
+    SB["snd%d" % _i] = (224, F16)
+    SB["lnd%d" % _i] = (224, F16)
 SCRATCH = {k: ("sbuf", [128, v[0]], v[1]) for k, v in SB.items()}
 for _i in range(8):
     SCRATCH["ps%d" % _i] = ("psum", [128, 512], F32)
@@ -121,8 +121,15 @@ def rank_program(g, core, T, topo):
         else:
             do("v", lambda: g.vector.tensor_scalar(o[0], a[0], v1, v2, o0, o1), o, r)
 
-    def act(o, i, scale=1.0, bias=0.0):
-        do("s", lambda: g.scalar.activation(o[0], i[0], Fn.Copy, bias=bias, scale=scale), o, [i])
+    def act(o, i, scale=1.0, bias=0.0, fn=Fn.Copy):
+        r = [i] + [s for s in (scale, bias) if isinstance(s, tuple)]
+        sv = scale[0] if isinstance(scale, tuple) else float(scale)
+        bv = bias[0] if isinstance(bias, tuple) else float(bias)
+        do("s", lambda: g.scalar.activation(o[0], i[0], fn, bias=bv, scale=sv), o, r)
+
+    def fill(o, c):
+        n = o[1][0][2] - o[1][0][1]
+        act(o, A("avs", 0, n), 0.0, c)
 
     def mm(o, l, r, st, sp, inc=None):
         do("t", lambda: g.tensor.matmul(o[0], l[0], r[0], st, sp), o, [l, r], inc=sp if inc is None else inc)
@@ -133,17 +140,19 @@ def rank_program(g, core, T, topo):
         else:
             do("g", lambda: g.iota(o[0], pat, base, cm), o, [])
 
-    def sel(o, i, pat, op, fill, base, cm):
-        do("g", lambda: g.affine_select(o[0], i[0], pat, op, fill, base, cm), o, [i])
+    def sel(o, i, pat, op, fill_, base, cm):
+        do("g", lambda: g.affine_select(o[0], i[0], pat, op, fill_, base, cm), o, [i])
 
-    def strip(o, i): ts(o, i, M16, Op.add, M16, Op.subtract)
     def S(j): return A("sm", 16 * j, 16 * j + 16)
-    def LI(j): return A("li", 16 * j, 16 * j + 16)
     def LC(j): return A("lc", 16 * j, 16 * j + 16)
     def PF(j): return A("pf", j, j + 1)
     def BD(l): return A("bdo", 14 * l, 14 * l + 14)
-    def AT(l): return A("W", A0 + 512 * l, A0 + 512 * l + 512)
+    def LL(j): return A("ll", 256 * j + 15, 256 * j + 256, 16)
+    def H(name, h, base=0): return A(name, base + h, base + h + 128)
     TW = A("TT")
+
+    def will(t, lo, hi, st=1):
+        return A("avs", lo, hi, st) if t == 0 else A("W", A0 + lo, A0 + hi, st)
 
     def send(x):
         order("g", [], A("snd%d" % x)[1])
@@ -163,189 +172,197 @@ def rank_program(g, core, T, topo):
         ends["loc"] = ends.get("loc", 0) + 7 * k
         note(A("lnd%d" % x)[1], [], "arr%d" % x, 7 * k, "arr")
 
-    def ghosts_pe(x):
+    def ghosts(x):
         for d in range(1, 8):
             mm(A("ps3", 32 * d - 32, 32 * d), A(("ident", "pm1", "pm2")[d % 3]), A("lnd%d" % x, 32 * d - 32, 32 * d), True, True, inc=d == 7)
-
-    def ghosts_v(x):
         l = x % 3
-        tt(A("TT", 2048 + 224 * l, 2272 + 224 * l), A("ps3", 0, 224), A("gc0", 224 * l, 224 * l + 224), Op.add)
-
-    def pair_ps(l):
-        return ("ps4", 0) if l == 1 else (("ps5", 0) if l == 2 else ("ps7", 0))
+        act(A("TT", 2048 + 224 * l, 2272 + 224 * l), A("ps3", 0, 224), 1.0, -1536.0)
 
     def pairs_pe(l, par):
         n = NP if l < 3 else NPT
-        b, c0 = pair_ps(l)
+        b = "ps2" if l == 2 else "ps1"
         for h in (0, 1):
             for a in (0, 1):
-                r = A("W", DCOL[l] + a, DCOL[l] + n, 2) if l < 3 else A("W", DB + par + 2 * a, DB + 2 * n, 4)
-                mm(A(b, c0 + h * n // 2, c0 + (h + 1) * n // 2), A("pp", 256 * h + 128 * a, 256 * h + 128 * a + 128), r, a == 0, a == 1, inc=h + a == 2)
+                r = A("d16", a, n, 2) if l == 1 else (A("W", 1024 + a, 1024 + n, 2) if l == 2 else A("W", 1536 + par + 2 * a, 1536 + 2 * n, 4))
+                mm(A(b, h * n // 2, (h + 1) * n // 2), A("ppb" if l == 1 else "pp", 256 * h + 128 * a, 256 * h + 128 * a + 128), r, a == 0, a == 1, inc=h + a == 2)
 
     def pairs_v(l):
         n = NP if l < 3 else NPT
-        b, c0 = pair_ps(l)
-        cp(A("op%d" % l), A(b, c0, c0 + n))
+        ts(A("op%d" % l), A("ps2" if l == 2 else "ps1", 0, n), 1536.0, Op.add)
 
     def plain_v(l, par):
         if l < 3:
-            cp(A("on%d" % l), A("W", DCOL[l] + NP, DCOL[l] + 512))
+            ts(A("on%d" % l), A("W", 512 * l + NP, 512 * l + 512), 1536.0, Op.add)
         else:
-            cp(A("on3"), A("W", DB + 2 * NPT + par, DB + 512, 2))
-
-    def released(l): strip(A("abd", 224 * l - 224, 224 * l), X(AT(l), BD(l)))
+            ts(A("on3"), A("W", 1536 + 2 * NPT + par, 2048, 2), 1536.0, Op.add)
 
     def level(l, x):
         n, m = (NP, 512 - NP) if l < 3 else (NPT, 256 - NPT)
         o, on = "op%d" % l, "on%d" % l
         pc, nc = chunks(PC[n]), chunks(NC[m])
+        def key(src, lo, hi): tt(A("KC", 512 * l + lo, 512 * l + hi) if l < 3 else A("ps0", lo, hi), src, A("ps0", lo, hi), Op.min)
         for j, (a, b) in enumerate(pc):
             if j == 0:
-                ts(A("gs", 16 * a, 16 * b), X(TW, A(o, n // 2 + a, n // 2 + b)), -4096.0, Op.add)
+                ts(A("gs", 16 * a, 16 * b), X(TW, A(o, n // 2 + a, n // 2 + b)), -1 / 16, Op.add)
             else:
-                act(A("gs", 16 * a, 16 * b), X(TW, A(o, n // 2 + a, n // 2 + b)), bias=-4096.0)
-        for a, b in nc[:2]:
+                act(A("gs", 16 * a, 16 * b), X(TW, A(o, n // 2 + a, n // 2 + b)), bias=-1 / 16)
+        for a, b in nc:
             act(A("gn", 16 * a, 16 * b), X(TW, A(on, a, b)))
         for a, b in [pc[1], pc[0]] + pc[2:]:
             tt(A("gp", 16 * a, 16 * b), X(TW, A(o, a, b)), A("gs", 16 * a, 16 * b), Op.min)
         for a in range(0, 8 * n, 1024):
             b = min(a + 1024, 8 * n)
             sc(A("sp", a, b), A("dP", 0, b - a), A("gp", a, b), Op.add, Op.min)
-        for a, b in nc[2:]:
-            act(A("gn", 16 * a, 16 * b), X(TW, A(on, a, b)))
+        def scan(a, b): sc(A("sn", 16 * a, 16 * b), A("dN", 0, 16 * (b - a)), A("gn", 16 * a, 16 * b), Op.add, Op.min)
+        scan(*nc[0])
+        key(A("sp", 7, 8 * n, 8), 0, n)
+        for a, b in nc[1:-1]:
+            scan(a, b)
+        a = nc[-2][0]
+        key(A("sn", 15, 16 * a, 16), n, n + a)
+        scan(*nc[-1])
+        key(A("sn", 16 * a + 15, 16 * m, 16), n + a, n + m)
         if l < 3:
-            act(A("hi", 0, n), A("sp", 7, 8 * n, 8), 1.0, M16)
-            act(A("hb", 0, n), A("hi", 0, n), 1.0, -M16)
-        for a, b in nc:
-            sc(A("sn", 16 * a, 16 * b), A("dN", 0, 16 * (b - a)), A("gn", 16 * a, 16 * b), Op.add, Op.min)
-        if l < 3:
-            a = nc[-1][0]
-            strip(A("hb", n, n + a), A("sn", 15, 16 * a, 16))
-            strip(A("hb", n + a, 512), A("sn", 16 * a + 15, 16 * m, 16))
-            tt(A("snd%d" % x), X(A("hb"), BD(l)), A("abd", 224 * l - 224, 224 * l), Op.min)
+            K = A("KC", 512 * l, 512 * l + 512)
+            ts(A("snd%d" % x), X(K, BD(l)), RND, Op.add)
             send(x)
-            tt(A("ps2"), A("ps%d" % (l - 1)), A("hb"), Op.add)
-            tt(A("TT", 512 * l, 512 * l + 512), A("ps2"), AT(l), Op.min)
-            act(A("KC", KCOL[l], KCOL[l] + n), A("sp", 7, 8 * n, 8))
-            act(A("KC", KCOL[l] + n, KCOL[l] + 512), A("sn", 15, 16 * m, 16))
-
-    HB = (("ps4", "ps7"), ("ps6", "ps2"), ("ps4", "ps7"))
-
-    def diag(j, out):
-        for h, b in zip((0, 128), HB[j]):
-            sc(A(out, h, h + 128), A("dC", 0, 128), A(b, 0, 128), Op.add, Op.max)
-
-    def pre(j):
-        for b in HB[j]:
-            mm(A(b, 0, 128), A("ident"), A("ng", 0, 128), True, False)
-
-    def pick(j, src, buf="mm", ones="bo"):
-        for h, b in zip((0, 128), HB[j]):
-            tt(A(buf, h, h + 128), src(h), A("mp", h, h + 128), Op.mult)
-            mm(A(b, 0, 128), A(ones), A(buf, h, h + 128), False, True)
-
-    def hop(tab): return lambda h: X(A(tab), A("oh", h // 16, h // 16 + 8))
-
-    def plain_a(lo, hi):
-        act(A("W", lo, hi), A("W", lo, hi), 2.0 ** -16, M0)
-        act(A("W", lo, hi), A("W", lo, hi), 1.0, -M0)
+            ts(A("rh"), K, RND, Op.add)
+            ts(A("TT", 512 * l, 512 * l + 512), A("rh"), -1536.0, Op.add)
 
     def odd_scan(j): sc(A("so", 1024 * j, 1024 * j + 1024), A("dO"), A("go", 1024 * j, 1024 * j + 1024), Op.add, Op.min)
-    def odd_get(j): act(A("go", 1024 * j, 1024 * j + 1024), X(TW, A("ono", 64 * j, 64 * j + 64)), 2.0 ** -16, -0.4375)
+    def odd_get(j): act(A("go", 512 * j, 512 * j + 512), X(TW, A("ono", 32 * j, 32 * j + 32)), 1.0, 127.0)
 
     def walk(t):
         par, last = t & 1, t == 2
-        K0 = A("ps2", 0, 256)
-        pre(0)
-        mm(A("ps5", 0, 256), A("ident"), A("c30"), True, False)
-        mm(A("ps3", 0, 256), A("ident"), A("tri"), True, False)
-        if last:
-            odd_get(0)
-        tt(A("ps2", 0, NPT), A("sp", 7, 8 * NPT, 8), A("ps6", 0, NPT), Op.min)
-        tt(A("ps2", NPT, 256), A("sn", 15, 16 * (256 - NPT), 16), A("ps6", NPT, 256), Op.min)
-        strip(A("rt"), K0)
-        act(A("KC", 0, 256), K0)
-        if last:
-            odd_get(1)
-            plain_a(A0 + 1024, A0 + 2048)
-            act(A("yro", 0, 512, 2), A("rt"), 2.0 ** -16)
-            odd_get(2); odd_get(3)
+        sh, w0, cd = (-256.0, A0, DE - 1024.0) if last else (1280.0, 512, -512.0)
+        WW = A("W", w0, WN if last else SP + 64)
+        EB, ZB = {0: "ps1", 128: "ps2"}, {0: "ps3", 128: "ps4"}
+        def odd(*js):
+            for j in js:
+                if last:
+                    odd_get(j)
+        def OH(j, h): return A("oh", 16 * j - 16 + h // 16, 16 * j - 8 + h // 16)
+        def preE(h): mm(A(EB[h], 0, 128), A("nbo"), H("rm", h), True, False)
+        def preZ(j, h): mm(A(ZB[h], 0, 128), A("ident"), A("ng2" if j == 2 else "ng", 0, 128), True, False)
+        def a_(j, h):
+            tt(H("m16", h), X(A("KC"), OH(j, h)), H("mp", h), Op.mult)
+            mm(A(EB[h], 0, 128), A("bob"), H("m16", h), False, True)
+        def c_(j, h): ts(H("eq", h, 256 * j), A(EB[h], 0, 128), PF(2), Op.is_equal)
+        def d_(j, h):
+            src = X(A("W", 0, 2728), OH(j, h)) if j else A("W", 1536 + par + 2 * h, 1536 + 2 * h + 256, 2)
+            tt(H("z16", h), src, H("eq", h, 256 * j), Op.mult)
+            mm(A(ZB[h], 0, 128), A("bob"), H("z16", h), False, True)
+        def f_(j, h): sc(H("ll", h, 256 * j), A("dC", 0, 128), A(ZB[h], 0, 128), Op.add, Op.max)
+        def g_(j, h): ts(OH(j + 1, h), A("ll", 256 * j + h + 15, 256 * j + h + 128, 16), 1536.0, Op.add)
+        def mark(j): mm(A("ps5", 0, 256), A("lm", 128 * j, 128 * j + 128), A("eq", 256 * j, 256 * j + 256), j == 0, j == 2)
+
+        K0 = A("ps0", 0, 256)
+        preZ(0, 0); preZ(0, 128)
+        mm(A("ps7", 0, 256), A("ident"), A("ng"), True, False)
+        odd(0, 1)
+        ts(A("rt"), K0, RND, Op.add)
         tr(A("rtt"), A("rt"))
         sc(A("ax"), A("dX"), A("rtt"), Op.add, Op.max)
-        tt(A("t2"), A("ps6", 256, 512), A("rtt"), Op.add)
+        tt(A("t2"), A("ps0", 256, 512), A("rtt"), Op.add)
         tt(A("mt"), X(A("ax"), A("oc")), A("t2"), Op.is_equal)
+        if last:
+            ts(A("yro", 0, 512, 2), A("rt"), -1409.0, Op.add)
         tr(A("mp"), A("mt"))
-        pick(0, lambda h: A("ps2", h, h + 128))
-        pre(1)
-        tt(A("rm"), A("rt"), A("mp"), Op.mult)
-        mm(A("ps5", 0, 256), A("nbo"), A("rm"), False, False)
-        act(A("mq"), A("mp"), 1.0 if last else 65536.0)
-        diag(0, "ll")
-        cp(LI(0), A("ll", 15, 256, 16))
-        ts(LI(3), LI(0), 4095, Op.bitwise_and)
-        pre(2)
-        tt(S(2), LI(3), LC(1), Op.max)
-        ts(A("oh"), S(2), -2816.0, Op.add)
-        pick(1, hop("KN"), "m16", "bob")
-        v, bv, ok, nm, rp, al, base = LI(6), S(3), S(4), S(5), S(6), S(7), S(10)
-        q2, t16 = A("l1", 15, 256, 16), A("t16", 0, 16)
-        ts(v, LI(0), 0xFF0000, Op.bitwise_and)
-        ts(nm, LI(3), 1.0, Op.is_equal)
-        sc(A("l1", 0, 128), A("dC", 0, 128), A(HB[1][0], 0, 128), Op.add, Op.max)
-        tt(bv, LC(6 + par), v, Op.subtract)
-        sc(A("l1", 128, 256), A("dC", 0, 128), A(HB[1][1], 0, 128), Op.add, Op.max)
-        ts(S(11), v, 2.0 ** 20, Op.min, -2.0 ** -16, Op.mult)
-        ts(ok, bv, 0.0, Op.is_le)
-        ts(A("oh"), q2, -32768.0, Op.add)
-        ts(S(12), bv, 0.0, Op.max, 2.0 ** -16, Op.mult)
-        ts(S(15), q2, 32768.0 + 256, Op.is_lt)
-        pick(2, hop("KC"))
-        mm(A("ps5", 0, 256), A("bo"), A("mm"), False, True)
-        tt(S(16), ok, nm, Op.max)
-        tt(S(15), S(15), LC(4 + par), Op.mult)
-        ts(S(9), q2, float(DB - 2560 + 2816 - 32768), Op.add)
-        tt(S(13), nm, LC(2 + par), Op.mult)
-        ts(rp, S(16), -1.0, Op.mult, 1.0, Op.add)
-        tt(S(15), S(15), S(9), Op.add)
-        tt(al, ok, nm, Op.is_gt)
-        ts(S(13), S(13), -1808.0, Op.add)
-        tt(S(15), S(15), rp, Op.mult)
-        ts(al, al, 2056.0, Op.mult)
-        tt(S(11), S(11), ok, Op.mult)
-        tt(base, S(15), S(13), Op.add)
-        diag(2, "ll")
-        tt(S(12), S(12), nm, Op.mult)
-        cp(LI(2), A("ll", 15, 256, 16))
-        tt(A("t16", 16, 32), S(11), S(12), Op.add)
-        ts(LI(5), LI(2), 4095, Op.bitwise_and)
-        tt(S(17), LI(5), al, Op.min)
-        tt(S(8), LI(5), rp, Op.mult)
-        tt(t16, S(17), base, Op.add)
+        for h in (0, 128):
+            tt(H("m16", h), H("ps0", h), H("mp", h), Op.mult)
+            mm(A(EB[h], 0, 128), A("bob"), H("m16", h), True, False)
+            tt(H("rm", h), H("rt", h), H("mp", h), Op.mult)
+            mm(A(EB[h], 0, 128), A("nbo"), H("rm", h), False, True)
+        mm(A("ps7", 0, 256), A("bob"), A("rm"), False, True)
+        odd(2, 3)
+        z1, z2, z3, v = LL(0), LL(1), LL(2), LL(3)
+        nbv, mv, okb, s1, x1, rp, al, als, nb, p1, s2, sb2, p2, q2, b3, dl = [S(j) for j in range(16)]
+        u = [S(16 + j) for j in range(12)]
+        t16, tf = A("t16", 0, 16), S(28)
+        c_(0, 0); c_(0, 128)
+        d_(0, 0); preE(0); d_(0, 128); preE(128); mark(0)
+        sc(A("ll", 768, 1024), A("dC"), A("ps7", 0, 256), Op.add, Op.max)
+        mm(A("ps7", 0, 256), A("ident"), A("tri"), True, False)
+        f_(0, 0); preZ(1, 0); f_(0, 128); preZ(1, 128)
+        g_(0, 0); tt(nbv, v, LC(6 + par), Op.subtract); g_(0, 128)
+        a_(1, 0); a_(1, 128)
+        ts(s1, z1, 0.0, Op.is_equal)
+        ts(mv, v, 1425.0, Op.min, 1409.0, Op.subtract)
+        c_(1, 0)
+        ts(okb, nbv, 0.0, Op.is_ge, 4096.0, Op.mult)
+        tt(x1, nbv, s1, Op.mult)
+        c_(1, 128)
+        d_(1, 0); preE(0); d_(1, 128); preE(128); mark(1)
+        odd(4, 5)
+        tt(u[0], s1, LC(2 + par), Op.mult)
+        tt(rp, nbv, x1, Op.is_lt)
+        tt(u[1], x1, okb, Op.add)
+        f_(1, 0); preZ(2, 0)
+        tt(p1, z1, u[0], Op.add)
+        f_(1, 128); preZ(2, 128)
+        g_(1, 0)
+        tt(A("t16", 16, 32), u[1], mv, Op.min)
+        g_(1, 128)
+        a_(2, 0); a_(2, 128)
+        ts(s2, z2, 0.0, Op.is_equal)
+        ts(sb2, z2, 0.0, Op.is_equal, 4096.0, Op.mult)
+        c_(2, 0)
+        tt(u[2], s2, p1, Op.mult)
+        tt(u[3], z1, sb2, Op.add)
+        c_(2, 128)
+        mark(2)
+        d_(2, 0); d_(2, 128)
         for r in range(16):
-            mm(A("ps6", r, 512, 16), A("slt", 128 * r, 128 * r + 128), A("t16"), True, True, inc=r == 15)
+            mm(A("ps0", r, 256, 16), A("slt", 128 * r, 128 * r + 128), A("t16", 16, 32), True, True, inc=r == 15)
+        act(A("sg"), A("ps5", 0, 256), 1.0, PF(7), Fn.Sign)
+        act(A("mk"), A("sg"), fn=Fn.Relu)
+        tt(p2, z2, u[2], Op.add)
+        tt(q2, u[3], LC(2 + par), Op.min)
+        ts(al, rp, -2048.0, Op.mult, 512.0, Op.add)
+        ts(u[4], p2, cd, Op.add)
+        tt(u[5], q2, p2, Op.subtract)
+        f_(2, 0)
+        tt(u[6], p2, al, Op.min)
+        ts(u[5], u[5], 1536.0, Op.add)
+        tt(b3, u[4], rp, Op.mult)
+        ts(als, rp, -2048.0, Op.mult, 512.0 + sh, Op.add)
+        tt(u[5], u[5], rp, Op.mult)
+        f_(2, 128)
+        ts(nb, rp, 4096.0, Op.mult, 1544.0 - 4096.0 - sh, Op.add)
+        tt(dl, u[5], u[6], Op.add)
+        ts(u[7], z3, sh, Op.is_equal)
+        tt(u[8], z3, als, Op.min)
+        tt(u[9], z3, nb, Op.add)
+        tt(u[10], u[7], dl, Op.mult)
+        tt(u[8], u[8], b3, Op.add)
+        tt(u[11], u[7], p2, Op.mult)
+        tt(t16, u[10], u[8], Op.add)
+        for r in range(16):
+            mm(A("ps6", r, 256, 16), A("slt", 128 * r, 128 * r + 128), t16, True, True, inc=r == 15)
         for k in range(1, 16):
-            mm(A("ps3", k, 256, 16), A("sh", 128 * k - 128, 128 * k), t16, False, k == 15)
-        tt(S(14), S(17), base, Op.add)
-        ts(A("os"), S(8), 0.0, Op.add)
-        ts(A("ot"), t16, 1808.0, Op.add)
-        act(A("nw"), X(A("W"), A("ot")))
-        ts(A("mk"), A("ps5", 0, 256), M12, Op.add, PF(2), Op.is_equal)
-        tt(S(18), t16, LC(8), Op.subtract)
+            mm(A("ps7", k, 256, 16), A("sh", 128 * k - 128, 128 * k), t16, False, k == 15)
+        tt(tf, u[10], u[8], Op.add)
+        tt(u[9], u[9], u[11], Op.add)
+        ts(A("ot"), t16, 1792.0, Op.add)
+        act(A("nw"), X(WW, A("ot")))
+        cp(A("os"), u[9])
+        tt(S(29), tf, LC(8), Op.subtract)
+        tt(K0, K0, A("mp"), Op.mult)
         tt(A("t2"), X(A("SD"), A("os")), A("mk"), Op.mult)
         for c in range(16):
             if c % 4:
-                ts(A("ne", 48 * c, 48 * c + 16 * (c % 4)), A("ps6", 64 * (c // 4), 16 * c), A("sm", 224 + c, 225 + c), Op.not_equal)
-        tt(A("ps2", 0, 256), A("ps6", 256, 512), A("mq"), Op.mult)
+                act(A("ne", 49 * c, 49 * c + 16 * (c % 4)), A("ps6", 64 * (c // 4), 16 * c), -1.0, A("sm", 448 + c, 449 + c), Fn.Abs)
+        odd(6, 7)
+        tt(A("t3"), A("t2"), K0, Op.subtract)
+        sc(A("ax"), A("ps7", 0, 256), A("dD"), Op.mult, Op.add)
+        ts(S(30), A("ax", 15, 256, 16), 0.0, Op.not_equal)
+        tt(S(29), S(29), S(30), Op.mult)
         sc(A("kp"), A("dE"), A("ne"), Op.add, Op.min)
-        sc(A("ax"), A("ps3", 0, 256), A("dD"), Op.mult, Op.add)
-        tt(S(18), S(18), A("kp", 47, 768, 48), Op.mult)
-        ts(S(19), A("ax", 15, 256, 16), 0.0, Op.not_equal)
-        tt(A("t3"), A("ps2", 0, 256), A("t2"), Op.add)
-        tt(S(19), S(19), S(18), Op.mult)
+        tt(S(30), S(29), A("kp", 48, 784, 49), Op.mult)
         for i in range(4):
-            ts((T.ow[:, i:16:4], [("ow", i, i + 1)]), A("sm", 304 + i, 320, 4), PF(3 + i), Op.add)
+            ts((T.ow[:, i:16:4], [("ow", i, i + 1)]), A("sm", 480 + i, 496, 4), PF(3 + i), Op.add, float(SP - w0), Op.add)
         for b in range(3, -1, -1):
-            tt(X(A("W"), (T.ow[:, 4 * b:4 * b + 4], [("ow", 0, 4)])), A("nw", 64 * b, 64 * b + 64), A("t3", 64 * b, 64 * b + 64), Op.add, scat=True)
+            tt(X(WW, (T.ow[:, 4 * b:4 * b + 4], [("ow", 0, 4)])), A("nw", 64 * b, 64 * b + 64), A("t3", 64 * b, 64 * b + 64), Op.add, scat=True)
 
     dma("y", lambda: g.sync.dma_start(T.bds[:], T.bd[:]), [A("bds")], [])
     dma("s", lambda: g.scalar.dma_start(T.avs[:, 0:512], T.av[:, 0:512]), [A("avs", 0, 512)], [])
@@ -353,151 +370,131 @@ def rank_program(g, core, T, topo):
     dma("s", lambda: g.scalar.dma_start(T.avs[:, 512:2048], T.av[:, 512:2048]), [A("avs", 512, 2048)], [])
     dma("y", lambda: g.sync.dma_start(T.dps[:, 512:1536], T.dp[:, 512:1536]), [A("dps", 512, 1536)], [])
     ms(A("one"), 1.0); ms(A("oneb"), 1.0)
-    iota(A("ramp"), [[1, 512]], 28680, 0)
     for h in (0, 1):
         for a in (0, 1):
-            sel(A("pp", 256 * h + 128 * a, 256 * h + 128 * a + 128), A("one"), [[-16, 8], [200, 2], [-2, 8]], Op.is_equal, 0.0, -200 * a - (1 - h), 1)
+            sel(A("ppb", 256 * h + 128 * a, 256 * h + 128 * a + 128), A("oneb"), [[-16, 8], [200, 2], [-2, 8]], Op.is_equal, 0.0, -200 * a - (1 - h), 1)
     iota(A("pi", 0, 1), [[0, 1]], 0, 1, False)
-    ms(A("dP"), -8192.0); ms(A("dN"), -4096.0)
-    ms(A("dP", 0, 1024, 8), 2.0 ** 25); ms(A("dN", 0, 1024, 16), 2.0 ** 25)
-    ms(A("TT", 2272, 2728), 255.0 * 65536 + 28680 + 2720)
-    ms(A("W", 0, A0), 0.0); ms(A("W", A0 + 2048, DB), 0.0)
-    ms(A("dX"), 2048.0); ms(A("dC"), 0.0); ms(A("dD"), 0.0); ms(A("c30"), 30720.0)
-    ms(A("dX", 0, 256, 16), -2.0 ** 25); ms(A("dC", 0, 256, 16), -2.0 ** 26); ms(A("dD", 0, 256, 16), 1.0)
-    act(A("ps0"), A("ramp"), 1.0, 3064.0 + 512)
-    for a in (512, 1024, 1536):
-        act(A("TT", a, a + 512), A("ramp"))
+    ms(A("TT", 512, 2728), 128.0)
+    ms(A("dP"), -1 / 8); ms(A("dN"), -1 / 16)
+    ms(A("dP", 0, 1024, 8), 1024.0); ms(A("dN", 0, 1024, 16), 1024.0)
     cp(A("bdo"), A("bds"))
-    ts(A("snd0"), X(A("avs", 0, 512), BD(0)), 65536.0, Op.mult)
+    ts(A("snd0"), X(A("avs", 0, 512), BD(0)), 1409.0, Op.add)
     send(0)
     sel(A("pm1"), A("oneb"), [[16, 8], [-1, 16]], Op.is_equal, 0.0, -112, 1)
     sel(A("pm2", 16, 128), A("oneb", 16, 128), [[16, 7], [-1, 16]], Op.is_equal, 0.0, -112, 1)
     sel(A("pm2", 0, 16), A("oneb", 0, 16), [[-1, 16]], Op.is_equal, 0.0, 0, 1)
     sel(A("ident"), A("oneb"), [[-1, 128]], Op.is_equal, 0.0, 0, 1)
-    iota(A("gc0"), [[1, 672]], 28680 + 2048, 0)
-    act(A("tmp", 0, 512), A("avs", 0, 512), 65536.0, -3576.0)
-    cp(A("W", DCOL[1], DCOL[1] + 512), A("dps", 0, 512))
+    act(A("TT", 0, 512), A("avs", 0, 512), 1.0, -127.0)
+    ts(A("d16"), A("dps", 0, NP), -1536.0, Op.add)
     pairs_pe(1, 0)
-    tt(A("TT", 0, 512), A("ps0"), A("tmp", 0, 512), Op.add)
-    plain_v(1, 0)
-    act(A("tmp", 512, 1024), A("avs", 512, 1024), 65536.0, -3064.0)
-    act(A("ps1"), A("ramp"), 1.0, 2040.0 + 1024)
-    tt(AT(1), A("ps0"), A("tmp", 512, 1024), Op.add)
-    released(1)
+    cp(A("on1"), A("dps", NP, 512))
     ts(A("gi", 0, 1), A("pi", 0, 1), 4, Op.arith_shift_right)
-    cp(A("W", DCOL[2], DCOL[2] + 512), A("dps", 512, 1024))
+    ms(A("dX"), 1 / 16); ms(A("dC"), 0.0); ms(A("dD"), 0.0)
+    ms(A("W", A0 + 2048, DE), 0.0)
     pairs_v(1)
+    ms(A("dX", 0, 256, 16), -2.0 ** 25); ms(A("dC", 0, 256, 16), -2.0 ** 26); ms(A("dD", 0, 256, 16), 1.0)
+    act(A("pp"), A("ppb"))
+    act(A("ps0"), A("avs", 512, 1024), 1.0, -STOP)
+    ts(A("W", 1024, 1536), A("dps", 512, 1024), -1536.0, Op.add)
+    ts(A("W", 1536, 2048), A("dps", 1024, 1536), -1536.0, Op.add)
+    ts(A("W", 512, 1024), A("dps", 0, 512), -1536.0, Op.add)
+    plain_v(2, 0); plain_v(3, 0)
     iota(A("colr"), [[0, 16], [1, 16]], 0, 0)
     iota(LC(0), [[16, 16]], 0, 1)
     iota(LC(9), [[1, 16]], 0, 0)
-    iota(LC(8), [[0, 4], [16, 4]], 256, 0)
+    iota(LC(1), [[0, 4], [16, 4]], 0, 0)
     sel(A("bo"), A("one"), [[-16, 8], [0, 16]], Op.is_ge, 0.0, 0, 1)
     sel(A("bo"), A("bo"), [[16, 8], [0, 16]], Op.is_ge, 0.0, 15, -1)
-    act(A("sh"), A("avs", 0, 1920), 0.0, 1.0 / 64)
+    fill(A("sh"), 1.0 / 64)
     dma("g", lambda: g.indirect_dma_start(T.sbs[:], None, T.sb[:], IndirectOffsetOnAxis(ap=T.gi[:, 0:1], axis=0), bounds_check=7), [A("sbs")], [A("gi")])
     dma("g", lambda: g.indirect_dma_start(T.ths[:], None, T.th[:], IndirectOffsetOnAxis(ap=T.gi[:, 0:1], axis=0), bounds_check=7), [A("ths")], [A("gi")])
     sel(A("sh"), A("sh"), [[-1, 15], [1, 128]], Op.is_equal, 0.0, -1, -1)
 
     def setup1():
-        act(A("tmp", 1024, 1536), A("avs", 1024, 1536), 65536.0, -2040.0)
-        act(AT(3), A("avs", 1536, 2048), 65536.0, -32767.0)
-        act(AT(0), A("TT", 0, 512))
-        act(A("KN", 0, 256), A("ramp", 0, 256), 1.0, -28680.0)
-        act(A("pc"), A("ramp"), 1.0, 256 - 28680.0)
-        act(A("KN", 768, 1280), A("ramp"), 1.0, 768 - 28680.0)
-        act(A("ne"), A("avs", 0, 768), 0.0, 1.0)
-        act(A("dE"), A("avs", 0, 768), 0.0, 0.0)
-        act(A("dE", 0, 768, 48), A("avs", 0, 16), 0.0, 2.0)
+        act(A("W", A0, A0 + 2048), A("avs"))
+        act(A("bob"), A("bo"))
+        act(A("nbo"), A("bo"), -1.0)
+        act(A("nb2"), A("bo"), -2.0)
         iota(A("SD"), [[-1, 2736]], 8, 0, False)
         dma("g", lambda: g.dma_start(T.SD[:, 8:1544], T.sbs[:, 0:1536], accum_op=Op.add), [A("SD", 8, 1544)], [A("sbs"), A("SD", 8, 1544)])
         dma("g", lambda: g.dma_start(T.SD[:, 2056:2728], T.sbs[:, 1536:2208], accum_op=Op.add), [A("SD", 2056, 2728)], [A("sbs"), A("SD", 2056, 2728)])
         sel(A("sh"), A("sh"), [[0, 15], [1, 128]], Op.not_equal, -1.0 / 64, 0, -1)
-        tt(AT(2), A("ps1"), A("tmp", 1024, 1536), Op.add)
-        cp(A("W", DB, DB + 512), A("dps", 1024, 1536))
-        released(2)
         ts(A("pi", 1, 2), A("pi", 0, 1), 15, Op.bitwise_and)
         ts(PF(1), A("gi", 0, 1), 16.0, Op.mult)
+        ms(PF(7), 0.5)
         cp(PF(0), A("pi", 1, 2))
         ts(LC(0), LC(0), PF(1), Op.subtract)
-        ts(PF(2), PF(0), 4096.0, Op.mult, M12, Op.add)
-        ts(LC(8), LC(8), PF(0), Op.add)
+        ts(PF(2), PF(0), 1 / 16, Op.mult, -1536 - 15 / 16, Op.add)
+        ts(LC(8), LC(1), PF(0), Op.add, SP - 3584 + 1280.0, Op.add)
         for i in range(4):
-            ts(PF(3 + i), PF(0), 2064.0 + 16 * i, Op.add)
+            ts(PF(3 + i), PF(0), 16.0 * i, Op.add)
         ts(A("dg"), A("colr"), PF(0), Op.is_equal)
         ts(A("tri"), A("colr"), PF(0), Op.is_gt)
+        ts(A("oc"), LC(9), 16.0, Op.mult, 15.0, Op.add)
+        for par in (0, 1):
+            ts(LC(2 + par), LC(0), 2.0, Op.mult, float(par), Op.add)
 
     def setup2():
+        for j, (src, d) in enumerate((("nbo", 0.0), ("nbo", 1.0), ("nb2", 2.0))):
+            sel(A("lm", 128 * j, 128 * j + 128), A(src), [[-1, 128]], Op.not_equal, d, 0, 1)
         sel(A("sh"), A("sh"), [[-1, 15], [0, 8], [1, 16]], Op.is_ge, 0.0, -1, 0)
-        act(A("ng"), A("dg"), 2.0 ** 25 + 32768, -2.0 ** 25)
-        act(A("bob"), A("bo"))
-        act(A("nbo"), A("bo"), -1.0)
-        for r in range(16):
-            do("s", lambda: g.scalar.activation(T.slt[:, 128 * r:128 * r + 128], T.bob[:], Fn.Copy, scale=T.dg[:, r:r + 1]), A("slt", 128 * r, 128 * r + 128), [A("bob"), A("dg")])
-        ts(A("oc"), LC(9), 16.0, Op.mult, 15.0, Op.add)
+        act(A("ng"), A("dg"), 2.0 ** 25, -2.0 ** 25)
+        act(A("ng2"), A("dg"), 2.0 ** 25 + 1280, -2.0 ** 25)
+        fill(A("KC", 0, 512), 1000.0); fill(A("KC", 1536, 2728), 1000.0); fill(A("W", 0, 512), 0.0)
+        ms(A("ne"), 1.0); ms(A("dE"), 0.0); ms(A("dE", 0, 784, 49), 2.0)
         ms(A("SD", 0, 4), 0)
-        ts(LC(1), LC(0), 2816.0, Op.add)
-        for par in (0, 1):
-            ts(LC(2 + par), LC(0), 2.0, Op.mult, 1536.0 + A0 + par, Op.add)
-            ts(LC(4 + par), LC(0), par - 256.0, Op.add)
+        for r in range(16):
+            ts(A("slt", 128 * r, 128 * r + 128), A("bob"), A("dg", r, r + 1), Op.mult)
 
     def thresholds(par):
         tt(A("mm"), A("ths", par, 512, 2), A("ng"), Op.add)
-        sc(A("ll"), A("dC"), A("mm"), Op.add, Op.max)
-        ts(LC(6 + par), A("ll", 15, 256, 16), -32768.0, Op.add, 65536.0, Op.mult)
+        sc(A("ax"), A("dC"), A("mm"), Op.add, Op.max)
+        ts(LC(6 + par), A("ax", 15, 256, 16), 1409.0, Op.add)
 
     for t in range(3):
         par = t & 1
         if t > 0:
-            strip(A("snd%d" % (3 * t)), X(AT(0), BD(0)))
+            ts(A("snd%d" % (3 * t)), X(A("W", A0, A0 + 512), BD(0)), 1409.0, Op.add)
             send(3 * t)
-            act(A("TT", 0, 512), AT(0))
+            act(A("TT", 0, 512), A("W", A0, A0 + 512), 1.0, -127.0)
+            act(A("ps0"), will(t, 512, 1024), 1.0, -STOP)
+            cp(A("d16"), A("W", 512, 512 + NP))
             pairs_pe(1, par)
-            plain_v(1, par); released(1); plain_v(2, par); released(2); plain_v(3, par)
+            plain_v(1, par); plain_v(2, par); plain_v(3, par)
+            pairs_v(1)
             if t == 2:
-                cp(A("ono"), A("W", DB + 1, DB + 512, 2))
+                ts(A("ono"), A("W", 1537, 2048, 2), 1536.0, Op.add)
                 ms(A("dO"), 0.0); ms(A("dO", 0, 1024, 16), 1024.0)
+                ts(LC(8), LC(8), -1536.0, Op.add)
+                act(A("W", DE, DE + 768), A("W", 512, 1280), 1.0, 1536.0)
             else:
                 thresholds(1)
-            pairs_v(1)
-        ghosts_pe(3 * t)
+        ghosts(3 * t)
         pairs_pe(2, par)
-        ghosts_v(3 * t)
-        if t > 0:
-            pairs_pe(3, par)
+        pairs_pe(3, par)
         level(1, 3 * t + 1)
-        pairs_v(2)
+        act(A("ps0"), will(t, 1024, 1536), 1.0, -STOP)
+        pairs_v(2); pairs_v(3)
         if t == 0:
-            plain_v(2, par)
             setup1()
-        else:
-            pairs_v(3)
-        ghosts_pe(3 * t + 1)
-        if t == 0:
-            pairs_pe(3, par)
-        ghosts_v(3 * t + 1)
-        level(2, 3 * t + 2)
-        act(A("ps6", 0, 256), A("W", A0 + 1536 + par, A0 + 2048, 2))
-        act(A("ps6", 256, 512), A("colr"), -2048.0, 30720.0)
-        ts(A("ki"), A("KC", 256, 768), 32768.0, Op.add)
-        ts(A("ki"), A("ki"), 4095, Op.bitwise_and)
-        ts(A("ps2"), A("ki"), -2816.0, Op.add)
-        tt(A("KN", 256, 768), A("ps2"), A("pc"), Op.max)
-        if t == 0:
-            pairs_v(3); plain_v(3, par)
-            setup2(); thresholds(0)
         if t == 2:
-            plain_a(A0, A0 + 1024)
-        ghosts_pe(3 * t + 2)
-        ghosts_v(3 * t + 2)
+            act(A("W", DE + 768, WN), A("W", 1280, 2048), 1.0, 1536.0)
+            act(A("ng2"), A("dg"), 2.0 ** 25 - 256, -2.0 ** 25)
+        ghosts(3 * t + 1)
+        level(2, 3 * t + 2)
+        act(A("ps0", 0, 256), will(t, 1536 + par, 2048, 2), 1.0, -STOP)
+        act(A("ps0", 256, 512), A("colr"), -1 / 16, 15 / 16)
+        if t == 0:
+            setup2(); thresholds(0)
+        ghosts(3 * t + 2)
         level(3, None)
         walk(t)
 
-    dma("g", lambda: g.dma_start(T.ya[:], T.W[:, A0:A0 + 2048]), [], [A("W")])
-    for l, e in ((1, "y"), (2, "s"), (3, "y")):
-        dma(e, lambda: Q[e].dma_start(T.yd[:, 512 * l - 512:512 * l], T.W[:, DCOL[l]:DCOL[l] + 512]), [], [A("W")])
+    dma("g", lambda: g.dma_start(T.ya[:], T.W[:, A0:A0 + 2048]), [], [A("W", A0, WN)])
+    for j, e in enumerate(("y", "s", "y")):
+        dma(e, lambda: Q[e].dma_start(T.yd[:, 512 * j:512 * j + 512], T.W[:, DE + 512 * j:DE + 512 * j + 512]), [], [A("W", A0, WN)])
     odd_scan(0); odd_scan(1); odd_scan(2); odd_scan(3)
-    ts(A("mm"), A("so", 15, 4096, 16), M0, Op.add, M0, Op.subtract)
-    tt(A("yro", 1, 512, 2), A("mm"), A("W", A0 + 1537, A0 + 2048, 2), Op.min)
+    tt(A("yro", 1, 512, 2), A("so", 15, 4096, 16), A("W", A0 + 1537, A0 + 2048, 2), Op.min)
     dma("s", lambda: g.scalar.dma_start(T.yr[:], T.yro[:]), [], [A("yro")])
     for sem, n in ends.items():
         g.sync.wait_ge(T.sem[sem], n)

@@ -2,11 +2,11 @@ from concourse.bass import DstId, RemoteDMATransfer, IndirectOffsetOnAxis
 from concourse.mybir import AluOpType as Op, ActivationFunctionType as Fn
 
 F32, BF, I32, U16, F16 = "float32", "bfloat16", "int32", "uint16", "float16"
-NP = 352
-NPT = 176
-PC = {NP: (16, 8, 24, 32, 48, 48), NPT: (16, 8, 24, 40)}
-NC = {512 - NP: (64, 48, 24, 16, 8), 256 - NPT: (40, 24, 8, 8)}
+PC = ((16, 8, 16, 24, 32, 44, 48), (16, 8, 16, 24, 28))
+NC = ((56, 40, 24, 8, 8), (40, 16, 8, 8))
+NP, NPT = 2 * sum(PC[0]), 2 * sum(PC[1])
 A0, SP, DE, WN = 2048, 4104, 4224, 5760
+NE = (0, 72, 208, 408, 672)
 STOP = 127 + 63 / 64
 RND = 1536 + 63 / 128
 SB = {
@@ -16,14 +16,14 @@ SB = {
     "go": (4096, BF), "so": (4096, BF),
     "on1": (512 - NP, U16), "on2": (512 - NP, U16), "on3": (256 - NPT, U16), "ono": (256, U16),
     "op1": (NP, U16), "op2": (NP, U16), "op3": (NPT, U16),
-    "dN": (1024, BF), "dP": (1024, BF), "dO": (1024, BF), "dX": (256, BF), "dC": (256, BF), "dD": (256, BF), "dE": (784, BF),
-    "one": (128, F32), "oneb": (128, BF), "ident": (128, BF), "pm1": (128, BF), "pm2": (128, BF),
-    "bo": (128, F32), "bob": (128, BF), "nbo": (128, BF), "nb2": (128, BF), "lm": (384, BF), "pp": (512, F32), "ppb": (512, BF),
-    "sh": (1920, BF), "slt": (2048, BF), "colr": (256, F32),
-    "dg": (256, F32), "ng": (256, BF), "ng2": (256, BF), "tri": (256, BF), "pi": (4, I32), "gi": (4, I32), "pf": (8, F32), "lc": (160, F32), "oc": (16, U16),
+    "dN": (1024, BF), "dP": (1024, BF), "dO": (1024, BF), "dX": (256, BF), "dC": (256, BF), "dE": (672, BF),
+    "one": (128, F32), "oneb": (144, BF), "ident": (128, BF), "pm1": (128, BF), "pm2": (128, BF),
+    "bo": (128, F32), "bob": (128, BF), "nbo": (128, BF), "nb2": (128, BF), "lm": (384, BF), "pp": (288, F32), "ppb": (288, BF),
+    "slt": (2048, BF), "colr": (256, F32), "yy": (16, F32),
+    "dg": (256, F32), "ng": (256, BF), "ng2": (256, BF), "pi": (4, I32), "gi": (4, I32), "pf": (12, F32), "lc": (160, F32), "oc": (16, U16),
     "rt": (256, F16), "rtt": (256, F16), "ax": (256, F32), "mt": (256, BF), "mp": (256, BF), "mm": (256, F32), "ll": (1024, F32),
     "sm": (640, F32), "oh": (32, U16), "os": (16, U16), "ot": (16, U16), "ow": (16, U16), "t16": (32, F16), "m16": (256, F16), "z16": (256, F16),
-    "rm": (256, F16), "eq": (768, BF), "ne": (784, BF), "kp": (784, BF), "sg": (256, BF), "mk": (256, BF), "t2": (256, F32), "t3": (256, F32), "nw": (256, F32),
+    "rm": (256, F16), "eq": (768, BF), "ne": (672, BF), "kp": (672, BF), "sg": (256, BF), "mk": (256, BF), "t2": (256, F32), "t3": (256, F32), "nw": (256, F32),
     "yro": (512, BF),
 }
 for _i in range(9):
@@ -127,10 +127,6 @@ def rank_program(g, core, T, topo):
         bv = bias[0] if isinstance(bias, tuple) else float(bias)
         do("s", lambda: g.scalar.activation(o[0], i[0], fn, bias=bv, scale=sv), o, r)
 
-    def fill(o, c):
-        n = o[1][0][2] - o[1][0][1]
-        act(o, A("avs", 0, n), 0.0, c)
-
     def mm(o, l, r, st, sp, inc=None):
         do("t", lambda: g.tensor.matmul(o[0], l[0], r[0], st, sp), o, [l, r], inc=sp if inc is None else inc)
 
@@ -140,8 +136,8 @@ def rank_program(g, core, T, topo):
         else:
             do("g", lambda: g.iota(o[0], pat, base, cm), o, [])
 
-    def sel(o, i, pat, op, fill_, base, cm):
-        do("g", lambda: g.affine_select(o[0], i[0], pat, op, fill_, base, cm), o, [i])
+    def sel(o, i, pat, op, fill, base, cm):
+        do("g", lambda: g.affine_select(o[0], i[0], pat, op, fill, base, cm), o, [i])
 
     def S(j): return A("sm", 16 * j, 16 * j + 16)
     def LC(j): return A("lc", 16 * j, 16 * j + 16)
@@ -149,7 +145,7 @@ def rank_program(g, core, T, topo):
     def BD(l): return A("bdo", 14 * l, 14 * l + 14)
     def LL(j): return A("ll", 256 * j + 15, 256 * j + 256, 16)
     def H(name, h, base=0): return A(name, base + h, base + h + 128)
-    TW = A("TT")
+    TW, ONE = A("TT"), A("oneb", 0, 128)
 
     def will(t, lo, hi, st=1):
         return A("avs", lo, hi, st) if t == 0 else A("W", A0 + lo, A0 + hi, st)
@@ -184,7 +180,7 @@ def rank_program(g, core, T, topo):
         for h in (0, 1):
             for a in (0, 1):
                 r = A("d16", a, n, 2) if l == 1 else (A("W", 1024 + a, 1024 + n, 2) if l == 2 else A("W", 1536 + par + 2 * a, 1536 + 2 * n, 4))
-                mm(A(b, h * n // 2, (h + 1) * n // 2), A("ppb" if l == 1 else "pp", 256 * h + 128 * a, 256 * h + 128 * a + 128), r, a == 0, a == 1, inc=h + a == 2)
+                mm(A(b, h * n // 2, (h + 1) * n // 2), A("ppb" if l == 1 else "pp", 160 - 152 * h - 8 * a, 288 - 152 * h - 8 * a), r, a == 0, a == 1, inc=h + a == 2)
 
     def pairs_v(l):
         n = NP if l < 3 else NPT
@@ -199,24 +195,26 @@ def rank_program(g, core, T, topo):
     def level(l, x):
         n, m = (NP, 512 - NP) if l < 3 else (NPT, 256 - NPT)
         o, on = "op%d" % l, "on%d" % l
-        pc, nc = chunks(PC[n]), chunks(NC[m])
+        pc, nc = chunks(PC[l // 3]), chunks(NC[l // 3])
         def key(src, lo, hi): tt(A("KC", 512 * l + lo, 512 * l + hi) if l < 3 else A("ps0", lo, hi), src, A("ps0", lo, hi), Op.min)
+        def pair(a, b): tt(A("gp", 16 * a, 16 * b), X(TW, A(o, a, b)), A("gs", 16 * a, 16 * b), Op.min)
+        def scan2(a, b): sc(A("sp", 16 * a, 16 * b), A("dP", 0, 16 * (b - a)), A("gp", 16 * a, 16 * b), Op.add, Op.min)
+        def scan(a, b): sc(A("sn", 16 * a, 16 * b), A("dN", 0, 16 * (b - a)), A("gn", 16 * a, 16 * b), Op.add, Op.min)
         for j, (a, b) in enumerate(pc):
             if j == 0:
-                ts(A("gs", 16 * a, 16 * b), X(TW, A(o, n // 2 + a, n // 2 + b)), -1 / 16, Op.add)
+                ts(A("gs", 16 * a, 16 * b), X(TW, A(o, n // 2 + a, n // 2 + b)), -0.5, Op.add)
             else:
-                act(A("gs", 16 * a, 16 * b), X(TW, A(o, n // 2 + a, n // 2 + b)), bias=-1 / 16)
+                act(A("gs", 16 * a, 16 * b), X(TW, A(o, n // 2 + a, n // 2 + b)), bias=-0.5)
         for a, b in nc:
             act(A("gn", 16 * a, 16 * b), X(TW, A(on, a, b)))
-        for a, b in [pc[1], pc[0]] + pc[2:]:
-            tt(A("gp", 16 * a, 16 * b), X(TW, A(o, a, b)), A("gs", 16 * a, 16 * b), Op.min)
-        for a in range(0, 8 * n, 1024):
-            b = min(a + 1024, 8 * n)
-            sc(A("sp", a, b), A("dP", 0, b - a), A("gp", a, b), Op.add, Op.min)
-        def scan(a, b): sc(A("sn", 16 * a, 16 * b), A("dN", 0, 16 * (b - a)), A("gn", 16 * a, 16 * b), Op.add, Op.min)
-        scan(*nc[0])
+        pair(*pc[1]); pair(*pc[0]); pair(*pc[2]); pair(*pc[3])
+        a = 0
+        for j in range(4, len(pc)):
+            scan2(a, pc[j - 1][0]); a = pc[j - 1][0]
+            pair(*pc[j])
+        scan2(a, pc[-1][0]); scan(*nc[0]); scan2(*pc[-1]); scan(*nc[1])
         key(A("sp", 7, 8 * n, 8), 0, n)
-        for a, b in nc[1:-1]:
+        for a, b in nc[2:-1]:
             scan(a, b)
         a = nc[-2][0]
         key(A("sn", 15, 16 * a, 16), n, n + a)
@@ -230,7 +228,7 @@ def rank_program(g, core, T, topo):
             ts(A("TT", 512 * l, 512 * l + 512), A("rh"), -1536.0, Op.add)
 
     def odd_scan(j): sc(A("so", 1024 * j, 1024 * j + 1024), A("dO"), A("go", 1024 * j, 1024 * j + 1024), Op.add, Op.min)
-    def odd_get(j): act(A("go", 512 * j, 512 * j + 512), X(TW, A("ono", 32 * j, 32 * j + 32)), 1.0, 127.0)
+    def odd_get(j): act(A("go", 256 * j, 256 * j + 256), X(TW, A("ono", 16 * j, 16 * j + 16)), 1.0, 127.0)
 
     def walk(t):
         par, last = t & 1, t == 2
@@ -249,18 +247,24 @@ def rank_program(g, core, T, topo):
             mm(A(EB[h], 0, 128), A("bob"), H("m16", h), False, True)
         def c_(j, h): ts(H("eq", h, 256 * j), A(EB[h], 0, 128), PF(2), Op.is_equal)
         def d_(j, h):
-            src = X(A("W", 0, 2728), OH(j, h)) if j else A("W", 1536 + par + 2 * h, 1536 + 2 * h + 256, 2)
+            src = X(A("W", 0, 2728), OH(j, h)) if j else H("ps6", h, 256)
             tt(H("z16", h), src, H("eq", h, 256 * j), Op.mult)
             mm(A(ZB[h], 0, 128), A("bob"), H("z16", h), False, True)
         def f_(j, h): sc(H("ll", h, 256 * j), A("dC", 0, 128), A(ZB[h], 0, 128), Op.add, Op.max)
         def g_(j, h): ts(OH(j + 1, h), A("ll", 256 * j + h + 15, 256 * j + h + 128, 16), 1536.0, Op.add)
         def mark(j): mm(A("ps5", 0, 256), A("lm", 128 * j, 128 * j + 128), A("eq", 256 * j, 256 * j + 256), j == 0, j == 2)
+        def spread(b, src, rs):
+            for r in rs:
+                mm(A(b, r, 256, 16), A("slt", 128 * r, 128 * r + 128), src, True, True, inc=r == 15)
 
         K0 = A("ps0", 0, 256)
         preZ(0, 0); preZ(0, 128)
         mm(A("ps7", 0, 256), A("ident"), A("ng"), True, False)
-        odd(0, 1)
+        odd(0, 1, 2, 3, 4)
+        if t == 0:
+            setup3()
         ts(A("rt"), K0, RND, Op.add)
+        mm(A("ps6", 0, 256), A("ident"), A("rt"), True, True)
         tr(A("rtt"), A("rt"))
         sc(A("ax"), A("dX"), A("rtt"), Op.add, Op.max)
         tt(A("t2"), A("ps0", 256, 512), A("rtt"), Op.add)
@@ -271,65 +275,62 @@ def rank_program(g, core, T, topo):
         for h in (0, 128):
             tt(H("m16", h), H("ps0", h), H("mp", h), Op.mult)
             mm(A(EB[h], 0, 128), A("bob"), H("m16", h), True, False)
-            tt(H("rm", h), H("rt", h), H("mp", h), Op.mult)
+            tt(H("rm", h), H("ps6", h), H("mp", h), Op.mult)
             mm(A(EB[h], 0, 128), A("nbo"), H("rm", h), False, True)
         mm(A("ps7", 0, 256), A("bob"), A("rm"), False, True)
-        odd(2, 3)
         z1, z2, z3, v = LL(0), LL(1), LL(2), LL(3)
         nbv, mv, okb, s1, x1, rp, al, als, nb, p1, s2, sb2, p2, q2, b3, dl = [S(j) for j in range(16)]
         u = [S(16 + j) for j in range(12)]
-        t16, tf = A("t16", 0, 16), S(28)
+        t16, val, tf = A("t16", 0, 16), A("t16", 16, 32), S(28)
+        odd(5, 6)
         c_(0, 0); c_(0, 128)
         d_(0, 0); preE(0); d_(0, 128); preE(128); mark(0)
         sc(A("ll", 768, 1024), A("dC"), A("ps7", 0, 256), Op.add, Op.max)
-        mm(A("ps7", 0, 256), A("ident"), A("tri"), True, False)
         f_(0, 0); preZ(1, 0); f_(0, 128); preZ(1, 128)
+        act(S(32), v, -1.0, PF(9), Fn.Relu); act(S(31), z1, fn=Fn.Abs)
+        act(mv, S(32), -1.0, 16.0); act(s1, S(31), -1.0, PF(8), Fn.Relu)
         g_(0, 0); tt(nbv, v, LC(6 + par), Op.subtract); g_(0, 128)
+        act(S(33), nbv, 1.0, PF(7), Fn.Sign); act(okb, S(33), 2048.0, 2048.0)
         a_(1, 0); a_(1, 128)
-        ts(s1, z1, 0.0, Op.is_equal)
-        ts(mv, v, 1425.0, Op.min, 1409.0, Op.subtract)
-        c_(1, 0)
-        ts(okb, nbv, 0.0, Op.is_ge, 4096.0, Op.mult)
+        odd(7)
         tt(x1, nbv, s1, Op.mult)
-        c_(1, 128)
-        d_(1, 0); preE(0); d_(1, 128); preE(128); mark(1)
-        odd(4, 5)
         tt(u[0], s1, LC(2 + par), Op.mult)
+        c_(1, 0)
         tt(rp, nbv, x1, Op.is_lt)
         tt(u[1], x1, okb, Op.add)
-        f_(1, 0); preZ(2, 0)
         tt(p1, z1, u[0], Op.add)
+        c_(1, 128)
+        d_(1, 0); preE(0); d_(1, 128); preE(128); mark(1)
+        act(al, rp, -2048.0, 512.0); act(als, rp, -2048.0, 512.0 + sh); act(nb, rp, 4096.0, 1544.0 - 4096.0 - sh)
+        tt(val, u[1], mv, Op.min)
+        f_(1, 0); preZ(2, 0)
         f_(1, 128); preZ(2, 128)
-        g_(1, 0)
-        tt(A("t16", 16, 32), u[1], mv, Op.min)
-        g_(1, 128)
+        spread("ps0", val, range(4))
+        act(S(31), z2, fn=Fn.Abs); act(s2, S(31), -1.0, PF(8), Fn.Relu); act(sb2, s2, 4096.0)
+        g_(1, 0); g_(1, 128)
         a_(2, 0); a_(2, 128)
-        ts(s2, z2, 0.0, Op.is_equal)
-        ts(sb2, z2, 0.0, Op.is_equal, 4096.0, Op.mult)
-        c_(2, 0)
+        spread("ps0", val, range(4, 12))
         tt(u[2], s2, p1, Op.mult)
+        c_(2, 0)
         tt(u[3], z1, sb2, Op.add)
+        tt(p2, z2, u[2], Op.add)
         c_(2, 128)
-        mark(2)
-        d_(2, 0); d_(2, 128)
-        for r in range(16):
-            mm(A("ps0", r, 256, 16), A("slt", 128 * r, 128 * r + 128), A("t16", 16, 32), True, True, inc=r == 15)
+        tt(q2, u[3], LC(2 + par), Op.min)
+        act(u[4], p2, 1.0, cd)
+        d_(2, 0); mark(2)
+        tt(u[5], q2, p2, Op.subtract)
+        act(u[5], u[5], 1.0, 1536.0)
+        d_(2, 128)
+        spread("ps0", val, range(12, 16))
         act(A("sg"), A("ps5", 0, 256), 1.0, PF(7), Fn.Sign)
         act(A("mk"), A("sg"), fn=Fn.Relu)
-        tt(p2, z2, u[2], Op.add)
-        tt(q2, u[3], LC(2 + par), Op.min)
-        ts(al, rp, -2048.0, Op.mult, 512.0, Op.add)
-        ts(u[4], p2, cd, Op.add)
-        tt(u[5], q2, p2, Op.subtract)
-        f_(2, 0)
+        odd(8)
         tt(u[6], p2, al, Op.min)
-        ts(u[5], u[5], 1536.0, Op.add)
         tt(b3, u[4], rp, Op.mult)
-        ts(als, rp, -2048.0, Op.mult, 512.0 + sh, Op.add)
         tt(u[5], u[5], rp, Op.mult)
-        f_(2, 128)
-        ts(nb, rp, 4096.0, Op.mult, 1544.0 - 4096.0 - sh, Op.add)
+        f_(2, 0)
         tt(dl, u[5], u[6], Op.add)
+        f_(2, 128)
         ts(u[7], z3, sh, Op.is_equal)
         tt(u[8], z3, als, Op.min)
         tt(u[9], z3, nb, Op.add)
@@ -337,10 +338,7 @@ def rank_program(g, core, T, topo):
         tt(u[8], u[8], b3, Op.add)
         tt(u[11], u[7], p2, Op.mult)
         tt(t16, u[10], u[8], Op.add)
-        for r in range(16):
-            mm(A("ps6", r, 256, 16), A("slt", 128 * r, 128 * r + 128), t16, True, True, inc=r == 15)
-        for k in range(1, 16):
-            mm(A("ps7", k, 256, 16), A("sh", 128 * k - 128, 128 * k), t16, False, k == 15)
+        spread("ps7", t16, range(16))
         tt(tf, u[10], u[8], Op.add)
         tt(u[9], u[9], u[11], Op.add)
         ts(A("ot"), t16, 1792.0, Op.add)
@@ -349,18 +347,17 @@ def rank_program(g, core, T, topo):
         tt(S(29), tf, LC(8), Op.subtract)
         tt(K0, K0, A("mp"), Op.mult)
         tt(A("t2"), X(A("SD"), A("os")), A("mk"), Op.mult)
-        for c in range(16):
-            if c % 4:
-                act(A("ne", 49 * c, 49 * c + 16 * (c % 4)), A("ps6", 64 * (c // 4), 16 * c), -1.0, A("sm", 448 + c, 449 + c), Fn.Abs)
-        odd(6, 7)
+        for i in range(3, -1, -1):
+            for b in range(4):
+                a, c = NE[i] + (18 + 16 * i) * b + 2, 4 * b + i
+                act(A("ne", a, a + 16 * i + 16), A("ps7", 64 * b, 16 * c + 16), -1.0, A("sm", 448 + c, 449 + c), Fn.Abs)
+        odd(*range(9, 16))
         tt(A("t3"), A("t2"), K0, Op.subtract)
-        sc(A("ax"), A("ps7", 0, 256), A("dD"), Op.mult, Op.add)
-        ts(S(30), A("ax", 15, 256, 16), 0.0, Op.not_equal)
-        tt(S(29), S(29), S(30), Op.mult)
-        sc(A("kp"), A("dE"), A("ne"), Op.add, Op.min)
-        tt(S(30), S(29), A("kp", 48, 784, 49), Op.mult)
-        for i in range(4):
-            ts((T.ow[:, i:16:4], [("ow", i, i + 1)]), A("sm", 480 + i, 496, 4), PF(3 + i), Op.add, float(SP - w0), Op.add)
+        def keep(i): sc(A("kp", NE[i], NE[i + 1]), A("ne", NE[i], NE[i + 1]), A("dE", NE[i], NE[i + 1]), Op.min, Op.add)
+        def kept(i): tt(A("yy", 4 * i, 4 * i + 4), A("sm", 464 + i, 480, 4), A("kp", NE[i] + 17 + 16 * i, NE[i + 1], 18 + 16 * i), Op.mult)
+        def place(i):
+            ts((T.ow[:, i:16:4], [("ow", i, i + 1)]), A("yy", 4 * i, 4 * i + 4), PF(3 + i), Op.add, float(SP - w0), Op.add)
+        keep(3); keep(2); kept(3); keep(1); kept(2); place(3); kept(1); place(2); keep(0); place(1); kept(0); place(0)
         for b in range(3, -1, -1):
             tt(X(WW, (T.ow[:, 4 * b:4 * b + 4], [("ow", 0, 4)])), A("nw", 64 * b, 64 * b + 64), A("t3", 64 * b, 64 * b + 64), Op.add, scat=True)
 
@@ -369,82 +366,82 @@ def rank_program(g, core, T, topo):
     dma("y", lambda: g.sync.dma_start(T.dps[:, 0:512], T.dp[:, 0:512]), [A("dps", 0, 512)], [])
     dma("s", lambda: g.scalar.dma_start(T.avs[:, 512:2048], T.av[:, 512:2048]), [A("avs", 512, 2048)], [])
     dma("y", lambda: g.sync.dma_start(T.dps[:, 512:1536], T.dp[:, 512:1536]), [A("dps", 512, 1536)], [])
-    ms(A("one"), 1.0); ms(A("oneb"), 1.0)
-    for h in (0, 1):
-        for a in (0, 1):
-            sel(A("ppb", 256 * h + 128 * a, 256 * h + 128 * a + 128), A("oneb"), [[-16, 8], [200, 2], [-2, 8]], Op.is_equal, 0.0, -200 * a - (1 - h), 1)
+    ms(A("oneb"), 1.0); ms(A("dP"), -1 / 16)
+    sel(A("ppb", 0, 144), A("oneb"), [[-16, 9], [200, 2], [-1, 8]], Op.is_equal, 0.0, -200, 1)
+    sel(A("ppb", 144, 288), A("oneb"), [[-16, 9], [200, 2], [-1, 8]], Op.is_equal, 0.0, 8, 1)
+    sel(A("pm1"), ONE, [[16, 8], [-1, 16]], Op.is_equal, 0.0, -112, 1)
+    sel(A("pm2", 16, 128), A("oneb", 16, 128), [[16, 7], [-1, 16]], Op.is_equal, 0.0, -112, 1)
+    sel(A("pm2", 0, 16), A("oneb", 0, 16), [[-1, 16]], Op.is_equal, 0.0, 0, 1)
+    sel(A("ident"), ONE, [[-1, 128]], Op.is_equal, 0.0, 0, 1)
     iota(A("pi", 0, 1), [[0, 1]], 0, 1, False)
-    ms(A("TT", 512, 2728), 128.0)
-    ms(A("dP"), -1 / 8); ms(A("dN"), -1 / 16)
-    ms(A("dP", 0, 1024, 8), 1024.0); ms(A("dN", 0, 1024, 16), 1024.0)
+    for a, b in ((512, 1536), (1536, 2560), (2560, 2728)):
+        act(A("TT", a, b), A("dP", 0, b - a), 0.0, 128.0)
+    ms(A("dN"), -1 / 16); ms(A("dE"), 0.0); ms(A("ne"), 1.0); ms(A("dX"), 1 / 16); ms(A("dC"), 0.0); ms(A("one"), 1.0)
     cp(A("bdo"), A("bds"))
     ts(A("snd0"), X(A("avs", 0, 512), BD(0)), 1409.0, Op.add)
     send(0)
-    sel(A("pm1"), A("oneb"), [[16, 8], [-1, 16]], Op.is_equal, 0.0, -112, 1)
-    sel(A("pm2", 16, 128), A("oneb", 16, 128), [[16, 7], [-1, 16]], Op.is_equal, 0.0, -112, 1)
-    sel(A("pm2", 0, 16), A("oneb", 0, 16), [[-1, 16]], Op.is_equal, 0.0, 0, 1)
-    sel(A("ident"), A("oneb"), [[-1, 128]], Op.is_equal, 0.0, 0, 1)
     act(A("TT", 0, 512), A("avs", 0, 512), 1.0, -127.0)
     ts(A("d16"), A("dps", 0, NP), -1536.0, Op.add)
     pairs_pe(1, 0)
     cp(A("on1"), A("dps", NP, 512))
     ts(A("gi", 0, 1), A("pi", 0, 1), 4, Op.arith_shift_right)
-    ms(A("dX"), 1 / 16); ms(A("dC"), 0.0); ms(A("dD"), 0.0)
+    ms(A("dP", 0, 1024, 8), 1024.0); ms(A("dN", 0, 1024, 16), 1024.0)
     ms(A("W", A0 + 2048, DE), 0.0)
     pairs_v(1)
-    ms(A("dX", 0, 256, 16), -2.0 ** 25); ms(A("dC", 0, 256, 16), -2.0 ** 26); ms(A("dD", 0, 256, 16), 1.0)
+    ts(A("W", 1024, 1536), A("dps", 512, 1024), -1536.0, Op.add)
     act(A("pp"), A("ppb"))
     act(A("ps0"), A("avs", 512, 1024), 1.0, -STOP)
-    ts(A("W", 1024, 1536), A("dps", 512, 1024), -1536.0, Op.add)
     ts(A("W", 1536, 2048), A("dps", 1024, 1536), -1536.0, Op.add)
-    ts(A("W", 512, 1024), A("dps", 0, 512), -1536.0, Op.add)
-    plain_v(2, 0); plain_v(3, 0)
+    ms(A("dX", 0, 256, 16), -2.0 ** 25); ms(A("dC", 0, 256, 16), -2.0 ** 26)
+    ts(A("pi", 1, 2), A("pi", 0, 1), 15, Op.bitwise_and)
     iota(A("colr"), [[0, 16], [1, 16]], 0, 0)
-    iota(LC(0), [[16, 16]], 0, 1)
-    iota(LC(9), [[1, 16]], 0, 0)
+    iota(A("lc", 32, 64), [[1, 2], [32, 16]], 0, 0)
+    iota(LC(9), [[16, 16]], 15, 0)
     iota(LC(1), [[0, 4], [16, 4]], 0, 0)
     sel(A("bo"), A("one"), [[-16, 8], [0, 16]], Op.is_ge, 0.0, 0, 1)
     sel(A("bo"), A("bo"), [[16, 8], [0, 16]], Op.is_ge, 0.0, 15, -1)
-    fill(A("sh"), 1.0 / 64)
     dma("g", lambda: g.indirect_dma_start(T.sbs[:], None, T.sb[:], IndirectOffsetOnAxis(ap=T.gi[:, 0:1], axis=0), bounds_check=7), [A("sbs")], [A("gi")])
     dma("g", lambda: g.indirect_dma_start(T.ths[:], None, T.th[:], IndirectOffsetOnAxis(ap=T.gi[:, 0:1], axis=0), bounds_check=7), [A("ths")], [A("gi")])
-    sel(A("sh"), A("sh"), [[-1, 15], [1, 128]], Op.is_equal, 0.0, -1, -1)
+    iota(A("KC", 0, 512), [[0, 512]], 1000, 0)
+    iota(A("KC", 1536, 2728), [[0, 1192]], 1000, 0)
 
     def setup1():
-        act(A("W", A0, A0 + 2048), A("avs"))
         act(A("bob"), A("bo"))
         act(A("nbo"), A("bo"), -1.0)
         act(A("nb2"), A("bo"), -2.0)
         iota(A("SD"), [[-1, 2736]], 8, 0, False)
         dma("g", lambda: g.dma_start(T.SD[:, 8:1544], T.sbs[:, 0:1536], accum_op=Op.add), [A("SD", 8, 1544)], [A("sbs"), A("SD", 8, 1544)])
         dma("g", lambda: g.dma_start(T.SD[:, 2056:2728], T.sbs[:, 1536:2208], accum_op=Op.add), [A("SD", 2056, 2728)], [A("sbs"), A("SD", 2056, 2728)])
-        sel(A("sh"), A("sh"), [[0, 15], [1, 128]], Op.not_equal, -1.0 / 64, 0, -1)
-        ts(A("pi", 1, 2), A("pi", 0, 1), 15, Op.bitwise_and)
-        ts(PF(1), A("gi", 0, 1), 16.0, Op.mult)
-        ms(PF(7), 0.5)
+        iota(A("W", 0, 512), [[0, 512]], 0, 0)
         cp(PF(0), A("pi", 1, 2))
-        ts(LC(0), LC(0), PF(1), Op.subtract)
+        cp(A("oc"), LC(9))
+        ms(PF(7), 0.5); ms(PF(8), 1.0); ms(PF(9), 1425.0)
         ts(PF(2), PF(0), 1 / 16, Op.mult, -1536 - 15 / 16, Op.add)
         ts(LC(8), LC(1), PF(0), Op.add, SP - 3584 + 1280.0, Op.add)
-        for i in range(4):
-            ts(PF(3 + i), PF(0), 16.0 * i, Op.add)
+        ts(A("pf", 3, 7), A("lc", 16, 20), PF(0), Op.add)
+        ts(A("lc", 32, 64), A("lc", 32, 64), PF(0), Op.add, PF(0), Op.add)
         ts(A("dg"), A("colr"), PF(0), Op.is_equal)
-        ts(A("tri"), A("colr"), PF(0), Op.is_gt)
-        ts(A("oc"), LC(9), 16.0, Op.mult, 15.0, Op.add)
-        for par in (0, 1):
-            ts(LC(2 + par), LC(0), 2.0, Op.mult, float(par), Op.add)
 
     def setup2():
         for j, (src, d) in enumerate((("nbo", 0.0), ("nbo", 1.0), ("nb2", 2.0))):
             sel(A("lm", 128 * j, 128 * j + 128), A(src), [[-1, 128]], Op.not_equal, d, 0, 1)
-        sel(A("sh"), A("sh"), [[-1, 15], [0, 8], [1, 16]], Op.is_ge, 0.0, -1, 0)
+        for r in range(16):
+            sel(A("slt", 128 * r, 128 * r + 128), ONE, [[-16, 8], [0, 16]], Op.is_equal, 0.0, -r, 1)
         act(A("ng"), A("dg"), 2.0 ** 25, -2.0 ** 25)
         act(A("ng2"), A("dg"), 2.0 ** 25 + 1280, -2.0 ** 25)
-        fill(A("KC", 0, 512), 1000.0); fill(A("KC", 1536, 2728), 1000.0); fill(A("W", 0, 512), 0.0)
-        ms(A("ne"), 1.0); ms(A("dE"), 0.0); ms(A("dE", 0, 784, 49), 2.0)
+        ts(A("W", 512, 1024), A("dps", 0, 512), -1536.0, Op.add)
         ms(A("SD", 0, 4), 0)
-        for r in range(16):
-            ts(A("slt", 128 * r, 128 * r + 128), A("bob"), A("dg", r, r + 1), Op.mult)
+
+    def setup3():
+        act(A("W", A0, A0 + 2048), A("avs"))
+        for i in range(4):
+            n = 18 + 16 * i
+            act(A("dE", NE[i], NE[i + 1], n), A("dg", 0, 4), 0.0, 1.0)
+            act(A("dE", NE[i] + n - 1, NE[i + 1], n), A("dg", 0, 4), 0.0, 10.0)
+        for i in range(4):
+            n = 18 + 16 * i
+            for b in range(4):
+                act(A("dE", NE[i] + n * b + n - 17, NE[i] + n * b + n - 1), A("dg", 0, 16), -10.0)
 
     def thresholds(par):
         tt(A("mm"), A("ths", par, 512, 2), A("ng"), Op.add)
@@ -463,36 +460,40 @@ def rank_program(g, core, T, topo):
             plain_v(1, par); plain_v(2, par); plain_v(3, par)
             pairs_v(1)
             if t == 2:
-                ts(A("ono"), A("W", 1537, 2048, 2), 1536.0, Op.add)
-                ms(A("dO"), 0.0); ms(A("dO", 0, 1024, 16), 1024.0)
-                ts(LC(8), LC(8), -1536.0, Op.add)
-                act(A("W", DE, DE + 768), A("W", 512, 1280), 1.0, 1536.0)
-            else:
-                thresholds(1)
+                act(A("W", DE, DE + 512), A("W", 512, 1024), 1.0, 1536.0)
         ghosts(3 * t)
         pairs_pe(2, par)
         pairs_pe(3, par)
         level(1, 3 * t + 1)
         act(A("ps0"), will(t, 1024, 1536), 1.0, -STOP)
-        pairs_v(2); pairs_v(3)
+        pairs_v(2)
         if t == 0:
-            setup1()
+            plain_v(2, 0); setup1()
+        if t == 1:
+            thresholds(1)
         if t == 2:
-            act(A("W", DE + 768, WN), A("W", 1280, 2048), 1.0, 1536.0)
-            act(A("ng2"), A("dg"), 2.0 ** 25 - 256, -2.0 ** 25)
+            act(A("W", DE + 512, WN), A("W", 1024, 2048), 1.0, 1536.0)
+            ts(A("ono"), A("W", 1537, 2048, 2), 1536.0, Op.add)
+            ts(LC(8), LC(8), -1536.0, Op.add)
         ghosts(3 * t + 1)
         level(2, 3 * t + 2)
         act(A("ps0", 0, 256), will(t, 1536 + par, 2048, 2), 1.0, -STOP)
         act(A("ps0", 256, 512), A("colr"), -1 / 16, 15 / 16)
+        act(A("ps6", 256, 512), A("W", 1536 + par, 2048, 2))
+        pairs_v(3)
         if t == 0:
-            setup2(); thresholds(0)
+            plain_v(3, 0); setup2(); thresholds(0)
+        if t == 1:
+            ms(A("dO"), 0.0); ms(A("dO", 0, 1024, 16), 1024.0)
+        if t == 2:
+            act(A("ng2"), A("dg"), 2.0 ** 25 - 256, -2.0 ** 25)
         ghosts(3 * t + 2)
         level(3, None)
         walk(t)
 
     dma("g", lambda: g.dma_start(T.ya[:], T.W[:, A0:A0 + 2048]), [], [A("W", A0, WN)])
-    for j, e in enumerate(("y", "s", "y")):
-        dma(e, lambda: Q[e].dma_start(T.yd[:, 512 * j:512 * j + 512], T.W[:, DE + 512 * j:DE + 512 * j + 512]), [], [A("W", A0, WN)])
+    for j in range(3):
+        dma("y", lambda: g.sync.dma_start(T.yd[:, 512 * j:512 * j + 512], T.W[:, DE + 512 * j:DE + 512 * j + 512]), [], [A("W", A0, WN)])
     odd_scan(0); odd_scan(1); odd_scan(2); odd_scan(3)
     tt(A("yro", 1, 512, 2), A("so", 15, 4096, 16), A("W", A0 + 1537, A0 + 2048, 2), Op.min)
     dma("s", lambda: g.scalar.dma_start(T.yr[:], T.yro[:]), [], [A("yro")])

@@ -2,36 +2,40 @@ from concourse.bass import DstId, RemoteDMATransfer, IndirectOffsetOnAxis
 from concourse.mybir import AluOpType as Op, ActivationFunctionType as Fn
 
 F32, BF, I32, U16, F16 = "float32", "bfloat16", "int32", "uint16", "float16"
-PC = ((16, 8, 16, 24, 32, 44, 48), (16, 8, 16, 24, 28))
-NC = ((56, 40, 24, 8, 8), (40, 16, 8, 8))
+PC = ((24, 12, 24, 36, 44, 52), (20, 8, 16, 20, 32))
+NC = ((56, 40, 24, 8), (32, 16, 8, 8))
 NP, NPT = 2 * sum(PC[0]), 2 * sum(PC[1])
 A0, SP, DE, WN = 2048, 4104, 4224, 5760
-NE = (0, 72, 208, 408, 672)
+NE = (0, 19, 54, 105, 172)
 STOP = 127 + 63 / 64
 RND = 1536 + 63 / 128
+CYCLE, WAIT, GATHER, FLIGHT = 0.91, 130, 1.56, 900
+ROUNDS = 2
+SLACK = 600
 SB = {
-    "avs": (2048, BF), "dps": (1536, I32), "bds": (42, I32), "bdo": (42, U16), "sbs": (2208, I32), "ths": (512, I32),
+    "avs": (2048, BF), "dps": (1536, I32), "bds": (42, I32), "bdo": (42, U16), "ths": (512, I32),
     "W": (WN, F32), "TT": (2728, BF), "KC": (2728, F32), "SD": (2736, I32), "d16": (NP, F16), "rh": (512, F16),
     "gs": (8 * NP, F32), "gp": (8 * NP, F16), "sp": (8 * NP, F16), "gn": (16 * (512 - NP), BF), "sn": (16 * (512 - NP), F16),
     "go": (4096, BF), "so": (4096, BF),
     "on1": (512 - NP, U16), "on2": (512 - NP, U16), "on3": (256 - NPT, U16), "ono": (256, U16),
     "op1": (NP, U16), "op2": (NP, U16), "op3": (NPT, U16),
-    "dN": (1024, BF), "dP": (1024, BF), "dO": (1024, BF), "dX": (256, BF), "dC": (256, BF), "dE": (672, BF),
+    "dN": (1024, BF), "dP": (1024, BF), "dO": (512, BF), "dX": (128, BF), "dC": (256, BF), "dE": (172, BF),
     "one": (128, F32), "oneb": (144, BF), "ident": (128, BF), "pm1": (128, BF), "pm2": (128, BF),
     "bo": (128, F32), "bob": (128, BF), "nbo": (128, BF), "nb2": (128, BF), "lm": (384, BF), "pp": (288, F32), "ppb": (288, BF),
-    "slt": (2048, BF), "colr": (256, F32), "yy": (16, F32),
-    "dg": (256, F32), "ng": (256, BF), "ng2": (256, BF), "pi": (4, I32), "gi": (4, I32), "pf": (12, F32), "lc": (160, F32), "oc": (16, U16),
-    "rt": (256, F16), "rtt": (256, F16), "ax": (256, F32), "mt": (256, BF), "mp": (256, BF), "mm": (256, F32), "ll": (1024, F32),
-    "sm": (640, F32), "oh": (32, U16), "os": (16, U16), "ot": (16, U16), "ow": (16, U16), "t16": (32, F16), "m16": (256, F16), "z16": (256, F16),
-    "rm": (256, F16), "eq": (768, BF), "ne": (672, BF), "kp": (672, BF), "sg": (256, BF), "mk": (256, BF), "t2": (256, F32), "t3": (256, F32), "nw": (256, F32),
+    "slt": (2048, BF), "colr": (256, F32),
+    "dg": (256, F32), "ng": (256, BF), "ng2": (128, BF), "pi": (4, I32), "gi": (4, I32), "pf": (12, F32), "lc": (160, F32), "oc": (20, U16),
+    "rt": (256, F16), "rtt": (256, F16), "ax": (256, F32), "mt": (256, BF), "mp": (256, BF), "mm": (256, F32), "m2": (256, F32), "ll": (1024, F32),
+    "sm": (720, F32), "oh": (32, U16), "oe": (2, U16), "ot": (32, U16), "ow": (64, U16), "t16": (32, F16), "m16": (256, F16), "z16": (256, F16),
+    "rm": (256, F16), "eq": (768, BF), "ne": (704, F32), "kp": (704, F32), "sg": (256, BF), "mk": (256, BF), "t2": (256, F32), "t3": (256, F32), "nw": (256, F32),
     "yro": (512, BF),
 }
-for _i in range(9):
-    SB["snd%d" % _i] = (224, F16)
-    SB["lnd%d" % _i] = (224, F16)
 SCRATCH = {k: ("sbuf", [128, v[0]], v[1]) for k, v in SB.items()}
+SCRATCH["sdd"] = ("dram", [8, 2736], I32)
+for _i in range(9):
+    SCRATCH["snd%d" % _i] = ("sbuf", [128, 224], F16 if _i % 3 else BF)
+    SCRATCH["lnd%d" % _i] = ("sbuf", [128, 7, 32], F16 if _i % 3 else BF)
 for _i in range(8):
-    SCRATCH["ps%d" % _i] = ("psum", [128, 512], F32)
+    SCRATCH["ps%d" % _i] = ("psum", [128, 16, 32] if _i == 3 else [128, 512], F32)
 SEMAPHORES = ["cv", "cs", "ct", "cg", "loc"] + ["arr%d" % i for i in range(9)] + ["dm%d" % i for i in range(16)]
 
 
@@ -42,102 +46,146 @@ def chunks(sizes):
     return out
 
 
+def schedule(calls):
+    n = len(calls)
+    fore, back = [[] for _ in calls], [[] for _ in calls]
+    for i, c in enumerate(calls):
+        for j, wait in c["after"].items():
+            gap = calls[j]["time"] - calls[j]["hold"] + WAIT if wait else 0
+            fore[i].append((j, calls[j]["hold"] + gap)); back[j].append((i, c["hold"] + gap))
+
+    def place(order, links, least, slack):
+        at, busy = [0.0] * n, {}
+        for i in order:
+            c = calls[i]
+            t = max([at[j] + d for j, d in links[i]] + [least[i]])
+            line = busy.setdefault(c["e"], [])
+            k = 0
+            while k < len(line) and line[k][0] < t + c["hold"] + (slack if c["e"] == "g" else 0):
+                t = max(t, line[k][1]); k += 1
+            line.insert(k, (t, t + c["hold"]))
+            at[i] = t
+        return at
+
+    tail = [c["time"] - c["hold"] for c in calls]
+    rest = list(tail)
+    for i in range(n - 1, -1, -1):
+        rest[i] = max([rest[j] + d for j, d in back[i]] + [tail[i]])
+    best = None
+    for _ in range(ROUNDS):
+        start = place(sorted(range(n), key=lambda i: (-rest[i] - calls[i]["hold"], i)), fore, [0.0] * n, SLACK)
+        end = max(start[i] + calls[i]["time"] for i in range(n))
+        if best is None or end < best[0]:
+            best = (end, start)
+        rest = place(sorted(range(n), key=lambda i: (-start[i], -i)), back, tail, 0)
+    return sorted(range(n), key=lambda i: (best[1][i], i))
+
+
 def rank_program(g, core, T, topo):
     rank = T.rank_of(core)
     if rank is None:
         return
     Q = {"v": g.vector, "s": g.scalar, "t": g.tensor, "g": g, "y": g.sync}
-    cnt = {"v": 0, "s": 0, "t": 0, "g": 0}
-    seen = {e: {} for e in Q}
-    hist = {}
-    ends = {}
-    ndma = [0]
+    calls, hist, bank, rows, ndma = [], {}, {}, {}, [0]
 
     def A(name, lo=0, hi=None, st=1):
-        if hi is None:
-            hi = SCRATCH[name][1][1]
-        ap = T[name][:, lo:hi] if st == 1 else T[name][:, lo:hi:st]
-        return (ap, [(name, lo, hi)])
+        if len(SCRATCH[name][1]) == 3:
+            lo, hi = lo, 224 if hi is None else hi
+            ap = T[name][:, lo // 32:hi // 32, :] if hi - lo > 32 else T[name][:, lo // 32, :]
+        else:
+            hi = SCRATCH[name][1][1] if hi is None else hi
+            ap = T[name][:, lo:hi] if st == 1 else T[name][:, lo:hi:st]
+        cols = range(lo, hi, st)
+        return (ap, [(name, a, a + 1) for a in cols] if st > 16 else [(name, lo, hi)], len(cols), 4 if SCRATCH[name][2] in (F32, I32) else 2, name[:2] == "ps", False)
 
     def X(win, off):
-        return (win[0].indirect(off[0]), win[1] + off[1])
+        return (win[0].indirect(off[0]), win[1] + off[1], 16 * off[2], win[3], False, True)
 
-    def order(e, w, r):
-        need = {}
-        for regs, isw in ((r, False), (w, True)):
+    def put(e, f, wr, rr, time, hold=None, sem=None):
+        i, after = len(calls), {}
+        for regs, isw in ((rr, False), (wr, True)):
             for name, lo, hi in regs:
-                ps = name[:2] == "ps"
-                for (a, b, sem, n, who, ww) in hist.get(name, ()):
-                    if who == e:
-                        hit = (ww or isw) and e != "t" and a < hi and lo < b
-                    else:
-                        hit = ps or ((ww or isw) and a < hi and lo < b)
-                    if hit and need.get(sem, 0) < n:
-                        need[sem] = n
-        for sem, n in need.items():
-            if seen[e].get(sem, 0) < n:
-                Q[e].wait_ge(T.sem[sem], n); seen[e][sem] = n
-
-    def note(w, r, sem, n, who):
-        for regs, isw in ((r, False), (w, True)):
+                for a, b, j, ww in hist.get(name, ()):
+                    if (ww or isw) and a < hi and lo < b:
+                        after[j] = True
+                if name[:2] == "ps":
+                    run = bank.setdefault(name, [e, [], []])
+                    if run[0] != e:
+                        run[0], run[1], run[2] = e, [], run[1]
+                    for j in run[2]:
+                        after[j] = True
+                    if e == "t" and run[1]:
+                        after[run[1][-1]] = True
+                    run[1].append(i)
+        after.pop(i, None)
+        for j in after:
+            after[j] = not (e == "t" and calls[j]["e"] == "t")
+        if e in rows:
+            if rows[e] is not None:
+                after.setdefault(rows[e], False)
+            rows[e] = i
+        for regs, isw in ((rr, False), (wr, True)):
             for name, lo, hi in regs:
                 h = hist.setdefault(name, [])
                 if isw:
-                    h[:] = [x for x in h if not (lo <= x[0] and x[1] <= hi and (x[4] == who or name[:2] != "ps"))]
-                else:
-                    h[:] = [x for x in h if not (x[4] == who and not x[5] and lo <= x[0] and x[1] <= hi)]
-                h.append((lo, hi, sem, n, who, isw))
-        ends[sem] = n
+                    h[:] = [x for x in h if not (lo <= x[0] and x[1] <= hi)]
+                h.append((lo, hi, i, isw))
+        calls.append({"e": e, "f": f, "after": after, "time": time, "hold": time if hold is None else hold, "sem": sem})
 
-    def do(e, f, w, r, inc=True, scat=False):
-        wr = list(w[1]); rr = [x for o in r for x in o[1]]
-        if scat:
+    def do(e, f, w, r, cycles):
+        wr, rr = list(w[1]), [x for o in r for x in o[1]]
+        if w[5]:
             rr += wr[1:]; wr = wr[:1]
-        order(e, wr, rr)
-        ins = f()
-        if inc:
-            cnt[e] += 1; ins.then_inc(T.sem["c" + e], 1)
-        note(wr, rr, "c" + e, cnt[e] + (0 if inc else 1), e)
+            put(e, f, wr, rr, 55 + 3.8 * CYCLE * w[2])
+        elif r and r[0][5]:
+            put(e, f, wr, rr, (55 if e == "v" else 70) + GATHER * CYCLE * w[2])
+        else:
+            put(e, f, wr, rr, max(64, cycles) * CYCLE)
 
-    def dma(e, f, w, r):
-        wr = [x for o in w for x in o[1]]; rr = [x for o in r for x in o[1]]
-        order(e, wr, rr)
-        sem = "dm%d" % ndma[0]; ndma[0] += 1
-        f().then_inc(T.sem[sem], 16)
-        note(wr, rr, sem, 16, sem)
+    def dma(e, f, w, r, size, hold=60):
+        put(e, f, [x for o in w for x in o[1]], [x for o in r for x in o[1]], hold + 1800 + size / 200, hold, ("dm%d" % ndma[0], 16))
+        ndma[0] += 1
 
-    def cp(o, i): do("v", lambda: g.vector.tensor_copy(o[0], i[0]), o, [i])
-    def tt(o, a, b, op, scat=False): do("v", lambda: g.vector.tensor_tensor(o[0], a[0], b[0], op), o, [a, b], scat=scat)
-    def ms(o, c): do("v", lambda: g.vector.memset(o[0], c), o, [])
-    def tr(o, i): do("v", lambda: g.vector.transpose(o[0], i[0]), o, [i])
-    def sc(o, a, b, o0, o1): do("v", lambda: g.vector.tensor_tensor_scan(o[0], a[0], b[0], 0.0, o0, o1), o, [a, b])
+    def wide(*ops): return ops[0][2] * (0.5 if max(o[3] for o in ops) == 2 else 1)
+    def cp(o, i): do("v", lambda: g.vector.tensor_copy(o[0], i[0]), o, [i], wide(o, i))
+    def tt(o, a, b, op): do("v", lambda: g.vector.tensor_tensor(o[0], a[0], b[0], op), o, [a, b], o[2] * (1 if a[4] or b[4] else 2))
+    def ms(o, c): do("v", lambda: g.vector.memset(o[0], c), o, [], wide(o))
+    def tr(o, i): do("v", lambda: g.vector.transpose(o[0], i[0]), o, [i], wide(o, i))
+    def sc(o, a, b, o0, o1): do("v", lambda: g.vector.tensor_tensor_scan(o[0], a[0], b[0], 0.0, o0, o1), o, [a, b], wide(o, a, b))
 
     def ts(o, a, s1, o0, s2=None, o1=None):
         r = [a] + [s for s in (s1, s2) if isinstance(s, tuple)]
         v1 = s1[0] if isinstance(s1, tuple) else s1
         v2 = s2[0] if isinstance(s2, tuple) else s2
         if o1 is None:
-            do("v", lambda: g.vector.tensor_scalar(o[0], a[0], v1, None, o0), o, r)
+            do("v", lambda: g.vector.tensor_scalar(o[0], a[0], v1, None, o0), o, r, wide(o, a))
         else:
-            do("v", lambda: g.vector.tensor_scalar(o[0], a[0], v1, v2, o0, o1), o, r)
+            do("v", lambda: g.vector.tensor_scalar(o[0], a[0], v1, v2, o0, o1), o, r, wide(o, a))
 
     def act(o, i, scale=1.0, bias=0.0, fn=Fn.Copy):
         r = [i] + [s for s in (scale, bias) if isinstance(s, tuple)]
         sv = scale[0] if isinstance(scale, tuple) else float(scale)
         bv = bias[0] if isinstance(bias, tuple) else float(bias)
-        do("s", lambda: g.scalar.activation(o[0], i[0], fn, bias=bv, scale=sv), o, r)
+        do("s", lambda: g.scalar.activation(o[0], i[0], fn, bias=bv, scale=sv), o, r, o[2])
 
-    def mm(o, l, r, st, sp, inc=None):
-        do("t", lambda: g.tensor.matmul(o[0], l[0], r[0], st, sp), o, [l, r], inc=sp if inc is None else inc)
+    def mms(group):
+        def f():
+            for o, l, r, st, sp in group:
+                ins = g.tensor.matmul(o[0], l[0], r[0], st, sp)
+            return ins
+        put("t", f, [x for m in group for x in m[0][1]], [x for m in group for x in m[1][1] + m[2][1]],
+            sum(max(64, m[0][2]) * (4 if m[2][3] == 4 else 1) * CYCLE for m in group))
+
+    def mm(o, l, r, st, sp): mms([(o, l, r, st, sp)])
 
     def iota(o, pat, base, cm, fl=True):
         if fl:
-            do("g", lambda: g.iota(o[0], pat, base, cm, allow_small_or_imprecise_dtypes=True), o, [])
+            do("g", lambda: g.iota(o[0], pat, base, cm, allow_small_or_imprecise_dtypes=True), o, [], 160 + 2 * o[2])
         else:
-            do("g", lambda: g.iota(o[0], pat, base, cm), o, [])
+            do("g", lambda: g.iota(o[0], pat, base, cm), o, [], 160 + 2 * o[2])
 
     def sel(o, i, pat, op, fill, base, cm):
-        do("g", lambda: g.affine_select(o[0], i[0], pat, op, fill, base, cm), o, [i])
+        do("g", lambda: g.affine_select(o[0], i[0], pat, op, fill, base, cm), o, [i], 205 + 2 * o[2])
 
     def S(j): return A("sm", 16 * j, 16 * j + 16)
     def LC(j): return A("lc", 16 * j, 16 * j + 16)
@@ -151,7 +199,6 @@ def rank_program(g, core, T, topo):
         return A("avs", lo, hi, st) if t == 0 else A("W", A0 + lo, A0 + hi, st)
 
     def send(x):
-        order("g", [], A("snd%d" % x)[1])
         trs = []
         used = [0, 0]
         for d in range(1, 8):
@@ -164,29 +211,23 @@ def rank_program(g, core, T, topo):
             used[same] += k
             trs.append(RemoteDMATransfer(dst_ids=[DstId(rid=rid, pnc=pid)], dma_engine_mask=sum(1 << e for e in mine),
                                          remote_sem=T.sem["arr%d" % x], src=A("snd%d" % x, 32 * d - 32, 32 * d)[0], dst=A("lnd%d" % x, 32 * d - 32, 32 * d)[0]))
-        g.remote_dma_fused(trs, local_sem=T.sem.loc)
-        ends["loc"] = ends.get("loc", 0) + 7 * k
-        note(A("lnd%d" % x)[1], [], "arr%d" % x, 7 * k, "arr")
+        hold = 400 if x else 1900
+        put("g", lambda: g.remote_dma_fused(trs, local_sem=T.sem.loc), A("lnd%d" % x)[1], A("snd%d" % x)[1], hold + FLIGHT, hold, ("arr%d" % x, 7 * k))
 
     def ghosts(x):
-        for d in range(1, 8):
-            mm(A("ps3", 32 * d - 32, 32 * d), A(("ident", "pm1", "pm2")[d % 3]), A("lnd%d" % x, 32 * d - 32, 32 * d), True, True, inc=d == 7)
+        def blocks(name, d): return (T[name][:, d - 1:7:3, :], [(name, 0, 224)], 32 * len(range(d, 8, 3)), 2, name == "ps3", False)
+        mms([(blocks("ps3", d), A(("ident", "pm1", "pm2")[d % 3]), blocks("lnd%d" % x, d), True, True) for d in (1, 2, 3)])
         l = x % 3
-        act(A("TT", 2048 + 224 * l, 2272 + 224 * l), A("ps3", 0, 224), 1.0, -1536.0)
+        act(A("TT", 2048 + 224 * l, 2272 + 224 * l), A("ps3", 0, 224), 1.0, -1536.0 if l else 0.0)
 
-    def pairs_pe(l, par):
+    def lists(l, par):
         n = NP if l < 3 else NPT
         b = "ps2" if l == 2 else "ps1"
         for h in (0, 1):
             for a in (0, 1):
                 r = A("d16", a, n, 2) if l == 1 else (A("W", 1024 + a, 1024 + n, 2) if l == 2 else A("W", 1536 + par + 2 * a, 1536 + 2 * n, 4))
-                mm(A(b, h * n // 2, (h + 1) * n // 2), A("ppb" if l == 1 else "pp", 160 - 152 * h - 8 * a, 288 - 152 * h - 8 * a), r, a == 0, a == 1, inc=h + a == 2)
-
-    def pairs_v(l):
-        n = NP if l < 3 else NPT
-        ts(A("op%d" % l), A("ps2" if l == 2 else "ps1", 0, n), 1536.0, Op.add)
-
-    def plain_v(l, par):
+                mm(A(b, h * n // 2, (h + 1) * n // 2), A("ppb" if l == 1 else "pp", 160 - 152 * h - 8 * a, 288 - 152 * h - 8 * a), r, a == 0, a == 1)
+        ts(A("op%d" % l), A(b, 0, n), 1536.0, Op.add)
         if l < 3:
             ts(A("on%d" % l), A("W", 512 * l + NP, 512 * l + 512), 1536.0, Op.add)
         else:
@@ -200,6 +241,7 @@ def rank_program(g, core, T, topo):
         def pair(a, b): tt(A("gp", 16 * a, 16 * b), X(TW, A(o, a, b)), A("gs", 16 * a, 16 * b), Op.min)
         def scan2(a, b): sc(A("sp", 16 * a, 16 * b), A("dP", 0, 16 * (b - a)), A("gp", 16 * a, 16 * b), Op.add, Op.min)
         def scan(a, b): sc(A("sn", 16 * a, 16 * b), A("dN", 0, 16 * (b - a)), A("gn", 16 * a, 16 * b), Op.add, Op.min)
+        rows["v"], rows["s"] = None, None
         for j, (a, b) in enumerate(pc):
             if j == 0:
                 ts(A("gs", 16 * a, 16 * b), X(TW, A(o, n // 2 + a, n // 2 + b)), -0.5, Op.add)
@@ -212,14 +254,21 @@ def rank_program(g, core, T, topo):
         for j in range(4, len(pc)):
             scan2(a, pc[j - 1][0]); a = pc[j - 1][0]
             pair(*pc[j])
-        scan2(a, pc[-1][0]); scan(*nc[0]); scan2(*pc[-1]); scan(*nc[1])
-        key(A("sp", 7, 8 * n, 8), 0, n)
+        scan2(a, pc[-1][0])
+        e = 0
+        if l == 3:
+            rows.clear()
+            e = 128
+            key(A("sp", 7, 8 * e, 8), 0, e)
+        scan(*nc[0]); scan2(*pc[-1]); scan(*nc[1])
+        key(A("sp", 8 * e + 7, 8 * n, 8), e, n)
         for a, b in nc[2:-1]:
             scan(a, b)
-        a = nc[-2][0]
-        key(A("sn", 15, 16 * a, 16), n, n + a)
+        e = nc[-2][0]
+        key(A("sn", 15, 16 * e, 16), n, n + e)
         scan(*nc[-1])
-        key(A("sn", 16 * a + 15, 16 * m, 16), n + a, n + m)
+        key(A("sn", 16 * e + 15, 16 * m, 16), n + e, n + m)
+        rows.clear()
         if l < 3:
             K = A("KC", 512 * l, 512 * l + 512)
             ts(A("snd%d" % x), X(K, BD(l)), RND, Op.add)
@@ -227,275 +276,232 @@ def rank_program(g, core, T, topo):
             ts(A("rh"), K, RND, Op.add)
             ts(A("TT", 512 * l, 512 * l + 512), A("rh"), -1536.0, Op.add)
 
-    def odd_scan(j): sc(A("so", 1024 * j, 1024 * j + 1024), A("dO"), A("go", 1024 * j, 1024 * j + 1024), Op.add, Op.min)
-    def odd_get(j): act(A("go", 256 * j, 256 * j + 256), X(TW, A("ono", 16 * j, 16 * j + 16)), 1.0, 127.0)
-
     def walk(t):
         par, last = t & 1, t == 2
-        sh, w0, cd = (-256.0, A0, DE - 1024.0) if last else (1280.0, 512, -512.0)
-        WW = A("W", w0, WN if last else SP + 64)
-        EB, ZB = {0: "ps1", 128: "ps2"}, {0: "ps3", 128: "ps4"}
-        def odd(*js):
-            for j in js:
-                if last:
-                    odd_get(j)
+        sh, w0, cd = (-256.0, A0 - 64, DE - 1024.0) if last else (1280.0, 448, -512.0)
+        WW = A("W", w0, WN if last else SP)
+        EB, ZB = {0: "ps1", 128: "ps2"}, {0: "ps5", 128: "ps4"}
         def OH(j, h): return A("oh", 16 * j - 16 + h // 16, 16 * j - 8 + h // 16)
-        def preE(h): mm(A(EB[h], 0, 128), A("nbo"), H("rm", h), True, False)
-        def preZ(j, h): mm(A(ZB[h], 0, 128), A("ident"), A("ng2" if j == 2 else "ng", 0, 128), True, False)
-        def a_(j, h):
-            tt(H("m16", h), X(A("KC"), OH(j, h)), H("mp", h), Op.mult)
-            mm(A(EB[h], 0, 128), A("bob"), H("m16", h), False, True)
-        def c_(j, h): ts(H("eq", h, 256 * j), A(EB[h], 0, 128), PF(2), Op.is_equal)
-        def d_(j, h):
-            src = X(A("W", 0, 2728), OH(j, h)) if j else H("ps6", h, 256)
-            tt(H("z16", h), src, H("eq", h, 256 * j), Op.mult)
-            mm(A(ZB[h], 0, 128), A("bob"), H("z16", h), False, True)
-        def f_(j, h): sc(H("ll", h, 256 * j), A("dC", 0, 128), A(ZB[h], 0, 128), Op.add, Op.max)
-        def g_(j, h): ts(OH(j + 1, h), A("ll", 256 * j + h + 15, 256 * j + h + 128, 16), 1536.0, Op.add)
-        def mark(j): mm(A("ps5", 0, 256), A("lm", 128 * j, 128 * j + 128), A("eq", 256 * j, 256 * j + 256), j == 0, j == 2)
-        def spread(b, src, rs):
-            for r in rs:
-                mm(A(b, r, 256, 16), A("slt", 128 * r, 128 * r + 128), src, True, True, inc=r == 15)
+        def spread(b, src, n):
+            for a in range(0, 16, n):
+                mms([(A(b, r, 256, 16), A("slt", 128 * r, 128 * r + 128), src, True, True) for r in range(a, a + n)])
 
-        K0 = A("ps0", 0, 256)
-        preZ(0, 0); preZ(0, 128)
         mm(A("ps7", 0, 256), A("ident"), A("ng"), True, False)
-        odd(0, 1, 2, 3, 4)
-        if t == 0:
-            setup3()
-        ts(A("rt"), K0, RND, Op.add)
-        mm(A("ps6", 0, 256), A("ident"), A("rt"), True, True)
-        tr(A("rtt"), A("rt"))
-        sc(A("ax"), A("dX"), A("rtt"), Op.add, Op.max)
-        tt(A("t2"), A("ps0", 256, 512), A("rtt"), Op.add)
-        tt(A("mt"), X(A("ax"), A("oc")), A("t2"), Op.is_equal)
+        for h in (0, 128):
+            ts(H("rt", h), H("ps0", h), RND, Op.add)
+            mm(H("ps6", h), A("ident"), H("rt", h), True, True)
+        for h in (0, 128):
+            tr(H("rtt", h), H("rt", h))
+            sc(H("ax", h), A("dX"), H("rtt", h), Op.add, Op.max)
+            tt(H("t2", h), A("ps0", 256, 384), H("rtt", h), Op.add)
+            tt(H("mt", h), X(H("ax", h), A("oc", 0, 8)), H("t2", h), Op.is_equal)
+            tr(H("mp", h), H("mt", h))
+            tt(H("rm", h), H("ps6", h), H("mp", h), Op.mult)
+            mm(A("ps7", h, h + 128), A("bob"), H("rm", h), False, h > 0)
+            for j in range(3):
+                tt(H("m16", h), X(A("KC"), OH(j, h)) if j else H("ps0", h), H("mp", h), Op.mult)
+                if j:
+                    mm(A(EB[h], 0, 128), A("nbo"), H("rm", h), True, False)
+                mm(A(EB[h], 0, 128), A("bob"), H("m16", h), j == 0, j > 0)
+                if j == 0:
+                    mm(A(EB[h], 0, 128), A("nbo"), H("rm", h), False, True)
+                ts(H("eq", h, 256 * j), A(EB[h], 0, 128), PF(2), Op.is_equal)
+                tt(H("z16", h), X(A("W", 0, 2728), OH(j, h)) if j else H("ps6", h, 256), H("eq", h, 256 * j), Op.mult)
+                mm(A(ZB[h], 0, 128), A("ident"), A("ng2" if j == 2 else "ng", 0, 128), True, False)
+                mm(A(ZB[h], 0, 128), A("bob"), H("z16", h), False, True)
+                sc(H("ll", h, 256 * j), A("dC", 0, 128), A(ZB[h], 0, 128), Op.add, Op.max)
+                if j < 2:
+                    ts(OH(j + 1, h), A("ll", 256 * j + h + 15, 256 * j + h + 128, 16), 1536.0, Op.add)
+        for j in range(3):
+            mm(A("ps3", 0, 256), A("lm", 128 * j, 128 * j + 128), A("eq", 256 * j, 256 * j + 256), j == 0, j == 2)
+        act(A("sg"), A("ps3", 0, 256), 1.0, PF(7), Fn.Sign)
+        act(A("mk"), A("sg"), fn=Fn.Relu)
         if last:
             ts(A("yro", 0, 512, 2), A("rt"), -1409.0, Op.add)
-        tr(A("mp"), A("mt"))
-        for h in (0, 128):
-            tt(H("m16", h), H("ps0", h), H("mp", h), Op.mult)
-            mm(A(EB[h], 0, 128), A("bob"), H("m16", h), True, False)
-            tt(H("rm", h), H("ps6", h), H("mp", h), Op.mult)
-            mm(A(EB[h], 0, 128), A("nbo"), H("rm", h), False, True)
-        mm(A("ps7", 0, 256), A("bob"), A("rm"), False, True)
-        z1, z2, z3, v = LL(0), LL(1), LL(2), LL(3)
-        nbv, mv, okb, s1, x1, rp, al, als, nb, p1, s2, sb2, p2, q2, b3, dl = [S(j) for j in range(16)]
-        u = [S(16 + j) for j in range(12)]
-        t16, val, tf = A("t16", 0, 16), A("t16", 16, 32), S(28)
-        odd(5, 6)
-        c_(0, 0); c_(0, 128)
-        d_(0, 0); preE(0); d_(0, 128); preE(128); mark(0)
-        sc(A("ll", 768, 1024), A("dC"), A("ps7", 0, 256), Op.add, Op.max)
-        f_(0, 0); preZ(1, 0); f_(0, 128); preZ(1, 128)
-        act(S(32), v, -1.0, PF(9), Fn.Relu); act(S(31), z1, fn=Fn.Abs)
-        act(mv, S(32), -1.0, 16.0); act(s1, S(31), -1.0, PF(8), Fn.Relu)
-        g_(0, 0); tt(nbv, v, LC(6 + par), Op.subtract); g_(0, 128)
-        act(S(33), nbv, 1.0, PF(7), Fn.Sign); act(okb, S(33), 2048.0, 2048.0)
-        a_(1, 0); a_(1, 128)
-        odd(7)
-        tt(x1, nbv, s1, Op.mult)
-        tt(u[0], s1, LC(2 + par), Op.mult)
-        c_(1, 0)
-        tt(rp, nbv, x1, Op.is_lt)
-        tt(u[1], x1, okb, Op.add)
-        tt(p1, z1, u[0], Op.add)
-        c_(1, 128)
-        d_(1, 0); preE(0); d_(1, 128); preE(128); mark(1)
-        act(al, rp, -2048.0, 512.0); act(als, rp, -2048.0, 512.0 + sh); act(nb, rp, 4096.0, 1544.0 - 4096.0 - sh)
-        tt(val, u[1], mv, Op.min)
-        f_(1, 0); preZ(2, 0)
-        f_(1, 128); preZ(2, 128)
-        spread("ps0", val, range(4))
-        act(S(31), z2, fn=Fn.Abs); act(s2, S(31), -1.0, PF(8), Fn.Relu); act(sb2, s2, 4096.0)
-        g_(1, 0); g_(1, 128)
-        a_(2, 0); a_(2, 128)
-        spread("ps0", val, range(4, 12))
-        tt(u[2], s2, p1, Op.mult)
-        c_(2, 0)
-        tt(u[3], z1, sb2, Op.add)
-        tt(p2, z2, u[2], Op.add)
-        c_(2, 128)
-        tt(q2, u[3], LC(2 + par), Op.min)
-        act(u[4], p2, 1.0, cd)
-        d_(2, 0); mark(2)
-        tt(u[5], q2, p2, Op.subtract)
-        act(u[5], u[5], 1.0, 1536.0)
-        d_(2, 128)
-        spread("ps0", val, range(12, 16))
-        act(A("sg"), A("ps5", 0, 256), 1.0, PF(7), Fn.Sign)
-        act(A("mk"), A("sg"), fn=Fn.Relu)
-        odd(8)
-        tt(u[6], p2, al, Op.min)
-        tt(b3, u[4], rp, Op.mult)
-        tt(u[5], u[5], rp, Op.mult)
-        f_(2, 0)
-        tt(dl, u[5], u[6], Op.add)
-        f_(2, 128)
-        ts(u[7], z3, sh, Op.is_equal)
-        tt(u[8], z3, als, Op.min)
-        tt(u[9], z3, nb, Op.add)
-        tt(u[10], u[7], dl, Op.mult)
-        tt(u[8], u[8], b3, Op.add)
-        tt(u[11], u[7], p2, Op.mult)
-        tt(t16, u[10], u[8], Op.add)
-        spread("ps7", t16, range(16))
-        tt(tf, u[10], u[8], Op.add)
-        tt(u[9], u[9], u[11], Op.add)
-        ts(A("ot"), t16, 1792.0, Op.add)
-        act(A("nw"), X(WW, A("ot")))
-        cp(A("os"), u[9])
-        tt(S(29), tf, LC(8), Op.subtract)
-        tt(K0, K0, A("mp"), Op.mult)
-        tt(A("t2"), X(A("SD"), A("os")), A("mk"), Op.mult)
-        for i in range(3, -1, -1):
-            for b in range(4):
-                a, c = NE[i] + (18 + 16 * i) * b + 2, 4 * b + i
-                act(A("ne", a, a + 16 * i + 16), A("ps7", 64 * b, 16 * c + 16), -1.0, A("sm", 448 + c, 449 + c), Fn.Abs)
-        odd(*range(9, 16))
-        tt(A("t3"), A("t2"), K0, Op.subtract)
-        def keep(i): sc(A("kp", NE[i], NE[i + 1]), A("ne", NE[i], NE[i + 1]), A("dE", NE[i], NE[i + 1]), Op.min, Op.add)
-        def kept(i): tt(A("yy", 4 * i, 4 * i + 4), A("sm", 464 + i, 480, 4), A("kp", NE[i] + 17 + 16 * i, NE[i + 1], 18 + 16 * i), Op.mult)
-        def place(i):
-            ts((T.ow[:, i:16:4], [("ow", i, i + 1)]), A("yy", 4 * i, 4 * i + 4), PF(3 + i), Op.add, float(SP - w0), Op.add)
-        keep(3); keep(2); kept(3); keep(1); kept(2); place(3); kept(1); place(2); keep(0); place(1); kept(0); place(0)
-        for b in range(3, -1, -1):
-            tt(X(WW, (T.ow[:, 4 * b:4 * b + 4], [("ow", 0, 4)])), A("nw", 64 * b, 64 * b + 64), A("t3", 64 * b, 64 * b + 64), Op.add, scat=True)
 
-    dma("y", lambda: g.sync.dma_start(T.bds[:], T.bd[:]), [A("bds")], [])
-    dma("s", lambda: g.scalar.dma_start(T.avs[:, 0:512], T.av[:, 0:512]), [A("avs", 0, 512)], [])
-    dma("y", lambda: g.sync.dma_start(T.dps[:, 0:512], T.dp[:, 0:512]), [A("dps", 0, 512)], [])
-    dma("s", lambda: g.scalar.dma_start(T.avs[:, 512:2048], T.av[:, 512:2048]), [A("avs", 512, 2048)], [])
-    dma("y", lambda: g.sync.dma_start(T.dps[:, 512:1536], T.dp[:, 512:1536]), [A("dps", 512, 1536)], [])
-    ms(A("oneb"), 1.0); ms(A("dP"), -1 / 16)
+        K0 = A("ps0", 0, 256)
+        z1, z2, z3, v = LL(0), LL(1), LL(2), LL(3)
+        def S2(j): return A("sm", 16 * j, 16 * j + 32)
+        e, nbv, o = LC(2 + 2 * par), LC(3), 1 - par
+        x1, okb, u1, de, mv, rp, al, als, nb = S(o), S(2 + o), S(5 + o), S(4 + 3 * par), S(10), S(12), S(14), S(15), S(16)
+        q2, p2, b3, dl, s3, tf = S(22 + par), S(22 + o), S(26), S(28), S(29), S(36)
+        t16, val = A("t16", 0, 16), A("t16", 16, 32)
+        sc(A("ll", 768, 1024), A("dC"), A("ps7", 0, 256), Op.add, Op.max)
+        act(S(11), v, -1.0, PF(9), Fn.Relu); act(mv, S(11), -1.0, 16.0)
+        tt(nbv, v, LC(6 + par), Op.subtract)
+        act(S(17), nbv, 1.0, PF(7), Fn.Sign); act(okb, S(17), 2048.0, 2048.0)
+        act(S(38), z1, fn=Fn.Abs); act(S(8), S(38), -1.0, PF(8), Fn.Relu); act(S(9), S(38), -1.0, PF(8), Fn.Relu)
+        act(S(2 + par), z1); act(S(20 + par), z1)
+        tt(S2(0), S2(8), A("lc", 32 + 16 * par, 64 + 16 * par), Op.mult)
+        tt(rp, nbv, x1, Op.is_lt)
+        tt(S2(5), S2(0), S2(2), Op.add)
+        tt(de, e, z1, Op.subtract)
+        act(S(13), rp); act(al, rp, -2048.0, 512.0); act(als, rp, -2048.0, 512.0 + sh); act(nb, rp, 4096.0, 1544.0 - 1856.0 - 4096.0 - sh)
+        tt(val, u1, mv, Op.min)
+        spread("ps0", val, 4)
+        for h in (128, 0):
+            tt(H("ps0", h), H("ps0", h), H("mp", h), Op.mult)
+        act(S(39), z2, fn=Fn.Abs); act(S(40), S(39), -1.0, PF(8), Fn.Relu); act(S(41), S(39), -1.0, PF(8), Fn.Relu)
+        act(S(20 + o), z2)
+        tt(S2(18), S2(40), S2(4 + 2 * par), Op.mult)
+        tt(S2(22), S2(18), S2(20), Op.add)
+        tt(S(42), q2, p2, Op.subtract); tt(S(43), p2, al, Op.min)
+        act(S(24), p2, 1.0, cd); act(S(25), S(42), 1.0, 1536.0)
+        tt(S2(26), S2(24), S2(12), Op.mult)
+        tt(dl, S(27), S(43), Op.add)
+        ts(s3, z3, sh, Op.is_equal)
+        tt(S(30), z3, als, Op.min)
+        tt(S(35), z3, nb, Op.add)
+        tt(S(32), s3, dl, Op.mult)
+        tt(S(34), S(30), b3, Op.add)
+        tt(S(33), s3, p2, Op.mult)
+        tt(t16, S(32), S(34), Op.add)
+        spread("ps7", t16, 4)
+        tt(S2(36), S2(32), S2(34), Op.add)
+        ts(A("ot"), S2(36), 1856.0, Op.add)
+        for h in (128, 0):
+            act(H("nw", h), X(WW, A("ot", h // 16, 8 + h // 16)))
+            tt(H("t2", h), X(A("SD"), A("ot", 16 + h // 16, 24 + h // 16)), H("mk", h), Op.mult)
+            tt(H("t3", h), H("t2", h), H("ps0", h), Op.subtract)
+        for i in range(4):
+            act(A("ne", NE[i + 1] - 1, 704, 176), A("sm", 576 + i, 592, 4), 1 / 4096, PF(3 + i), Fn.Identity)
+        tt(A("m16", 0, 64), X(tf, A("oc", 16, 20)), A("dg", 0, 64), Op.mult)
+        mm(A("ps2", 0, 64), A("bob"), A("m16", 0, 64), True, True)
+        for b in range(3, -1, -1):
+            for i in range(4):
+                c = 4 * b + i
+                act(A("ne", 176 * b + NE[i] + 2, 176 * b + NE[i + 1] - 1), A("ps7", 64 * b, 16 * c + 16) if b < 3 else A("ps2", 0, 16 * i + 16), -1.0, A("sm", 576 + c, 577 + c), Fn.Abs)
+            sc(A("kp", 176 * b, 176 * b + 172), A("ne", 176 * b, 176 * b + 172), A("dE"), Op.min, Op.add)
+            ts(A("ow", 16 * b, 16 * b + 16), X(A("kp", 176 * b, 176 * b + 172), A("oe", 0, 1)), 4096.0, Op.mult)
+            tt(X(WW, A("ow", 16 * b, 16 * b + 4)), A("nw", 64 * b, 64 * b + 64), A("t3", 64 * b, 64 * b + 64), Op.add)
+
+    dma("y", lambda: g.sync.dma_start(T.bds[:], T.bd[:]), [A("bds")], [], 21504)
+    dma("s", lambda: g.scalar.dma_start(T.avs[:, 0:512], T.av[:, 0:512]), [A("avs", 0, 512)], [], 131072)
+    dma("y", lambda: g.sync.dma_start(T.dps[:, 0:512], T.dp[:, 0:512]), [A("dps", 0, 512)], [], 262144)
+    dma("s", lambda: g.scalar.dma_start(T.avs[:, 512:2048], T.av[:, 512:2048]), [A("avs", 512, 2048)], [], 393216)
+    dma("y", lambda: g.sync.dma_start(T.dps[:, 512:1536], T.dp[:, 512:1536]), [A("dps", 512, 1536)], [], 524288)
+    ms(A("oneb"), 1.0); ms(A("one"), 1.0); ms(A("dP"), -1 / 16); ms(A("dN"), -1 / 16); ms(A("dX"), 1 / 16); ms(A("dC"), 0.0); ms(A("dE"), 0.0)
+    for a, b in ((512, 1536), (1536, 2560), (2560, 2728)):
+        act(A("TT", a, b), A("dP", 0, b - a), 0.0, 128.0)
+    ms(A("dP", 0, 1024, 8), 1024.0); ms(A("dN", 0, 1024, 16), 1024.0)
+    ms(A("dX", 0, 128, 16), -2.0 ** 25); ms(A("dC", 0, 256, 16), -2.0 ** 26)
+    ms(A("W", A0 + 2048, DE), 0.0); ms(PF(7), 0.5); ms(PF(8), 1.0); ms(PF(9), 1425.0)
     sel(A("ppb", 0, 144), A("oneb"), [[-16, 9], [200, 2], [-1, 8]], Op.is_equal, 0.0, -200, 1)
     sel(A("ppb", 144, 288), A("oneb"), [[-16, 9], [200, 2], [-1, 8]], Op.is_equal, 0.0, 8, 1)
     sel(A("pm1"), ONE, [[16, 8], [-1, 16]], Op.is_equal, 0.0, -112, 1)
     sel(A("pm2", 16, 128), A("oneb", 16, 128), [[16, 7], [-1, 16]], Op.is_equal, 0.0, -112, 1)
     sel(A("pm2", 0, 16), A("oneb", 0, 16), [[-1, 16]], Op.is_equal, 0.0, 0, 1)
     sel(A("ident"), ONE, [[-1, 128]], Op.is_equal, 0.0, 0, 1)
-    iota(A("pi", 0, 1), [[0, 1]], 0, 1, False)
-    for a, b in ((512, 1536), (1536, 2560), (2560, 2728)):
-        act(A("TT", a, b), A("dP", 0, b - a), 0.0, 128.0)
-    ms(A("dN"), -1 / 16); ms(A("dE"), 0.0); ms(A("ne"), 1.0); ms(A("dX"), 1 / 16); ms(A("dC"), 0.0); ms(A("one"), 1.0)
-    cp(A("bdo"), A("bds"))
-    ts(A("snd0"), X(A("avs", 0, 512), BD(0)), 1409.0, Op.add)
-    send(0)
-    act(A("TT", 0, 512), A("avs", 0, 512), 1.0, -127.0)
-    ts(A("d16"), A("dps", 0, NP), -1536.0, Op.add)
-    pairs_pe(1, 0)
-    cp(A("on1"), A("dps", NP, 512))
-    ts(A("gi", 0, 1), A("pi", 0, 1), 4, Op.arith_shift_right)
-    ms(A("dP", 0, 1024, 8), 1024.0); ms(A("dN", 0, 1024, 16), 1024.0)
-    ms(A("W", A0 + 2048, DE), 0.0)
-    pairs_v(1)
-    ts(A("W", 1024, 1536), A("dps", 512, 1024), -1536.0, Op.add)
-    act(A("pp"), A("ppb"))
-    act(A("ps0"), A("avs", 512, 1024), 1.0, -STOP)
-    ts(A("W", 1536, 2048), A("dps", 1024, 1536), -1536.0, Op.add)
-    ms(A("dX", 0, 256, 16), -2.0 ** 25); ms(A("dC", 0, 256, 16), -2.0 ** 26)
-    ts(A("pi", 1, 2), A("pi", 0, 1), 15, Op.bitwise_and)
-    iota(A("colr"), [[0, 16], [1, 16]], 0, 0)
-    iota(A("lc", 32, 64), [[1, 2], [32, 16]], 0, 0)
-    iota(LC(9), [[16, 16]], 15, 0)
-    iota(LC(1), [[0, 4], [16, 4]], 0, 0)
     sel(A("bo"), A("one"), [[-16, 8], [0, 16]], Op.is_ge, 0.0, 0, 1)
     sel(A("bo"), A("bo"), [[16, 8], [0, 16]], Op.is_ge, 0.0, 15, -1)
-    dma("g", lambda: g.indirect_dma_start(T.sbs[:], None, T.sb[:], IndirectOffsetOnAxis(ap=T.gi[:, 0:1], axis=0), bounds_check=7), [A("sbs")], [A("gi")])
-    dma("g", lambda: g.indirect_dma_start(T.ths[:], None, T.th[:], IndirectOffsetOnAxis(ap=T.gi[:, 0:1], axis=0), bounds_check=7), [A("ths")], [A("gi")])
-    iota(A("KC", 0, 512), [[0, 512]], 1000, 0)
-    iota(A("KC", 1536, 2728), [[0, 1192]], 1000, 0)
-
-    def setup1():
-        act(A("bob"), A("bo"))
-        act(A("nbo"), A("bo"), -1.0)
-        act(A("nb2"), A("bo"), -2.0)
-        iota(A("SD"), [[-1, 2736]], 8, 0, False)
-        dma("g", lambda: g.dma_start(T.SD[:, 8:1544], T.sbs[:, 0:1536], accum_op=Op.add), [A("SD", 8, 1544)], [A("sbs"), A("SD", 8, 1544)])
-        dma("g", lambda: g.dma_start(T.SD[:, 2056:2728], T.sbs[:, 1536:2208], accum_op=Op.add), [A("SD", 2056, 2728)], [A("sbs"), A("SD", 2056, 2728)])
-        iota(A("W", 0, 512), [[0, 512]], 0, 0)
-        cp(PF(0), A("pi", 1, 2))
-        cp(A("oc"), LC(9))
-        ms(PF(7), 0.5); ms(PF(8), 1.0); ms(PF(9), 1425.0)
-        ts(PF(2), PF(0), 1 / 16, Op.mult, -1536 - 15 / 16, Op.add)
-        ts(LC(8), LC(1), PF(0), Op.add, SP - 3584 + 1280.0, Op.add)
-        ts(A("pf", 3, 7), A("lc", 16, 20), PF(0), Op.add)
-        ts(A("lc", 32, 64), A("lc", 32, 64), PF(0), Op.add, PF(0), Op.add)
-        ts(A("dg"), A("colr"), PF(0), Op.is_equal)
-
-    def setup2():
-        for j, (src, d) in enumerate((("nbo", 0.0), ("nbo", 1.0), ("nb2", 2.0))):
-            sel(A("lm", 128 * j, 128 * j + 128), A(src), [[-1, 128]], Op.not_equal, d, 0, 1)
-        for r in range(16):
-            sel(A("slt", 128 * r, 128 * r + 128), ONE, [[-16, 8], [0, 16]], Op.is_equal, 0.0, -r, 1)
-        act(A("ng"), A("dg"), 2.0 ** 25, -2.0 ** 25)
-        act(A("ng2"), A("dg"), 2.0 ** 25 + 1280, -2.0 ** 25)
-        ts(A("W", 512, 1024), A("dps", 0, 512), -1536.0, Op.add)
-        ms(A("SD", 0, 4), 0)
-
-    def setup3():
-        act(A("W", A0, A0 + 2048), A("avs"))
-        for i in range(4):
-            n = 18 + 16 * i
-            act(A("dE", NE[i], NE[i + 1], n), A("dg", 0, 4), 0.0, 1.0)
-            act(A("dE", NE[i] + n - 1, NE[i + 1], n), A("dg", 0, 4), 0.0, 10.0)
-        for i in range(4):
-            n = 18 + 16 * i
-            for b in range(4):
-                act(A("dE", NE[i] + n * b + n - 17, NE[i] + n * b + n - 1), A("dg", 0, 16), -10.0)
-
-    def thresholds(par):
-        tt(A("mm"), A("ths", par, 512, 2), A("ng"), Op.add)
-        sc(A("ax"), A("dC"), A("mm"), Op.add, Op.max)
-        ts(LC(6 + par), A("ax", 15, 256, 16), 1409.0, Op.add)
+    for r in range(16):
+        sel(A("slt", 128 * r, 128 * r + 128), ONE, [[-16, 8], [0, 16]], Op.is_equal, 0.0, -r, 1)
+    iota(A("pi", 0, 1), [[0, 1]], 0, 1, False)
+    iota(A("colr"), [[0, 16], [1, 16]], 0, 0)
+    iota(LC(1), [[32, 16]], 0, 0)
+    iota(LC(9), [[16, 16]], 15, 0)
+    for a in (0, 1536, 2132):
+        iota(A("KC", a, a + (596 if a else 512)), [[0, 596 if a else 512]], 1000, 0)
+    iota(A("W", 0, 512), [[0, 512]], 0, 0)
+    iota(A("SD", 0, 8), [[0, 8]], 0, 0, False)
+    for a in range(8, 2736, 682):
+        iota(A("SD", a, a + 682), [[-1, 682]], 8 - a, 0, False)
+    act(A("pp"), A("ppb")); act(A("bob"), A("bo")); act(A("nbo"), A("bo"), -1.0); act(A("nb2"), A("bo"), -2.0)
+    for j, (src, d) in enumerate((("nbo", 0.0), ("nbo", 1.0), ("nb2", 2.0))):
+        sel(A("lm", 128 * j, 128 * j + 128), A(src), [[-1, 128]], Op.not_equal, d, 0, 1)
+    ts(A("gi", 0, 1), A("pi", 0, 1), 4, Op.arith_shift_right)
+    ts(A("pi", 1, 2), A("pi", 0, 1), 15, Op.bitwise_and)
+    cp(PF(0), A("pi", 1, 2)); cp(A("oc", 0, 16), LC(9)); cp(A("oc", 16, 20), A("colr", 12, 16))
+    ts(PF(2), PF(0), 1 / 16, Op.mult, -1536 - 15 / 16, Op.add)
+    ts(LC(2), LC(1), PF(0), Op.add, PF(0), Op.add)
+    act(LC(4), LC(2), 1.0, 1.0)
+    ts(A("dg"), A("colr"), PF(0), Op.is_equal)
+    act(A("ng"), A("dg"), 2.0 ** 25, -2.0 ** 25)
+    act(A("ng2"), A("dg", 0, 128), 2.0 ** 25 + 1280, -2.0 ** 25)
+    dma("g", lambda: g.dma_start(T.SD[0:8, 8:1544], T.sb[:, 0:1536], accum_op=Op.add), [A("SD", 8, 1544)], [A("SD", 8, 1544)], 98304, 1800)
+    dma("g", lambda: g.dma_start(T.SD[0:8, 2056:2728], T.sb[:, 1536:2208], accum_op=Op.add), [A("SD", 2056, 2728)], [A("SD", 2056, 2728)], 43008, 300)
+    dma("y", lambda: g.sync.dma_start(T.sdd[:], T.SD[0:8, :]), [A("sdd")], [A("SD")], 87552)
+    act(A("ne"), A("dN", 0, 704), 0.0, 1.0)
+    for i in range(4):
+        act(A("dE", NE[i], NE[i] + 1), PF(0), 0.0, 1.0)
+        act(A("dE", NE[i + 1] - 18, NE[i + 1] - 2), A("dg", 0, 16), -4.0)
+        act(A("dE", NE[i + 1] - 2, NE[i + 1] - 1), PF(0), 0.0, 4.0)
+        act(A("dE", NE[i + 1] - 1, NE[i + 1]), PF(0), 1 / 4096, i / 256)
+        act(PF(3 + i), PF(0), -1 / 4096, (1856 - 16 * i) / 4096)
+    act(PF(10), PF(0), 8.0, 27.0)
+    ts(PF(11), PF(10), PF(0), Op.mult, 18.0, Op.add)
+    ts(A("oe", 0, 1), PF(11), 171.0, Op.min)
+    cp(A("bdo"), A("bds"))
+    for l in (1, 2, 3):
+        ts(A("W", 512 * l, 512 * l + 512), A("dps", 512 * l - 512, 512 * l), -1536.0, Op.add)
+    for a in range(0, 2048, 512):
+        act(A("W", A0 + a, A0 + a + 512), A("avs", a, a + 512))
 
     for t in range(3):
         par = t & 1
-        if t > 0:
-            ts(A("snd%d" % (3 * t)), X(A("W", A0, A0 + 512), BD(0)), 1409.0, Op.add)
-            send(3 * t)
-            act(A("TT", 0, 512), A("W", A0, A0 + 512), 1.0, -127.0)
-            act(A("ps0"), will(t, 512, 1024), 1.0, -STOP)
-            cp(A("d16"), A("W", 512, 512 + NP))
-            pairs_pe(1, par)
-            plain_v(1, par); plain_v(2, par); plain_v(3, par)
-            pairs_v(1)
-            if t == 2:
-                act(A("W", DE, DE + 512), A("W", 512, 1024), 1.0, 1536.0)
-        ghosts(3 * t)
-        pairs_pe(2, par)
-        pairs_pe(3, par)
-        level(1, 3 * t + 1)
-        act(A("ps0"), will(t, 1024, 1536), 1.0, -STOP)
-        pairs_v(2)
-        if t == 0:
-            plain_v(2, 0); setup1()
-        if t == 1:
-            thresholds(1)
+        ts(A("snd%d" % (3 * t), 0, 128), X(will(t, 0, 512), A("bdo", 0, 8)), -127.0, Op.add)
+        act(A("snd%d" % (3 * t), 128, 224), X(will(t, 0, 512), A("bdo", 8, 14)), 1.0, -127.0)
+        send(3 * t)
+        act(A("TT", 0, 512), will(t, 0, 512), 1.0, -127.0)
+        cp(A("d16"), A("W", 512, 512 + NP))
+        for l in (1, 2, 3):
+            if l < 3:
+                act(A("ps0"), will(t, 512 * l, 512 * l + 512), 1.0, -STOP)
+            else:
+                act(A("ps0", 0, 256), will(t, 1536 + par, 2048, 2), 1.0, -STOP)
+                act(A("ps0", 256, 384), A("colr", 0, 128), -1 / 16, 15 / 16)
+                act(A("ps6", 256, 512), A("W", 1536 + par, 2048, 2))
+            lists(l, par)
+            ghosts(3 * t + l - 1)
+            if t == 0 and l < 3:
+                o, i = (("ths", T.th), ("SD", T.sdd))[l - 1]
+                dma("g", lambda o=o, i=i: g.indirect_dma_start(T[o][:], None, i[:], IndirectOffsetOnAxis(ap=T.gi[:, 0:1], axis=0), bounds_check=7),
+                    [A(o)], [A("gi"), A("sdd" if l == 2 else "gi"), A("lnd%d" % (l - 1))], 512 * A(o)[2], 1700)
+            if t < 2 and l == 2:
+                tt(A("mm"), A("ths", par, 512, 2), A("ng"), Op.add)
+                sc(A("m2"), A("dC"), A("mm"), Op.add, Op.max)
+                ts(LC(6 + par), A("m2", 15, 256, 16), 1409.0, Op.add)
+            level(l, 3 * t + l)
         if t == 2:
-            act(A("W", DE + 512, WN), A("W", 1024, 2048), 1.0, 1536.0)
+            for a in range(0, 1536, 512):
+                act(A("W", DE + a, DE + a + 512), A("W", 512 + a, 1024 + a), 1.0, 1536.0)
+            act(A("ng2"), A("dg", 0, 128), 2.0 ** 25 - 256, -2.0 ** 25)
+            act(A("dO"), A("TT", 0, 512), 0.0, 0.0); act(A("dO", 0, 512, 16), A("dN", 0, 32), 0.0, 1024.0)
             ts(A("ono"), A("W", 1537, 2048, 2), 1536.0, Op.add)
-            ts(LC(8), LC(8), -1536.0, Op.add)
-        ghosts(3 * t + 1)
-        level(2, 3 * t + 2)
-        act(A("ps0", 0, 256), will(t, 1536 + par, 2048, 2), 1.0, -STOP)
-        act(A("ps0", 256, 512), A("colr"), -1 / 16, 15 / 16)
-        act(A("ps6", 256, 512), A("W", 1536 + par, 2048, 2))
-        pairs_v(3)
-        if t == 0:
-            plain_v(3, 0); setup2(); thresholds(0)
-        if t == 1:
-            ms(A("dO"), 0.0); ms(A("dO", 0, 1024, 16), 1024.0)
-        if t == 2:
-            act(A("ng2"), A("dg"), 2.0 ** 25 - 256, -2.0 ** 25)
-        ghosts(3 * t + 2)
-        level(3, None)
+            for j in range(16):
+                act(A("go", 256 * j, 256 * j + 256), X(TW, A("ono", 16 * j, 16 * j + 16)), 1.0, 127.0)
+            for j in range(8):
+                sc(A("so", 512 * j, 512 * j + 512), A("dO", 0, 512), A("go", 512 * j, 512 * j + 512), Op.add, Op.min)
+            act(A("ps4", 256, 512), A("W", A0 + 1537, A0 + 2048, 2))
         walk(t)
 
-    dma("g", lambda: g.dma_start(T.ya[:], T.W[:, A0:A0 + 2048]), [], [A("W", A0, WN)])
+    tt(A("yro", 1, 512, 2), A("so", 15, 4096, 16), A("ps4", 256, 512), Op.min)
+    dma("g", lambda: g.dma_start(T.ya[:], T.W[:, A0:A0 + 2048]), [], [A("W", A0, WN)], 524288, 300)
     for j in range(3):
-        dma("y", lambda: g.sync.dma_start(T.yd[:, 512 * j:512 * j + 512], T.W[:, DE + 512 * j:DE + 512 * j + 512]), [], [A("W", A0, WN)])
-    odd_scan(0); odd_scan(1); odd_scan(2); odd_scan(3)
-    tt(A("yro", 1, 512, 2), A("so", 15, 4096, 16), A("W", A0 + 1537, A0 + 2048, 2), Op.min)
-    dma("s", lambda: g.scalar.dma_start(T.yr[:], T.yro[:]), [], [A("yro")])
+        dma("y", lambda j=j: g.sync.dma_start(T.yd[:, 512 * j:512 * j + 512], T.W[:, DE + 512 * j:DE + 512 * j + 512]), [], [A("W", A0, WN)], 262144)
+    dma("s", lambda: g.scalar.dma_start(T.yr[:], T.yro[:]), [], [A("yro")], 131072)
+
+    cnt, seen, ends, done = {e: 0 for e in Q}, {e: {} for e in Q}, {"loc": 0}, {}
+    for i in schedule(calls):
+        c = calls[i]
+        e = c["e"]
+        need = {}
+        for j, wait in c["after"].items():
+            if wait:
+                need[done[j][0]] = max(need.get(done[j][0], 0), done[j][1])
+        for sem, n in need.items():
+            if seen[e].get(sem, 0) < n:
+                Q[e].wait_ge(T.sem[sem], n); seen[e][sem] = n
+        ins = c["f"]()
+        if c["sem"] is None:
+            cnt[e] += 1
+            done[i] = ("c" + e, cnt[e]); ins.then_inc(T.sem["c" + e], 1)
+        else:
+            done[i] = c["sem"]
+            if c["sem"][0][:2] == "dm":
+                ins.then_inc(T.sem[c["sem"][0]], 16)
+            else:
+                ends["loc"] += c["sem"][1]
+        ends[done[i][0]] = done[i][1]
     for sem, n in ends.items():
         g.sync.wait_ge(T.sem[sem], n)

from concourse.bass import DstId, RemoteDMATransfer, IndirectOffsetOnAxis
from concourse.mybir import AluOpType as Op, ActivationFunctionType as Fn

F32, BF, I32, U16, F16 = "float32", "bfloat16", "int32", "uint16", "float16"
PC = ((24, 12, 24, 36, 44, 52), (20, 8, 16, 20, 32))
NC = ((56, 40, 24, 8), (32, 16, 8, 8))
NP, NPT = 2 * sum(PC[0]), 2 * sum(PC[1])
A0, SP, DE, WN = 2048, 4104, 4224, 5760
NE = (0, 19, 54, 105, 172)
STOP = 127 + 63 / 64
RND = 1536 + 63 / 128
CYCLE, WAIT, GATHER, FLIGHT = 0.91, 130, 1.56, 900
ROUNDS = 2
SLACK = 600
SB = {
    "avs": (2048, BF), "dps": (1536, I32), "bds": (42, I32), "bdo": (42, U16), "ths": (512, I32),
    "W": (WN, F32), "TT": (2728, BF), "KC": (2728, F32), "SD": (2736, I32), "d16": (NP, F16), "rh": (512, F16),
    "gs": (8 * NP, F32), "gp": (8 * NP, F16), "sp": (8 * NP, F16), "gn": (16 * (512 - NP), BF), "sn": (16 * (512 - NP), F16),
    "go": (4096, BF), "so": (4096, BF),
    "on1": (512 - NP, U16), "on2": (512 - NP, U16), "on3": (256 - NPT, U16), "ono": (256, U16),
    "op1": (NP, U16), "op2": (NP, U16), "op3": (NPT, U16),
    "dN": (1024, BF), "dP": (1024, BF), "dO": (512, BF), "dX": (128, BF), "dC": (256, BF), "dE": (172, BF),
    "one": (128, F32), "oneb": (144, BF), "ident": (128, BF), "pm1": (128, BF), "pm2": (128, BF),
    "bo": (128, F32), "bob": (128, BF), "nbo": (128, BF), "nb2": (128, BF), "lm": (384, BF), "pp": (288, F32), "ppb": (288, BF),
    "slt": (2048, BF), "colr": (256, F32),
    "dg": (256, F32), "ng": (256, BF), "ng2": (128, BF), "pi": (4, I32), "gi": (4, I32), "pf": (12, F32), "lc": (160, F32), "oc": (20, U16),
    "rt": (256, F16), "rtt": (256, F16), "ax": (256, F32), "mt": (256, BF), "mp": (256, BF), "mm": (256, F32), "m2": (256, F32), "ll": (1024, F32),
    "sm": (720, F32), "oh": (32, U16), "oe": (2, U16), "ot": (32, U16), "ow": (64, U16), "t16": (32, F16), "m16": (256, F16), "z16": (256, F16),
    "rm": (256, F16), "eq": (768, BF), "ne": (704, F32), "kp": (704, F32), "sg": (256, BF), "mk": (256, BF), "t2": (256, F32), "t3": (256, F32), "nw": (256, F32),
    "yro": (512, BF),
}
SCRATCH = {k: ("sbuf", [128, v[0]], v[1]) for k, v in SB.items()}
SCRATCH["sdd"] = ("dram", [8, 2736], I32)
for _i in range(9):
    SCRATCH["snd%d" % _i] = ("sbuf", [128, 224], F16 if _i % 3 else BF)
    SCRATCH["lnd%d" % _i] = ("sbuf", [128, 7, 32], F16 if _i % 3 else BF)
for _i in range(8):
    SCRATCH["ps%d" % _i] = ("psum", [128, 16, 32] if _i == 3 else [128, 512], F32)
SEMAPHORES = ["cv", "cs", "ct", "cg", "loc"] + ["arr%d" % i for i in range(9)] + ["dm%d" % i for i in range(16)]


def chunks(sizes):
    out, a = [], 0
    for n in sizes:
        out.append((a, a + n)); a += n
    return out


def schedule(calls):
    n = len(calls)
    fore, back = [[] for _ in calls], [[] for _ in calls]
    for i, c in enumerate(calls):
        for j, wait in c["after"].items():
            gap = calls[j]["time"] - calls[j]["hold"] + WAIT if wait else 0
            fore[i].append((j, calls[j]["hold"] + gap)); back[j].append((i, c["hold"] + gap))

    def place(order, links, least, slack):
        at, busy = [0.0] * n, {}
        for i in order:
            c = calls[i]
            t = max([at[j] + d for j, d in links[i]] + [least[i]])
            line = busy.setdefault(c["e"], [])
            k = 0
            while k < len(line) and line[k][0] < t + c["hold"] + (slack if c["e"] == "g" else 0):
                t = max(t, line[k][1]); k += 1
            line.insert(k, (t, t + c["hold"]))
            at[i] = t
        return at

    tail = [c["time"] - c["hold"] for c in calls]
    rest = list(tail)
    for i in range(n - 1, -1, -1):
        rest[i] = max([rest[j] + d for j, d in back[i]] + [tail[i]])
    best = None
    for _ in range(ROUNDS):
        start = place(sorted(range(n), key=lambda i: (-rest[i] - calls[i]["hold"], i)), fore, [0.0] * n, SLACK)
        end = max(start[i] + calls[i]["time"] for i in range(n))
        if best is None or end < best[0]:
            best = (end, start)
        rest = place(sorted(range(n), key=lambda i: (-start[i], -i)), back, tail, 0)
    return sorted(range(n), key=lambda i: (best[1][i], i))


def rank_program(g, core, T, topo):
    rank = T.rank_of(core)
    if rank is None:
        return
    Q = {"v": g.vector, "s": g.scalar, "t": g.tensor, "g": g, "y": g.sync}
    calls, hist, bank, rows, ndma = [], {}, {}, {}, [0]

    def A(name, lo=0, hi=None, st=1):
        if len(SCRATCH[name][1]) == 3:
            lo, hi = lo, 224 if hi is None else hi
            ap = T[name][:, lo // 32:hi // 32, :] if hi - lo > 32 else T[name][:, lo // 32, :]
        else:
            hi = SCRATCH[name][1][1] if hi is None else hi
            ap = T[name][:, lo:hi] if st == 1 else T[name][:, lo:hi:st]
        cols = range(lo, hi, st)
        return (ap, [(name, a, a + 1) for a in cols] if st > 16 else [(name, lo, hi)], len(cols), 4 if SCRATCH[name][2] in (F32, I32) else 2, name[:2] == "ps", False)

    def X(win, off):
        return (win[0].indirect(off[0]), win[1] + off[1], 16 * off[2], win[3], False, True)

    def put(e, f, wr, rr, time, hold=None, sem=None):
        i, after = len(calls), {}
        for regs, isw in ((rr, False), (wr, True)):
            for name, lo, hi in regs:
                for a, b, j, ww in hist.get(name, ()):
                    if (ww or isw) and a < hi and lo < b:
                        after[j] = True
                if name[:2] == "ps":
                    run = bank.setdefault(name, [e, [], []])
                    if run[0] != e:
                        run[0], run[1], run[2] = e, [], run[1]
                    for j in run[2]:
                        after[j] = True
                    if e == "t" and run[1]:
                        after[run[1][-1]] = True
                    run[1].append(i)
        after.pop(i, None)
        for j in after:
            after[j] = not (e == "t" and calls[j]["e"] == "t")
        if e in rows:
            if rows[e] is not None:
                after.setdefault(rows[e], False)
            rows[e] = i
        for regs, isw in ((rr, False), (wr, True)):
            for name, lo, hi in regs:
                h = hist.setdefault(name, [])
                if isw:
                    h[:] = [x for x in h if not (lo <= x[0] and x[1] <= hi)]
                h.append((lo, hi, i, isw))
        calls.append({"e": e, "f": f, "after": after, "time": time, "hold": time if hold is None else hold, "sem": sem})

    def do(e, f, w, r, cycles):
        wr, rr = list(w[1]), [x for o in r for x in o[1]]
        if w[5]:
            rr += wr[1:]; wr = wr[:1]
            put(e, f, wr, rr, 55 + 3.8 * CYCLE * w[2])
        elif r and r[0][5]:
            put(e, f, wr, rr, (55 if e == "v" else 70) + GATHER * CYCLE * w[2])
        else:
            put(e, f, wr, rr, max(64, cycles) * CYCLE)

    def dma(e, f, w, r, size, hold=60):
        put(e, f, [x for o in w for x in o[1]], [x for o in r for x in o[1]], hold + 1800 + size / 200, hold, ("dm%d" % ndma[0], 16))
        ndma[0] += 1

    def wide(*ops): return ops[0][2] * (0.5 if max(o[3] for o in ops) == 2 else 1)
    def cp(o, i): do("v", lambda: g.vector.tensor_copy(o[0], i[0]), o, [i], wide(o, i))
    def tt(o, a, b, op): do("v", lambda: g.vector.tensor_tensor(o[0], a[0], b[0], op), o, [a, b], o[2] * (1 if a[4] or b[4] else 2))
    def ms(o, c): do("v", lambda: g.vector.memset(o[0], c), o, [], wide(o))
    def tr(o, i): do("v", lambda: g.vector.transpose(o[0], i[0]), o, [i], wide(o, i))
    def sc(o, a, b, o0, o1): do("v", lambda: g.vector.tensor_tensor_scan(o[0], a[0], b[0], 0.0, o0, o1), o, [a, b], wide(o, a, b))

    def ts(o, a, s1, o0, s2=None, o1=None):
        r = [a] + [s for s in (s1, s2) if isinstance(s, tuple)]
        v1 = s1[0] if isinstance(s1, tuple) else s1
        v2 = s2[0] if isinstance(s2, tuple) else s2
        if o1 is None:
            do("v", lambda: g.vector.tensor_scalar(o[0], a[0], v1, None, o0), o, r, wide(o, a))
        else:
            do("v", lambda: g.vector.tensor_scalar(o[0], a[0], v1, v2, o0, o1), o, r, wide(o, a))

    def act(o, i, scale=1.0, bias=0.0, fn=Fn.Copy):
        r = [i] + [s for s in (scale, bias) if isinstance(s, tuple)]
        sv = scale[0] if isinstance(scale, tuple) else float(scale)
        bv = bias[0] if isinstance(bias, tuple) else float(bias)
        do("s", lambda: g.scalar.activation(o[0], i[0], fn, bias=bv, scale=sv), o, r, o[2])

    def mms(group):
        def f():
            for o, l, r, st, sp in group:
                ins = g.tensor.matmul(o[0], l[0], r[0], st, sp)
            return ins
        put("t", f, [x for m in group for x in m[0][1]], [x for m in group for x in m[1][1] + m[2][1]],
            sum(max(64, m[0][2]) * (4 if m[2][3] == 4 else 1) * CYCLE for m in group))

    def mm(o, l, r, st, sp): mms([(o, l, r, st, sp)])

    def iota(o, pat, base, cm, fl=True):
        if fl:
            do("g", lambda: g.iota(o[0], pat, base, cm, allow_small_or_imprecise_dtypes=True), o, [], 160 + 2 * o[2])
        else:
            do("g", lambda: g.iota(o[0], pat, base, cm), o, [], 160 + 2 * o[2])

    def sel(o, i, pat, op, fill, base, cm):
        do("g", lambda: g.affine_select(o[0], i[0], pat, op, fill, base, cm), o, [i], 205 + 2 * o[2])

    def S(j): return A("sm", 16 * j, 16 * j + 16)
    def LC(j): return A("lc", 16 * j, 16 * j + 16)
    def PF(j): return A("pf", j, j + 1)
    def BD(l): return A("bdo", 14 * l, 14 * l + 14)
    def LL(j): return A("ll", 256 * j + 15, 256 * j + 256, 16)
    def H(name, h, base=0): return A(name, base + h, base + h + 128)
    TW, ONE = A("TT"), A("oneb", 0, 128)

    def will(t, lo, hi, st=1):
        return A("avs", lo, hi, st) if t == 0 else A("W", A0 + lo, A0 + hi, st)

    def send(x):
        trs = []
        used = [0, 0]
        for d in range(1, 8):
            dst = T.cores[rank ^ d]
            rid, pid, _ = topo.addr(dst)
            en = topo.engines(core, dst)
            k = len(en) // 8
            same = int(topo.die(dst) == topo.die(core))
            mine = en[same::2][used[same]:used[same] + k]
            used[same] += k
            trs.append(RemoteDMATransfer(dst_ids=[DstId(rid=rid, pnc=pid)], dma_engine_mask=sum(1 << e for e in mine),
                                         remote_sem=T.sem["arr%d" % x], src=A("snd%d" % x, 32 * d - 32, 32 * d)[0], dst=A("lnd%d" % x, 32 * d - 32, 32 * d)[0]))
        hold = 400 if x else 1900
        put("g", lambda: g.remote_dma_fused(trs, local_sem=T.sem.loc), A("lnd%d" % x)[1], A("snd%d" % x)[1], hold + FLIGHT, hold, ("arr%d" % x, 7 * k))

    def ghosts(x):
        def blocks(name, d): return (T[name][:, d - 1:7:3, :], [(name, 0, 224)], 32 * len(range(d, 8, 3)), 2, name == "ps3", False)
        mms([(blocks("ps3", d), A(("ident", "pm1", "pm2")[d % 3]), blocks("lnd%d" % x, d), True, True) for d in (1, 2, 3)])
        l = x % 3
        act(A("TT", 2048 + 224 * l, 2272 + 224 * l), A("ps3", 0, 224), 1.0, -1536.0 if l else 0.0)

    def lists(l, par):
        n = NP if l < 3 else NPT
        b = "ps2" if l == 2 else "ps1"
        for h in (0, 1):
            for a in (0, 1):
                r = A("d16", a, n, 2) if l == 1 else (A("W", 1024 + a, 1024 + n, 2) if l == 2 else A("W", 1536 + par + 2 * a, 1536 + 2 * n, 4))
                mm(A(b, h * n // 2, (h + 1) * n // 2), A("ppb" if l == 1 else "pp", 160 - 152 * h - 8 * a, 288 - 152 * h - 8 * a), r, a == 0, a == 1)
        ts(A("op%d" % l), A(b, 0, n), 1536.0, Op.add)
        if l < 3:
            ts(A("on%d" % l), A("W", 512 * l + NP, 512 * l + 512), 1536.0, Op.add)
        else:
            ts(A("on3"), A("W", 1536 + 2 * NPT + par, 2048, 2), 1536.0, Op.add)

    def level(l, x):
        n, m = (NP, 512 - NP) if l < 3 else (NPT, 256 - NPT)
        o, on = "op%d" % l, "on%d" % l
        pc, nc = chunks(PC[l // 3]), chunks(NC[l // 3])
        def key(src, lo, hi): tt(A("KC", 512 * l + lo, 512 * l + hi) if l < 3 else A("ps0", lo, hi), src, A("ps0", lo, hi), Op.min)
        def pair(a, b): tt(A("gp", 16 * a, 16 * b), X(TW, A(o, a, b)), A("gs", 16 * a, 16 * b), Op.min)
        def scan2(a, b): sc(A("sp", 16 * a, 16 * b), A("dP", 0, 16 * (b - a)), A("gp", 16 * a, 16 * b), Op.add, Op.min)
        def scan(a, b): sc(A("sn", 16 * a, 16 * b), A("dN", 0, 16 * (b - a)), A("gn", 16 * a, 16 * b), Op.add, Op.min)
        rows["v"], rows["s"] = None, None
        for j, (a, b) in enumerate(pc):
            if j == 0:
                ts(A("gs", 16 * a, 16 * b), X(TW, A(o, n // 2 + a, n // 2 + b)), -0.5, Op.add)
            else:
                act(A("gs", 16 * a, 16 * b), X(TW, A(o, n // 2 + a, n // 2 + b)), bias=-0.5)
        for a, b in nc:
            act(A("gn", 16 * a, 16 * b), X(TW, A(on, a, b)))
        pair(*pc[1]); pair(*pc[0]); pair(*pc[2]); pair(*pc[3])
        a = 0
        for j in range(4, len(pc)):
            scan2(a, pc[j - 1][0]); a = pc[j - 1][0]
            pair(*pc[j])
        scan2(a, pc[-1][0])
        e = 0
        if l == 3:
            rows.clear()
            e = 128
            key(A("sp", 7, 8 * e, 8), 0, e)
        scan(*nc[0]); scan2(*pc[-1]); scan(*nc[1])
        key(A("sp", 8 * e + 7, 8 * n, 8), e, n)
        for a, b in nc[2:-1]:
            scan(a, b)
        e = nc[-2][0]
        key(A("sn", 15, 16 * e, 16), n, n + e)
        scan(*nc[-1])
        key(A("sn", 16 * e + 15, 16 * m, 16), n + e, n + m)
        rows.clear()
        if l < 3:
            K = A("KC", 512 * l, 512 * l + 512)
            ts(A("snd%d" % x), X(K, BD(l)), RND, Op.add)
            send(x)
            ts(A("rh"), K, RND, Op.add)
            ts(A("TT", 512 * l, 512 * l + 512), A("rh"), -1536.0, Op.add)

    def walk(t):
        par, last = t & 1, t == 2
        sh, w0, cd = (-256.0, A0 - 64, DE - 1024.0) if last else (1280.0, 448, -512.0)
        WW = A("W", w0, WN if last else SP)
        EB, ZB = {0: "ps1", 128: "ps2"}, {0: "ps5", 128: "ps4"}
        def OH(j, h): return A("oh", 16 * j - 16 + h // 16, 16 * j - 8 + h // 16)
        def spread(b, src, n):
            for a in range(0, 16, n):
                mms([(A(b, r, 256, 16), A("slt", 128 * r, 128 * r + 128), src, True, True) for r in range(a, a + n)])

        mm(A("ps7", 0, 256), A("ident"), A("ng"), True, False)
        for h in (0, 128):
            ts(H("rt", h), H("ps0", h), RND, Op.add)
            mm(H("ps6", h), A("ident"), H("rt", h), True, True)
        for h in (0, 128):
            tr(H("rtt", h), H("rt", h))
            sc(H("ax", h), A("dX"), H("rtt", h), Op.add, Op.max)
            tt(H("t2", h), A("ps0", 256, 384), H("rtt", h), Op.add)
            tt(H("mt", h), X(H("ax", h), A("oc", 0, 8)), H("t2", h), Op.is_equal)
            tr(H("mp", h), H("mt", h))
            tt(H("rm", h), H("ps6", h), H("mp", h), Op.mult)
            mm(A("ps7", h, h + 128), A("bob"), H("rm", h), False, h > 0)
            for j in range(3):
                tt(H("m16", h), X(A("KC"), OH(j, h)) if j else H("ps0", h), H("mp", h), Op.mult)
                if j:
                    mm(A(EB[h], 0, 128), A("nbo"), H("rm", h), True, False)
                mm(A(EB[h], 0, 128), A("bob"), H("m16", h), j == 0, j > 0)
                if j == 0:
                    mm(A(EB[h], 0, 128), A("nbo"), H("rm", h), False, True)
                ts(H("eq", h, 256 * j), A(EB[h], 0, 128), PF(2), Op.is_equal)
                tt(H("z16", h), X(A("W", 0, 2728), OH(j, h)) if j else H("ps6", h, 256), H("eq", h, 256 * j), Op.mult)
                mm(A(ZB[h], 0, 128), A("ident"), A("ng2" if j == 2 else "ng", 0, 128), True, False)
                mm(A(ZB[h], 0, 128), A("bob"), H("z16", h), False, True)
                sc(H("ll", h, 256 * j), A("dC", 0, 128), A(ZB[h], 0, 128), Op.add, Op.max)
                if j < 2:
                    ts(OH(j + 1, h), A("ll", 256 * j + h + 15, 256 * j + h + 128, 16), 1536.0, Op.add)
        for j in range(3):
            mm(A("ps3", 0, 256), A("lm", 128 * j, 128 * j + 128), A("eq", 256 * j, 256 * j + 256), j == 0, j == 2)
        act(A("sg"), A("ps3", 0, 256), 1.0, PF(7), Fn.Sign)
        act(A("mk"), A("sg"), fn=Fn.Relu)
        if last:
            ts(A("yro", 0, 512, 2), A("rt"), -1409.0, Op.add)

        K0 = A("ps0", 0, 256)
        z1, z2, z3, v = LL(0), LL(1), LL(2), LL(3)
        def S2(j): return A("sm", 16 * j, 16 * j + 32)
        e, nbv, o = LC(2 + 2 * par), LC(3), 1 - par
        x1, okb, u1, de, mv, rp, al, als, nb = S(o), S(2 + o), S(5 + o), S(4 + 3 * par), S(10), S(12), S(14), S(15), S(16)
        q2, p2, b3, dl, s3, tf = S(22 + par), S(22 + o), S(26), S(28), S(29), S(36)
        t16, val = A("t16", 0, 16), A("t16", 16, 32)
        sc(A("ll", 768, 1024), A("dC"), A("ps7", 0, 256), Op.add, Op.max)
        act(S(11), v, -1.0, PF(9), Fn.Relu); act(mv, S(11), -1.0, 16.0)
        tt(nbv, v, LC(6 + par), Op.subtract)
        act(S(17), nbv, 1.0, PF(7), Fn.Sign); act(okb, S(17), 2048.0, 2048.0)
        act(S(38), z1, fn=Fn.Abs); act(S(8), S(38), -1.0, PF(8), Fn.Relu); act(S(9), S(38), -1.0, PF(8), Fn.Relu)
        act(S(2 + par), z1); act(S(20 + par), z1)
        tt(S2(0), S2(8), A("lc", 32 + 16 * par, 64 + 16 * par), Op.mult)
        tt(rp, nbv, x1, Op.is_lt)
        tt(S2(5), S2(0), S2(2), Op.add)
        tt(de, e, z1, Op.subtract)
        act(S(13), rp); act(al, rp, -2048.0, 512.0); act(als, rp, -2048.0, 512.0 + sh); act(nb, rp, 4096.0, 1544.0 - 1856.0 - 4096.0 - sh)
        tt(val, u1, mv, Op.min)
        spread("ps0", val, 4)
        for h in (128, 0):
            tt(H("ps0", h), H("ps0", h), H("mp", h), Op.mult)
        act(S(39), z2, fn=Fn.Abs); act(S(40), S(39), -1.0, PF(8), Fn.Relu); act(S(41), S(39), -1.0, PF(8), Fn.Relu)
        act(S(20 + o), z2)
        tt(S2(18), S2(40), S2(4 + 2 * par), Op.mult)
        tt(S2(22), S2(18), S2(20), Op.add)
        tt(S(42), q2, p2, Op.subtract); tt(S(43), p2, al, Op.min)
        act(S(24), p2, 1.0, cd); act(S(25), S(42), 1.0, 1536.0)
        tt(S2(26), S2(24), S2(12), Op.mult)
        tt(dl, S(27), S(43), Op.add)
        ts(s3, z3, sh, Op.is_equal)
        tt(S(30), z3, als, Op.min)
        tt(S(35), z3, nb, Op.add)
        tt(S(32), s3, dl, Op.mult)
        tt(S(34), S(30), b3, Op.add)
        tt(S(33), s3, p2, Op.mult)
        tt(t16, S(32), S(34), Op.add)
        spread("ps7", t16, 4)
        tt(S2(36), S2(32), S2(34), Op.add)
        ts(A("ot"), S2(36), 1856.0, Op.add)
        for h in (128, 0):
            act(H("nw", h), X(WW, A("ot", h // 16, 8 + h // 16)))
            tt(H("t2", h), X(A("SD"), A("ot", 16 + h // 16, 24 + h // 16)), H("mk", h), Op.mult)
            tt(H("t3", h), H("t2", h), H("ps0", h), Op.subtract)
        for i in range(4):
            act(A("ne", NE[i + 1] - 1, 704, 176), A("sm", 576 + i, 592, 4), 1 / 4096, PF(3 + i), Fn.Identity)
        tt(A("m16", 0, 64), X(tf, A("oc", 16, 20)), A("dg", 0, 64), Op.mult)
        mm(A("ps2", 0, 64), A("bob"), A("m16", 0, 64), True, True)
        for b in range(3, -1, -1):
            for i in range(4):
                c = 4 * b + i
                act(A("ne", 176 * b + NE[i] + 2, 176 * b + NE[i + 1] - 1), A("ps7", 64 * b, 16 * c + 16) if b < 3 else A("ps2", 0, 16 * i + 16), -1.0, A("sm", 576 + c, 577 + c), Fn.Abs)
            sc(A("kp", 176 * b, 176 * b + 172), A("ne", 176 * b, 176 * b + 172), A("dE"), Op.min, Op.add)
            ts(A("ow", 16 * b, 16 * b + 16), X(A("kp", 176 * b, 176 * b + 172), A("oe", 0, 1)), 4096.0, Op.mult)
            tt(X(WW, A("ow", 16 * b, 16 * b + 4)), A("nw", 64 * b, 64 * b + 64), A("t3", 64 * b, 64 * b + 64), Op.add)

    dma("y", lambda: g.sync.dma_start(T.bds[:], T.bd[:]), [A("bds")], [], 21504)
    dma("s", lambda: g.scalar.dma_start(T.avs[:, 0:512], T.av[:, 0:512]), [A("avs", 0, 512)], [], 131072)
    dma("y", lambda: g.sync.dma_start(T.dps[:, 0:512], T.dp[:, 0:512]), [A("dps", 0, 512)], [], 262144)
    dma("s", lambda: g.scalar.dma_start(T.avs[:, 512:2048], T.av[:, 512:2048]), [A("avs", 512, 2048)], [], 393216)
    dma("y", lambda: g.sync.dma_start(T.dps[:, 512:1536], T.dp[:, 512:1536]), [A("dps", 512, 1536)], [], 524288)
    ms(A("oneb"), 1.0); ms(A("one"), 1.0); ms(A("dP"), -1 / 16); ms(A("dN"), -1 / 16); ms(A("dX"), 1 / 16); ms(A("dC"), 0.0); ms(A("dE"), 0.0)
    for a, b in ((512, 1536), (1536, 2560), (2560, 2728)):
        act(A("TT", a, b), A("dP", 0, b - a), 0.0, 128.0)
    ms(A("dP", 0, 1024, 8), 1024.0); ms(A("dN", 0, 1024, 16), 1024.0)
    ms(A("dX", 0, 128, 16), -2.0 ** 25); ms(A("dC", 0, 256, 16), -2.0 ** 26)
    ms(A("W", A0 + 2048, DE), 0.0); ms(PF(7), 0.5); ms(PF(8), 1.0); ms(PF(9), 1425.0)
    sel(A("ppb", 0, 144), A("oneb"), [[-16, 9], [200, 2], [-1, 8]], Op.is_equal, 0.0, -200, 1)
    sel(A("ppb", 144, 288), A("oneb"), [[-16, 9], [200, 2], [-1, 8]], Op.is_equal, 0.0, 8, 1)
    sel(A("pm1"), ONE, [[16, 8], [-1, 16]], Op.is_equal, 0.0, -112, 1)
    sel(A("pm2", 16, 128), A("oneb", 16, 128), [[16, 7], [-1, 16]], Op.is_equal, 0.0, -112, 1)
    sel(A("pm2", 0, 16), A("oneb", 0, 16), [[-1, 16]], Op.is_equal, 0.0, 0, 1)
    sel(A("ident"), ONE, [[-1, 128]], Op.is_equal, 0.0, 0, 1)
    sel(A("bo"), A("one"), [[-16, 8], [0, 16]], Op.is_ge, 0.0, 0, 1)
    sel(A("bo"), A("bo"), [[16, 8], [0, 16]], Op.is_ge, 0.0, 15, -1)
    for r in range(16):
        sel(A("slt", 128 * r, 128 * r + 128), ONE, [[-16, 8], [0, 16]], Op.is_equal, 0.0, -r, 1)
    iota(A("pi", 0, 1), [[0, 1]], 0, 1, False)
    iota(A("colr"), [[0, 16], [1, 16]], 0, 0)
    iota(LC(1), [[32, 16]], 0, 0)
    iota(LC(9), [[16, 16]], 15, 0)
    for a in (0, 1536, 2132):
        iota(A("KC", a, a + (596 if a else 512)), [[0, 596 if a else 512]], 1000, 0)
    iota(A("W", 0, 512), [[0, 512]], 0, 0)
    iota(A("SD", 0, 8), [[0, 8]], 0, 0, False)
    for a in range(8, 2736, 682):
        iota(A("SD", a, a + 682), [[-1, 682]], 8 - a, 0, False)
    act(A("pp"), A("ppb")); act(A("bob"), A("bo")); act(A("nbo"), A("bo"), -1.0); act(A("nb2"), A("bo"), -2.0)
    for j, (src, d) in enumerate((("nbo", 0.0), ("nbo", 1.0), ("nb2", 2.0))):
        sel(A("lm", 128 * j, 128 * j + 128), A(src), [[-1, 128]], Op.not_equal, d, 0, 1)
    ts(A("gi", 0, 1), A("pi", 0, 1), 4, Op.arith_shift_right)
    ts(A("pi", 1, 2), A("pi", 0, 1), 15, Op.bitwise_and)
    cp(PF(0), A("pi", 1, 2)); cp(A("oc", 0, 16), LC(9)); cp(A("oc", 16, 20), A("colr", 12, 16))
    ts(PF(2), PF(0), 1 / 16, Op.mult, -1536 - 15 / 16, Op.add)
    ts(LC(2), LC(1), PF(0), Op.add, PF(0), Op.add)
    act(LC(4), LC(2), 1.0, 1.0)
    ts(A("dg"), A("colr"), PF(0), Op.is_equal)
    act(A("ng"), A("dg"), 2.0 ** 25, -2.0 ** 25)
    act(A("ng2"), A("dg", 0, 128), 2.0 ** 25 + 1280, -2.0 ** 25)
    dma("g", lambda: g.dma_start(T.SD[0:8, 8:1544], T.sb[:, 0:1536], accum_op=Op.add), [A("SD", 8, 1544)], [A("SD", 8, 1544)], 98304, 1800)
    dma("g", lambda: g.dma_start(T.SD[0:8, 2056:2728], T.sb[:, 1536:2208], accum_op=Op.add), [A("SD", 2056, 2728)], [A("SD", 2056, 2728)], 43008, 300)
    dma("y", lambda: g.sync.dma_start(T.sdd[:], T.SD[0:8, :]), [A("sdd")], [A("SD")], 87552)
    act(A("ne"), A("dN", 0, 704), 0.0, 1.0)
    for i in range(4):
        act(A("dE", NE[i], NE[i] + 1), PF(0), 0.0, 1.0)
        act(A("dE", NE[i + 1] - 18, NE[i + 1] - 2), A("dg", 0, 16), -4.0)
        act(A("dE", NE[i + 1] - 2, NE[i + 1] - 1), PF(0), 0.0, 4.0)
        act(A("dE", NE[i + 1] - 1, NE[i + 1]), PF(0), 1 / 4096, i / 256)
        act(PF(3 + i), PF(0), -1 / 4096, (1856 - 16 * i) / 4096)
    act(PF(10), PF(0), 8.0, 27.0)
    ts(PF(11), PF(10), PF(0), Op.mult, 18.0, Op.add)
    ts(A("oe", 0, 1), PF(11), 171.0, Op.min)
    cp(A("bdo"), A("bds"))
    for l in (1, 2, 3):
        ts(A("W", 512 * l, 512 * l + 512), A("dps", 512 * l - 512, 512 * l), -1536.0, Op.add)
    for a in range(0, 2048, 512):
        act(A("W", A0 + a, A0 + a + 512), A("avs", a, a + 512))

    for t in range(3):
        par = t & 1
        ts(A("snd%d" % (3 * t), 0, 128), X(will(t, 0, 512), A("bdo", 0, 8)), -127.0, Op.add)
        act(A("snd%d" % (3 * t), 128, 224), X(will(t, 0, 512), A("bdo", 8, 14)), 1.0, -127.0)
        send(3 * t)
        act(A("TT", 0, 512), will(t, 0, 512), 1.0, -127.0)
        cp(A("d16"), A("W", 512, 512 + NP))
        for l in (1, 2, 3):
            if l < 3:
                act(A("ps0"), will(t, 512 * l, 512 * l + 512), 1.0, -STOP)
            else:
                act(A("ps0", 0, 256), will(t, 1536 + par, 2048, 2), 1.0, -STOP)
                act(A("ps0", 256, 384), A("colr", 0, 128), -1 / 16, 15 / 16)
                act(A("ps6", 256, 512), A("W", 1536 + par, 2048, 2))
            lists(l, par)
            ghosts(3 * t + l - 1)
            if t == 0 and l < 3:
                o, i = (("ths", T.th), ("SD", T.sdd))[l - 1]
                dma("g", lambda o=o, i=i: g.indirect_dma_start(T[o][:], None, i[:], IndirectOffsetOnAxis(ap=T.gi[:, 0:1], axis=0), bounds_check=7),
                    [A(o)], [A("gi"), A("sdd" if l == 2 else "gi"), A("lnd%d" % (l - 1))], 512 * A(o)[2], 1700)
            if t < 2 and l == 2:
                tt(A("mm"), A("ths", par, 512, 2), A("ng"), Op.add)
                sc(A("m2"), A("dC"), A("mm"), Op.add, Op.max)
                ts(LC(6 + par), A("m2", 15, 256, 16), 1409.0, Op.add)
            level(l, 3 * t + l)
        if t == 2:
            for a in range(0, 1536, 512):
                act(A("W", DE + a, DE + a + 512), A("W", 512 + a, 1024 + a), 1.0, 1536.0)
            act(A("ng2"), A("dg", 0, 128), 2.0 ** 25 - 256, -2.0 ** 25)
            act(A("dO"), A("TT", 0, 512), 0.0, 0.0); act(A("dO", 0, 512, 16), A("dN", 0, 32), 0.0, 1024.0)
            ts(A("ono"), A("W", 1537, 2048, 2), 1536.0, Op.add)
            for j in range(16):
                act(A("go", 256 * j, 256 * j + 256), X(TW, A("ono", 16 * j, 16 * j + 16)), 1.0, 127.0)
            for j in range(8):
                sc(A("so", 512 * j, 512 * j + 512), A("dO", 0, 512), A("go", 512 * j, 512 * j + 512), Op.add, Op.min)
            act(A("ps4", 256, 512), A("W", A0 + 1537, A0 + 2048, 2))
        walk(t)

    tt(A("yro", 1, 512, 2), A("so", 15, 4096, 16), A("ps4", 256, 512), Op.min)
    dma("g", lambda: g.dma_start(T.ya[:], T.W[:, A0:A0 + 2048]), [], [A("W", A0, WN)], 524288, 300)
    for j in range(3):
        dma("y", lambda j=j: g.sync.dma_start(T.yd[:, 512 * j:512 * j + 512], T.W[:, DE + 512 * j:DE + 512 * j + 512]), [], [A("W", A0, WN)], 262144)
    dma("s", lambda: g.scalar.dma_start(T.yr[:], T.yro[:]), [], [A("yro")], 131072)

    cnt, seen, ends, done = {e: 0 for e in Q}, {e: {} for e in Q}, {"loc": 0}, {}
    for i in schedule(calls):
        c = calls[i]
        e = c["e"]
        need = {}
        for j, wait in c["after"].items():
            if wait:
                need[done[j][0]] = max(need.get(done[j][0], 0), done[j][1])
        for sem, n in need.items():
            if seen[e].get(sem, 0) < n:
                Q[e].wait_ge(T.sem[sem], n); seen[e][sem] = n
        ins = c["f"]()
        if c["sem"] is None:
            cnt[e] += 1
            done[i] = ("c" + e, cnt[e]); ins.then_inc(T.sem["c" + e], 1)
        else:
            done[i] = c["sem"]
            if c["sem"][0][:2] == "dm":
                ins.then_inc(T.sem[c["sem"][0]], 16)
            else:
                ends["loc"] += c["sem"][1]
        ends[done[i][0]] = done[i][1]
    for sem, n in ends.items():
        g.sync.wait_ge(T.sem[sem], n)
